import numpy as np
import ml_dtypes


def mxq(x, axis, fmt="e4m3"):
    dtype, down = {"e4m3": (ml_dtypes.float8_e4m3fn, 7), "e5m2": (ml_dtypes.float8_e5m2, 14)}[fmt]
    v = np.moveaxis(np.asarray(x, np.float32).astype(ml_dtypes.bfloat16).astype(np.float64), axis, -1)
    blocks = v.reshape(v.shape[:-1] + (-1, 32))
    amax = np.abs(blocks).max(-1, keepdims=True)
    byte = np.maximum(np.where(amax > 0, np.frexp(amax)[1] - 1 + 127, 0) - down, 1)
    scale = np.exp2(byte - 127.0)
    codes = (blocks / scale).astype(np.float32).astype(dtype).astype(np.float64)
    return np.moveaxis((codes * scale).reshape(v.shape), -1, axis)


WIDE = False


def mx_kscale(k):
    if not WIDE:
        return np.ones(k)
    levels = np.array([10, -10, 5, -5, 0])
    if k % 512:
        return np.exp2(np.random.permutation(np.resize(levels, k // 32))).repeat(32)
    a = np.empty((k // 512, 16))
    for p in range(k // 512):
        a[p, :8] = np.random.permutation(np.resize(levels, 8))
        for g in range(8):
            far = levels[np.abs(levels - a[p, g]) >= 10]
            a[p, g + 8] = far[np.random.randint(len(far))]
    return np.exp2(a.ravel()).repeat(32)


def f64(x):
    return np.asarray(x).astype(np.float64)


def striped8(idx):
    return np.concatenate([x.reshape(-1, 16).T for x in idx]).astype(np.uint16)


def runs(offs, k):
    lists = np.stack([offs[16 * r : 16 * r + 16].T.reshape(-1) for r in range(8)]).astype(np.int64)
    return lists[np.arange(k) % 512 // 64]


def pack_weight(w):
    k, n = w.shape
    w = f64(np.asarray(w, np.float32).astype(ml_dtypes.bfloat16)).reshape(k // 32, 32, n)
    amax = np.abs(w).max(1)
    byte = np.clip(np.where(amax > 0, np.frexp(amax)[1] - 1 + 127 - 7, 1), 1, 254)
    scaled = (w * np.exp2(127.0 - byte)[:, None, :]).reshape(k, n).astype(np.float32)
    words = np.ascontiguousarray(scaled.reshape(k // 512, 128, 4, n).transpose(0, 1, 3, 2)).astype(ml_dtypes.float8_e4m3fn).view(np.uint8)
    return words, np.ascontiguousarray(byte.astype(np.uint8).reshape(k // 512, 16, n))


def unpack_weight(words, scales):
    g, p, n, _ = words.shape
    vals = np.ascontiguousarray(words).view(ml_dtypes.float8_e4m3fn).astype(np.float64) * np.repeat(np.exp2(scales.astype(np.float64) - 127.0), 8, axis=1)[..., None]
    return vals.transpose(0, 1, 3, 2).reshape(g * 512, n)


K, T, S, N, U = 512, 2048, 512, 512, 1024


def setup_inputs():
    n = np.random.standard_normal
    s = mx_kscale(K)[:, None]
    packed_xT = pack_weight(n((K, T)) * s)
    return {
        "x_words": packed_xT[0],
        "x_scales": packed_xT[1],
        "w1": (n((K, N)) / np.sqrt(K) / s).astype(np.float32),
        "par": n((N, U)).astype(np.float32),
        "ssq": np.random.uniform(0.5, 3.0, (N, U)).astype(np.float32),
        "offs": striped8(np.stack([np.random.permutation(T)[:S] for _ in range(8)])),
        "ent": striped8(np.stack([np.random.permutation(U)[:S] for _ in range(8)])),
    }


def reference(x_words, x_scales, w1, par, ssq, offs, ent):
    xq = unpack_weight(x_words, x_scales)[np.arange(K)[:, None], runs(offs, K)]
    y = mxq(f64(w1), 0, "e4m3").T @ xq
    b = np.sqrt(f64(ssq)[np.arange(N)[:, None], runs(ent, N)] + (y) ** 2)
    pn = f64(par)[np.arange(N)[:, None], runs(ent, N)] - (y / b)
    out = f64(par).copy()
    out[np.arange(N)[:, None], runs(ent, N)] = pn
    return out

@@ -1,0 +1,136 @@
+from contextlib import ExitStack
+
+import concourse.mybir as mybir
+
+K, T, S, N, U = 512, 2048, 512, 512, 1024
+FLOPS = 2 * K * N * S
+
+F32 = mybir.dt.float32
+BF16 = mybir.dt.bfloat16
+I32 = mybir.dt.int32
+U32 = mybir.dt.uint32
+U16 = mybir.dt.uint16
+U8 = mybir.dt.uint8
+FP8X4 = mybir.dt.float8_e4m3fn_x4
+ALU = mybir.AluOpType
+ACT = mybir.ActivationFunctionType
+
+P = 128
+PACK = 4
+BLOCKS = N // P
+
+
+def tile_picked_adagr8_none_p_kernel(tc, x_words, x_scales, w1, par, ssq, offs, ent, out):
+    nc = tc.nc
+    par_rows = par.rearrange("(p t) u -> t p u", t=BLOCKS)
+    ssq_rows = ssq.rearrange("(p t) u -> t p u", t=BLOCKS)
+    out_rows = out.rearrange("(p t) u -> t p u", t=BLOCKS)
+
+    with ExitStack() as ctx:
+        lists = ctx.enter_context(tc.tile_pool(name="lists", bufs=1))
+        keep = ctx.enter_context(tc.tile_pool(name="keep", bufs=1))
+        work = ctx.enter_context(tc.tile_pool(name="work", bufs=2))
+        psum = ctx.enter_context(tc.psum_pool(name="psum", bufs=1))
+
+        offs_sb = lists.tile([P, S // 16], U16, name="offs_sb")
+        ent_sb = lists.tile([P, S // 16], U16, name="ent_sb")
+        nc.sync.dma_start(offs_sb[:], offs)
+
+        scale_table = keep.tile([P, T], U8, name="scale_table", align_bytes=64)
+        nc.vector.memset(scale_table[:].bitcast(I32), 0)
+        for r in range(2):
+            nc.scalar.dma_start(scale_table[r:P:16, :].bitcast(I32), x_scales[0, r:16:2, :].bitcast(I32))
+
+        w_raw = keep.tile([P, PACK, N], F32, name="w_raw", tag="slot_a", align_bytes=64)
+        nc.sync.dma_start(w_raw[:], w1.rearrange("(p j) c -> p j c", j=PACK))
+        word_table = keep.tile([P, T], I32, name="word_table", tag="slot_b", align_bytes=64)
+        nc.sync.dma_start(word_table[:], x_words[0].rearrange("p c r -> p (c r)").bitcast(I32))
+        nc.sync.dma_start(ent_sb[:], ent)
+
+        def load_rows(rows, t, name, tag):
+            tile = keep.tile([P, U], F32, name=name, tag=tag, align_bytes=64)
+            nc.sync.dma_start(tile[:], rows[t])
+            return tile
+
+        par_sb = [load_rows(par_rows, 0, "par0", "par0")]
+        ssq_sb = [load_rows(ssq_rows, 0, "ssq0", "slot_d")]
+
+        picked_scales = keep.tile([P, S], U8, name="picked_scales", align_bytes=64)
+        nc.vector.tensor_copy(picked_scales[:], scale_table[:].indirect(offs_sb[:]))
+        x_plane = keep.tile([P, S], U8, name="x_plane", align_bytes=64)
+        nc.vector.tensor_copy(x_plane[:].bitcast(I32), picked_scales[:].bitcast(I32))
+        for r in range(2):
+            nc.scalar.dma_start(x_plane[2 + r : P : 32, :].bitcast(I32), picked_scales[16 + r : P : 32, :].bitcast(I32))
+
+        w_cols = w_raw[:].rearrange("p j (m t) -> p m t j", t=BLOCKS)
+        w_codes = keep.tile([P, N], U32, name="w_codes", align_bytes=64)
+        w_plane = keep.tile([P, N], U8, name="w_plane", align_bytes=64)
+        w_lo = keep.tile([P, 2, P, PACK], BF16, name="w_lo", align_bytes=64)
+        w_hi = keep.tile([P, 2, P, PACK], BF16, name="w_hi", tag="slot_c", align_bytes=64)
+        nc.vector.tensor_copy(w_lo[:].rearrange("p t m j -> p m t j"), w_cols[:, :, 0:2, :])
+        nc.scalar.copy(w_hi[:].rearrange("p t m j -> p m t j"), w_cols[:, :, 2:4, :])
+
+        def quantize(half, w_bf):
+            cols = slice(half * 2 * P, (half + 1) * 2 * P)
+            nc.vector.quantize_mx(
+                out=w_codes[:, cols].bitcast(FP8X4),
+                scales=w_plane[:, cols],
+                in_=w_bf[:].rearrange("p t m j -> p (t m j)"),
+            )
+
+        quantize(0, w_lo)
+        x_codes = keep.tile([P, S], U32, name="x_codes", align_bytes=64)
+        nc.vector.tensor_copy(x_codes[:], word_table[:].bitcast(U32).indirect(offs_sb[:]))
+        quantize(1, w_hi)
+
+        ssq_sb.append(load_rows(ssq_rows, 1, "ssq1", "slot_a"))
+        par_sb.append(load_rows(par_rows, 1, "par1", "slot_b"))
+        par_sb.append(load_rows(par_rows, 2, "par2", "slot_c"))
+
+        y = []
+        y_sq = []
+        for t in range(BLOCKS):
+            cols = slice(t * P, (t + 1) * P)
+            bank = psum.tile([P, S], F32, name="y%d" % t)
+            nc.tensor.matmul_mx(
+                out=bank[:],
+                lhsT=w_codes[:, cols].bitcast(FP8X4),
+                lhsT_scale=w_plane[:, cols],
+                rhs=x_codes[:].bitcast(FP8X4),
+                rhs_scale=x_plane[:],
+                start=True,
+                stop=True,
+            )
+            sq = keep.tile([P, S], F32, name="y_sq%d" % t)
+            nc.scalar.activation(sq[:], bank[:], ACT.Square)
+            y.append(bank)
+            y_sq.append(sq)
+
+        def fetch_par(t):
+            old = work.tile([P, S], F32, name="old")
+            nc.vector.tensor_copy(old[:], par_sb[t][:].indirect(ent_sb[:]))
+            return old
+
+        def inverse_root(t):
+            total = work.tile([P, S], F32, name="total")
+            nc.vector.tensor_tensor(total[:], ssq_sb[t][:].indirect(ent_sb[:]), y_sq[t][:], ALU.add)
+            inv = work.tile([P, S], F32, name="inv")
+            nc.scalar.activation(inv[:], total[:], ACT.Abs_reciprocal_sqrt)
+            return inv
+
+        old = fetch_par(0)
+        inv = inverse_root(0)
+        ssq_sb.append(load_rows(ssq_rows, 2, "ssq2", "slot_d"))
+        for t in range(BLOCKS):
+            step = work.tile([P, S], F32, name="step")
+            nc.vector.scalar_tensor_tensor(step[:], y[t][:], -1.0, inv[:], ALU.mult, ALU.mult)
+            if t + 1 < BLOCKS:
+                inv = inverse_root(t + 1)
+            if t == 0:
+                ssq_sb.append(load_rows(ssq_rows, 3, "ssq3", "slot_a"))
+            if t == 1:
+                par_sb.append(load_rows(par_rows, 3, "par3", "slot_d"))
+            nc.vector.tensor_tensor(par_sb[t][:].indirect(ent_sb[:]), old[:], step[:], ALU.add)
+            nc.sync.dma_start(out_rows[t], par_sb[t][:])
+            if t + 1 < BLOCKS:
+                old = fetch_par(t + 1)

@@ -28,6 +28,7 @@ def tile_picked_adagr8_none_p_kernel(tc, x_words, x_scales, w1, par, ssq, offs, 
 
     with ExitStack() as ctx:
         lists = ctx.enter_context(tc.tile_pool(name="lists", bufs=1))
+        first = ctx.enter_context(tc.tile_pool(name="first", bufs=1))
         keep = ctx.enter_context(tc.tile_pool(name="keep", bufs=1))
         work = ctx.enter_context(tc.tile_pool(name="work", bufs=2))
         psum = ctx.enter_context(tc.psum_pool(name="psum", bufs=1))
@@ -36,31 +37,38 @@ def tile_picked_adagr8_none_p_kernel(tc, x_words, x_scales, w1, par, ssq, offs, 
         ent_sb = lists.tile([P, S // 16], U16, name="ent_sb")
         nc.sync.dma_start(offs_sb[:], offs)
 
-        scale_table = keep.tile([P, T], U8, name="scale_table", align_bytes=64)
+        nc.sync.dma_start(ent_sb[:], ent)
+
+        scale_table = first.tile([P, T], U8, name="scale_table", align_bytes=64, offset=3072)
         nc.vector.memset(scale_table[:].bitcast(I32), 0)
-        for r in range(2):
-            nc.scalar.dma_start(scale_table[r:P:16, :].bitcast(I32), x_scales[0, r:16:2, :].bitcast(I32))
+        nc.sync.dma_start(scale_table[0:P:8, :].bitcast(I32), x_scales[0].bitcast(I32))
+        x_plane = keep.tile([P, S], U8, name="x_plane", align_bytes=64)
+        nc.vector.memset(x_plane[:].bitcast(I32), 0)
+        warm = keep.tile([P, 8], F32, name="warm")
+        nc.gpsimd.memset(warm[:, 0:1], 1.0)
+        warm_out = keep.tile([P, 8], F32, name="warm_out")
+        nc.scalar.activation(warm_out[:, 0:1], warm[:, 0:1], ACT.Abs_reciprocal_sqrt)
 
         w_raw = keep.tile([P, PACK, N], F32, name="w_raw", tag="slot_a", align_bytes=64)
         nc.sync.dma_start(w_raw[:], w1.rearrange("(p j) c -> p j c", j=PACK))
         word_table = keep.tile([P, T], I32, name="word_table", tag="slot_b", align_bytes=64)
         nc.sync.dma_start(word_table[:], x_words[0].rearrange("p c r -> p (c r)").bitcast(I32))
-        nc.sync.dma_start(ent_sb[:], ent)
 
         def load_rows(rows, t, name, tag):
             tile = keep.tile([P, U], F32, name=name, tag=tag, align_bytes=64)
             nc.sync.dma_start(tile[:], rows[t])
             return tile
 
-        par_sb = [load_rows(par_rows, 0, "par0", "par0")]
-        ssq_sb = [load_rows(ssq_rows, 0, "ssq0", "slot_d")]
-
         picked_scales = keep.tile([P, S], U8, name="picked_scales", align_bytes=64)
         nc.vector.tensor_copy(picked_scales[:], scale_table[:].indirect(offs_sb[:]))
-        x_plane = keep.tile([P, S], U8, name="x_plane", align_bytes=64)
-        nc.vector.tensor_copy(x_plane[:].bitcast(I32), picked_scales[:].bitcast(I32))
-        for r in range(2):
-            nc.scalar.dma_start(x_plane[2 + r : P : 32, :].bitcast(I32), picked_scales[16 + r : P : 32, :].bitcast(I32))
+        for r in range(4):
+            nc.sync.dma_start(x_plane[r:P:32, :].bitcast(I32), picked_scales[8 * r : P : 32, :].bitcast(I32))
+        par0 = first.tile([P, U], F32, name="par0", align_bytes=64, offset=0)
+        nc.sync.dma_start(par0[:], par_rows[0])
+        ssq0 = first.tile([P, U], F32, name="ssq0", align_bytes=64, offset=4096)
+        nc.sync.dma_start(ssq0[:], ssq_rows[0])
+        par_sb = [par0]
+        ssq_sb = [ssq0]
 
         w_cols = w_raw[:].rearrange("p j (m t) -> p m t j", t=BLOCKS)
         w_codes = keep.tile([P, N], U32, name="w_codes", align_bytes=64)
@@ -120,7 +128,9 @@ def tile_picked_adagr8_none_p_kernel(tc, x_words, x_scales, w1, par, ssq, offs, 
 
         old = fetch_par(0)
         inv = inverse_root(0)
-        ssq_sb.append(load_rows(ssq_rows, 2, "ssq2", "slot_d"))
+        ssq2 = first.tile([P, U], F32, name="ssq2", align_bytes=64, offset=4096)
+        nc.sync.dma_start(ssq2[:], ssq_rows[2])
+        ssq_sb.append(ssq2)
         for t in range(BLOCKS):
             step = work.tile([P, S], F32, name="step")
             nc.vector.scalar_tensor_tensor(step[:], y[t][:], -1.0, inv[:], ALU.mult, ALU.mult)
@@ -129,7 +139,9 @@ def tile_picked_adagr8_none_p_kernel(tc, x_words, x_scales, w1, par, ssq, offs, 
             if t == 0:
                 ssq_sb.append(load_rows(ssq_rows, 3, "ssq3", "slot_a"))
             if t == 1:
-                par_sb.append(load_rows(par_rows, 3, "par3", "slot_d"))
+                par3 = first.tile([P, U], F32, name="par3", align_bytes=64, offset=4096)
+                nc.sync.dma_start(par3[:], par_rows[3])
+                par_sb.append(par3)
             nc.vector.tensor_tensor(par_sb[t][:].indirect(ent_sb[:]), old[:], step[:], ALU.add)
             nc.sync.dma_start(out_rows[t], par_sb[t][:])
             if t + 1 < BLOCKS:

@@ -18,6 +18,7 @@ ACT = mybir.ActivationFunctionType
 P = 128
 PACK = 4
 BLOCKS = N // P
+HALF = S // 2
 
 
 def tile_picked_adagr8_none_p_kernel(tc, x_words, x_scales, w1, par, ssq, offs, ent, out):
@@ -30,14 +31,15 @@ def tile_picked_adagr8_none_p_kernel(tc, x_words, x_scales, w1, par, ssq, offs, 
         lists = ctx.enter_context(tc.tile_pool(name="lists", bufs=1))
         first = ctx.enter_context(tc.tile_pool(name="first", bufs=1))
         keep = ctx.enter_context(tc.tile_pool(name="keep", bufs=1))
-        work = ctx.enter_context(tc.tile_pool(name="work", bufs=2))
         psum = ctx.enter_context(tc.psum_pool(name="psum", bufs=1))
 
         offs_sb = lists.tile([P, S // 16], U16, name="offs_sb")
         ent_sb = lists.tile([P, S // 16], U16, name="ent_sb")
         nc.sync.dma_start(offs_sb[:], offs)
 
-        nc.sync.dma_start(ent_sb[:], ent)
+        w_raw = first.tile([P, PACK, N], F32, name="w_raw", align_bytes=64, offset=10240)
+        w_rows = w1.rearrange("(p j) c -> p j c", j=PACK)
+        nc.sync.dma_start(w_raw[:, 0:1, :], w_rows[:, 0:1, :])
 
         scale_table = first.tile([P, T], U8, name="scale_table", align_bytes=64, offset=3072)
         nc.vector.memset(scale_table[:].bitcast(I32), 0)
@@ -49,13 +51,13 @@ def tile_picked_adagr8_none_p_kernel(tc, x_words, x_scales, w1, par, ssq, offs, 
         warm_out = keep.tile([P, 8], F32, name="warm_out")
         nc.scalar.activation(warm_out[:, 0:1], warm[:, 0:1], ACT.Abs_reciprocal_sqrt)
 
-        w_raw = keep.tile([P, PACK, N], F32, name="w_raw", tag="slot_a", align_bytes=64)
-        nc.sync.dma_start(w_raw[:], w1.rearrange("(p j) c -> p j c", j=PACK))
-        word_table = keep.tile([P, T], I32, name="word_table", tag="slot_b", align_bytes=64)
+        nc.sync.dma_start(w_raw[:, 1:PACK, :], w_rows[:, 1:PACK, :])
+        word_table = first.tile([P, T], I32, name="word_table", align_bytes=64, offset=22528)
         nc.sync.dma_start(word_table[:], x_words[0].rearrange("p c r -> p (c r)").bitcast(I32))
+        nc.sync.dma_start(ent_sb[:], ent)
 
-        def load_rows(rows, t, name, tag):
-            tile = keep.tile([P, U], F32, name=name, tag=tag, align_bytes=64)
+        def load_rows(rows, t, name, offset):
+            tile = first.tile([P, U], F32, name=name, align_bytes=64, offset=offset)
             nc.sync.dma_start(tile[:], rows[t])
             return tile
 
@@ -74,7 +76,7 @@ def tile_picked_adagr8_none_p_kernel(tc, x_words, x_scales, w1, par, ssq, offs, 
         w_codes = keep.tile([P, N], U32, name="w_codes", align_bytes=64)
         w_plane = keep.tile([P, N], U8, name="w_plane", align_bytes=64)
         w_lo = keep.tile([P, 2, P, PACK], BF16, name="w_lo", align_bytes=64)
-        w_hi = keep.tile([P, 2, P, PACK], BF16, name="w_hi", tag="slot_c", align_bytes=64)
+        w_hi = keep.tile([P, 2, P, PACK], BF16, name="w_hi", align_bytes=64)
         nc.vector.tensor_copy(w_lo[:].rearrange("p t m j -> p m t j"), w_cols[:, :, 0:2, :])
         nc.scalar.copy(w_hi[:].rearrange("p t m j -> p m t j"), w_cols[:, :, 2:4, :])
 
@@ -88,61 +90,81 @@ def tile_picked_adagr8_none_p_kernel(tc, x_words, x_scales, w1, par, ssq, offs, 
 
         quantize(0, w_lo)
         x_codes = keep.tile([P, S], U32, name="x_codes", align_bytes=64)
-        nc.vector.tensor_copy(x_codes[:], word_table[:].bitcast(U32).indirect(offs_sb[:]))
+        for h in range(2):
+            nc.vector.tensor_copy(
+                x_codes[:, h * HALF : (h + 1) * HALF],
+                word_table[:].bitcast(U32).indirect(offs_sb[:, h * HALF // 16 : (h + 1) * HALF // 16]),
+            )
         quantize(1, w_hi)
 
-        ssq_sb.append(load_rows(ssq_rows, 1, "ssq1", "slot_a"))
-        par_sb.append(load_rows(par_rows, 1, "par1", "slot_b"))
-        par_sb.append(load_rows(par_rows, 2, "par2", "slot_c"))
+        for t in range(1, BLOCKS):
+            ssq_sb.append(load_rows(ssq_rows, t, "ssq%d" % t, 4096 * (1 + t)))
+        for t in range(1, BLOCKS):
+            par_sb.append(load_rows(par_rows, t, "par%d" % t, 4096 * (4 + t)))
 
-        y = []
-        y_sq = []
-        for t in range(BLOCKS):
+        def product(t):
             cols = slice(t * P, (t + 1) * P)
             bank = psum.tile([P, S], F32, name="y%d" % t)
-            nc.tensor.matmul_mx(
-                out=bank[:],
-                lhsT=w_codes[:, cols].bitcast(FP8X4),
-                lhsT_scale=w_plane[:, cols],
-                rhs=x_codes[:].bitcast(FP8X4),
-                rhs_scale=x_plane[:],
-                start=True,
-                stop=True,
-            )
-            sq = keep.tile([P, S], F32, name="y_sq%d" % t)
-            nc.scalar.activation(sq[:], bank[:], ACT.Square)
-            y.append(bank)
-            y_sq.append(sq)
+            width = HALF if t == 0 else S
+            for start in range(0, S, width):
+                picked = slice(start, start + width)
+                nc.tensor.matmul_mx(
+                    out=bank[:, picked],
+                    lhsT=w_codes[:, cols].bitcast(FP8X4),
+                    lhsT_scale=w_plane[:, cols],
+                    rhs=x_codes[:, picked].bitcast(FP8X4),
+                    rhs_scale=x_plane[:, picked],
+                    start=True,
+                    stop=True,
+                )
+            return bank
+
+        y = [product(t) for t in range(BLOCKS)]
+
+        def square(t):
+            sq = keep.tile([P, S], F32, name="y_sq%d" % t, align_bytes=64)
+            nc.scalar.activation(sq[:], y[t][:], ACT.Square)
+            return sq
 
         def fetch_par(t):
-            old = work.tile([P, S], F32, name="old")
+            old = keep.tile([P, S], F32, name="old%d" % t)
             nc.vector.tensor_copy(old[:], par_sb[t][:].indirect(ent_sb[:]))
             return old
 
-        def inverse_root(t):
-            total = work.tile([P, S], F32, name="total")
-            nc.vector.tensor_tensor(total[:], ssq_sb[t][:].indirect(ent_sb[:]), y_sq[t][:], ALU.add)
-            inv = work.tile([P, S], F32, name="inv")
+        def inverse_root(t, sq):
+            total = keep.tile([P, S], F32, name="total%d" % t)
+            nc.vector.tensor_tensor(total[:], ssq_sb[t][:].indirect(ent_sb[:]), sq[:], ALU.add)
+            inv = keep.tile([P, S], F32, name="inv%d" % t)
             nc.scalar.activation(inv[:], total[:], ACT.Abs_reciprocal_sqrt)
             return inv
 
-        old = fetch_par(0)
-        inv = inverse_root(0)
-        ssq2 = first.tile([P, U], F32, name="ssq2", align_bytes=64, offset=4096)
-        nc.sync.dma_start(ssq2[:], ssq_rows[2])
-        ssq_sb.append(ssq2)
-        for t in range(BLOCKS):
-            step = work.tile([P, S], F32, name="step")
-            nc.vector.scalar_tensor_tensor(step[:], y[t][:], -1.0, inv[:], ALU.mult, ALU.mult)
-            if t + 1 < BLOCKS:
-                inv = inverse_root(t + 1)
-            if t == 0:
-                ssq_sb.append(load_rows(ssq_rows, 3, "ssq3", "slot_a"))
-            if t == 1:
-                par3 = first.tile([P, U], F32, name="par3", align_bytes=64, offset=4096)
-                nc.sync.dma_start(par3[:], par_rows[3])
-                par_sb.append(par3)
-            nc.vector.tensor_tensor(par_sb[t][:].indirect(ent_sb[:]), old[:], step[:], ALU.add)
+        def step_of(t):
+            y_sb = keep.tile([P, S], F32, name="y_sb%d" % t)
+            nc.scalar.copy(y_sb[:], y[t][:])
+            step = keep.tile([P, S], F32, name="step")
+            nc.gpsimd.tensor_tensor(step[:], y_sb[:], inv[t][:], ALU.mult)
+            return step
+
+        def new_values(t, old, step):
+            new = keep.tile([P, S], F32, name="new%d" % t)
+            nc.gpsimd.tensor_tensor(new[:], old[:], step[:], ALU.subtract)
+            return new
+
+        def put_back(t, new):
+            nc.vector.tensor_copy(par_sb[t][:].indirect(ent_sb[:]), new[:])
             nc.sync.dma_start(out_rows[t], par_sb[t][:])
-            if t + 1 < BLOCKS:
-                old = fetch_par(t + 1)
+
+        old = [fetch_par(0)]
+        squares = [square(t) for t in range(2)]
+        inv = []
+        for t in range(BLOCKS):
+            inv.append(inverse_root(t, squares[t]))
+            if t + 2 < BLOCKS:
+                squares.append(square(t + 2))
+        last = BLOCKS - 1
+        old.extend(fetch_par(t) for t in range(1, last))
+        new_last = keep.tile([P, S], F32, name="new_last")
+        nc.vector.tensor_tensor(new_last[:], par_sb[last][:].indirect(ent_sb[:]), step_of(last)[:], ALU.subtract)
+        put_back(last, new_last)
+        for t in range(last):
+            put_back(t, new_values(t, old[t], step_of(t)))

@@ -17,8 +17,14 @@ ACT = mybir.ActivationFunctionType
 
 P = 128
 PACK = 4
+GROUP = 16
+QUADRANT = 32
+BLOCK_ROWS = 8
 BLOCKS = N // P
 HALF = S // 2
+ALIGN = 64
+VECTOR_COLS = 80
+SLOT = U * 4
 
 
 def tile_picked_adagr8_none_p_kernel(tc, x_words, x_scales, w1, par, ssq, offs, ent, out):
@@ -26,90 +32,88 @@ def tile_picked_adagr8_none_p_kernel(tc, x_words, x_scales, w1, par, ssq, offs, 
     par_rows = par.rearrange("(p t) u -> t p u", t=BLOCKS)
     ssq_rows = ssq.rearrange("(p t) u -> t p u", t=BLOCKS)
     out_rows = out.rearrange("(p t) u -> t p u", t=BLOCKS)
+    w_rows = w1.rearrange("(p r) c -> p r c", r=PACK)
 
     with ExitStack() as ctx:
         lists = ctx.enter_context(tc.tile_pool(name="lists", bufs=1))
-        first = ctx.enter_context(tc.tile_pool(name="first", bufs=1))
+        staged = ctx.enter_context(tc.tile_pool(name="staged", bufs=1))
         keep = ctx.enter_context(tc.tile_pool(name="keep", bufs=1))
         psum = ctx.enter_context(tc.psum_pool(name="psum", bufs=1))
 
-        offs_sb = lists.tile([P, S // 16], U16, name="offs_sb")
-        ent_sb = lists.tile([P, S // 16], U16, name="ent_sb")
-        nc.sync.dma_start(offs_sb[:], offs)
+        scale_table = staged.tile([P, T], U8, name="scale_table", align_bytes=ALIGN, offset=SLOT - T // 2)
+        w_raw = staged.tile([P, PACK, N], F32, name="w_raw", align_bytes=ALIGN, offset=2 * SLOT + SLOT // 2)
+        word_table = staged.tile([P, T], I32, name="word_table", align_bytes=ALIGN, offset=5 * SLOT + SLOT // 2)
+        offs_sb = lists.tile([P, S // GROUP], U16, name="offs_sb")
+        ent_sb = lists.tile([P, S // GROUP], U16, name="ent_sb")
 
-        w_raw = first.tile([P, PACK, N], F32, name="w_raw", align_bytes=64, offset=10240)
-        w_rows = w1.rearrange("(p j) c -> p j c", j=PACK)
-        nc.sync.dma_start(w_raw[:, 0:1, :], w_rows[:, 0:1, :])
-
-        scale_table = first.tile([P, T], U8, name="scale_table", align_bytes=64, offset=3072)
-        nc.vector.memset(scale_table[:].bitcast(I32), 0)
-        nc.sync.dma_start(scale_table[0:P:8, :].bitcast(I32), x_scales[0].bitcast(I32))
-        x_plane = keep.tile([P, S], U8, name="x_plane", align_bytes=64)
-        nc.vector.memset(x_plane[:].bitcast(I32), 0)
-        warm = keep.tile([P, 8], F32, name="warm")
-        nc.gpsimd.memset(warm[:, 0:1], 1.0)
-        warm_out = keep.tile([P, 8], F32, name="warm_out")
-        nc.scalar.activation(warm_out[:, 0:1], warm[:, 0:1], ACT.Abs_reciprocal_sqrt)
-
-        nc.sync.dma_start(w_raw[:, 1:PACK, :], w_rows[:, 1:PACK, :])
-        word_table = first.tile([P, T], I32, name="word_table", align_bytes=64, offset=22528)
-        nc.sync.dma_start(word_table[:], x_words[0].rearrange("p c r -> p (c r)").bitcast(I32))
-        nc.sync.dma_start(ent_sb[:], ent)
-
-        def load_rows(rows, t, name, offset):
-            tile = first.tile([P, U], F32, name=name, align_bytes=64, offset=offset)
+        def load_block(rows, t, name, slot):
+            tile = staged.tile([P, U], F32, name="%s%d" % (name, t), align_bytes=ALIGN, offset=slot * SLOT)
             nc.sync.dma_start(tile[:], rows[t])
             return tile
 
-        picked_scales = keep.tile([P, S], U8, name="picked_scales", align_bytes=64)
+        nc.sync.dma_start(w_raw[:, 0:1, :], w_rows[:, 0:1, :])
+        nc.sync.dma_start(offs_sb[:], offs)
+        nc.vector.memset(scale_table[:].bitcast(I32), 0)
+        nc.sync.dma_start(scale_table[0:P:BLOCK_ROWS, :].bitcast(I32), x_scales[0].bitcast(I32))
+        x_plane = keep.tile([P, S], U8, name="x_plane", align_bytes=ALIGN)
+        nc.vector.memset(x_plane[:].bitcast(I32), 0)
+
+        warm_in = keep.tile([P, 1], F32, name="warm_in")
+        warm_out = keep.tile([P, 1], F32, name="warm_out")
+        nc.gpsimd.memset(warm_in[:], 1.0)
+        nc.scalar.activation(warm_out[:], warm_in[:], ACT.Abs_reciprocal_sqrt)
+
+        nc.sync.dma_start(w_raw[:, 1:PACK, :], w_rows[:, 1:PACK, :])
+        nc.sync.dma_start(word_table[:], x_words[0].rearrange("p c r -> p (c r)").bitcast(I32))
+        nc.sync.dma_start(ent_sb[:], ent)
+
+        picked_scales = keep.tile([P, S], U8, name="picked_scales", align_bytes=ALIGN)
         nc.vector.tensor_copy(picked_scales[:], scale_table[:].indirect(offs_sb[:]))
-        for r in range(4):
-            nc.sync.dma_start(x_plane[r:P:32, :].bitcast(I32), picked_scales[8 * r : P : 32, :].bitcast(I32))
-        par0 = first.tile([P, U], F32, name="par0", align_bytes=64, offset=0)
-        nc.sync.dma_start(par0[:], par_rows[0])
-        ssq0 = first.tile([P, U], F32, name="ssq0", align_bytes=64, offset=4096)
-        nc.sync.dma_start(ssq0[:], ssq_rows[0])
-        par_sb = [par0]
-        ssq_sb = [ssq0]
+        for i in range(QUADRANT // BLOCK_ROWS):
+            nc.sync.dma_start(
+                x_plane[i:P:QUADRANT, :].bitcast(I32),
+                picked_scales[BLOCK_ROWS * i : P : QUADRANT, :].bitcast(I32),
+            )
 
-        w_cols = w_raw[:].rearrange("p j (m t) -> p m t j", t=BLOCKS)
-        w_codes = keep.tile([P, N], U32, name="w_codes", align_bytes=64)
-        w_plane = keep.tile([P, N], U8, name="w_plane", align_bytes=64)
-        w_lo = keep.tile([P, 2, P, PACK], BF16, name="w_lo", align_bytes=64)
-        w_hi = keep.tile([P, 2, P, PACK], BF16, name="w_hi", align_bytes=64)
-        nc.vector.tensor_copy(w_lo[:].rearrange("p t m j -> p m t j"), w_cols[:, :, 0:2, :])
-        nc.scalar.copy(w_hi[:].rearrange("p t m j -> p m t j"), w_cols[:, :, 2:4, :])
+        par_sb = {1: load_block(par_rows, 1, "par", 0)}
+        ssq_sb = {0: load_block(ssq_rows, 0, "ssq", 1)}
 
-        def quantize(half, w_bf):
-            cols = slice(half * 2 * P, (half + 1) * 2 * P)
+        w_bf = keep.tile([P, BLOCKS, P, PACK], BF16, name="w_bf", align_bytes=ALIGN)
+        w_from = w_raw[:].rearrange("p r (m t) -> p m t r", t=BLOCKS)
+        w_to = w_bf[:].rearrange("p t m r -> p m t r")
+        nc.vector.tensor_copy(w_to[:, 0:VECTOR_COLS], w_from[:, 0:VECTOR_COLS])
+        nc.scalar.copy(w_to[:, VECTOR_COLS:P], w_from[:, VECTOR_COLS:P])
+        w_codes = keep.tile([P, N], U32, name="w_codes", align_bytes=ALIGN)
+        w_plane = keep.tile([P, N], U8, name="w_plane", align_bytes=ALIGN)
+        for t in range(0, BLOCKS, 2):
+            cols = slice(t * P, (t + 2) * P)
             nc.vector.quantize_mx(
                 out=w_codes[:, cols].bitcast(FP8X4),
                 scales=w_plane[:, cols],
-                in_=w_bf[:].rearrange("p t m j -> p (t m j)"),
+                in_=w_bf[:, t : t + 2].rearrange("p t m r -> p (t m r)"),
             )
 
-        quantize(0, w_lo)
-        x_codes = keep.tile([P, S], U32, name="x_codes", align_bytes=64)
-        for h in range(2):
+        x_codes = keep.tile([P, S], U32, name="x_codes", align_bytes=ALIGN)
+        for start in range(0, S, HALF):
             nc.vector.tensor_copy(
-                x_codes[:, h * HALF : (h + 1) * HALF],
-                word_table[:].bitcast(U32).indirect(offs_sb[:, h * HALF // 16 : (h + 1) * HALF // 16]),
+                x_codes[:, start : start + HALF],
+                word_table[:].bitcast(U32).indirect(offs_sb[:, start // GROUP : (start + HALF) // GROUP]),
             )
-        quantize(1, w_hi)
 
         for t in range(1, BLOCKS):
-            ssq_sb.append(load_rows(ssq_rows, t, "ssq%d" % t, 4096 * (1 + t)))
-        for t in range(1, BLOCKS):
-            par_sb.append(load_rows(par_rows, t, "par%d" % t, 4096 * (4 + t)))
+            ssq_sb[t] = load_block(ssq_rows, t, "ssq", 1 + t)
+        for slot, t in ((5, 2), (6, 3), (7, 0)):
+            par_sb[t] = load_block(par_rows, t, "par", slot)
 
         def product(t):
             cols = slice(t * P, (t + 1) * P)
-            bank = psum.tile([P, S], F32, name="y%d" % t)
             width = HALF if t == 0 else S
+            pieces = []
             for start in range(0, S, width):
                 picked = slice(start, start + width)
+                bank = psum.tile([P, width], F32, name="y%d_%d" % (t, start))
                 nc.tensor.matmul_mx(
-                    out=bank[:, picked],
+                    out=bank[:],
                     lhsT=w_codes[:, cols].bitcast(FP8X4),
                     lhsT_scale=w_plane[:, cols],
                     rhs=x_codes[:, picked].bitcast(FP8X4),
@@ -117,54 +121,57 @@ def tile_picked_adagr8_none_p_kernel(tc, x_words, x_scales, w1, par, ssq, offs, 
                     start=True,
                     stop=True,
                 )
-            return bank
+                pieces.append((picked, bank))
+            return pieces
 
         y = [product(t) for t in range(BLOCKS)]
 
         def square(t):
-            sq = keep.tile([P, S], F32, name="y_sq%d" % t, align_bytes=64)
-            nc.scalar.activation(sq[:], y[t][:], ACT.Square)
-            return sq
+            y_sq = keep.tile([P, S], F32, name="y_sq%d" % t)
+            for picked, bank in y[t]:
+                nc.scalar.activation(y_sq[:, picked], bank[:], ACT.Square)
+            return y_sq
+
+        def copy_out(t):
+            y_sb = keep.tile([P, S], F32, name="y_sb%d" % t)
+            for picked, bank in y[t]:
+                nc.scalar.copy(y_sb[:, picked], bank[:])
+            return y_sb
 
         def fetch_par(t):
             old = keep.tile([P, S], F32, name="old%d" % t)
             nc.vector.tensor_copy(old[:], par_sb[t][:].indirect(ent_sb[:]))
             return old
 
-        def inverse_root(t, sq):
+        def inverse_root(t, y_sq):
             total = keep.tile([P, S], F32, name="total%d" % t)
-            nc.vector.tensor_tensor(total[:], ssq_sb[t][:].indirect(ent_sb[:]), sq[:], ALU.add)
+            nc.vector.tensor_tensor(total[:], ssq_sb[t][:].indirect(ent_sb[:]), y_sq[:], ALU.add)
             inv = keep.tile([P, S], F32, name="inv%d" % t)
             nc.scalar.activation(inv[:], total[:], ACT.Abs_reciprocal_sqrt)
             return inv
 
-        def step_of(t):
-            y_sb = keep.tile([P, S], F32, name="y_sb%d" % t)
-            nc.scalar.copy(y_sb[:], y[t][:])
-            step = keep.tile([P, S], F32, name="step")
-            nc.gpsimd.tensor_tensor(step[:], y_sb[:], inv[t][:], ALU.mult)
+        def step_of(y_sb, inv):
+            step = keep.tile([P, S], F32, name="step", tag="y_sq%d" % (BLOCKS - 1))
+            nc.gpsimd.tensor_tensor(step[:], y_sb[:], inv[:], ALU.mult)
             return step
-
-        def new_values(t, old, step):
-            new = keep.tile([P, S], F32, name="new%d" % t)
-            nc.gpsimd.tensor_tensor(new[:], old[:], step[:], ALU.subtract)
-            return new
 
         def put_back(t, new):
             nc.vector.tensor_copy(par_sb[t][:].indirect(ent_sb[:]), new[:])
             nc.sync.dma_start(out_rows[t], par_sb[t][:])
 
-        old = [fetch_par(0)]
-        squares = [square(t) for t in range(2)]
-        inv = []
-        for t in range(BLOCKS):
-            inv.append(inverse_root(t, squares[t]))
-            if t + 2 < BLOCKS:
-                squares.append(square(t + 2))
-        last = BLOCKS - 1
-        old.extend(fetch_par(t) for t in range(1, last))
-        new_last = keep.tile([P, S], F32, name="new_last")
-        nc.vector.tensor_tensor(new_last[:], par_sb[last][:].indirect(ent_sb[:]), step_of(last)[:], ALU.subtract)
-        put_back(last, new_last)
-        for t in range(last):
-            put_back(t, new_values(t, old[t], step_of(t)))
+        old_par = {1: fetch_par(1)}
+        squares = [square(t) for t in range(BLOCKS)]
+        y_first = copy_out(0)
+        inverses = [inverse_root(t, squares[t]) for t in range(BLOCKS)]
+        for t in range(2, BLOCKS):
+            old_par[t] = fetch_par(t)
+
+        new_first = keep.tile([P, S], F32, name="new0")
+        step_first = step_of(y_first, inverses[0])
+        nc.vector.tensor_tensor(new_first[:], par_sb[0][:].indirect(ent_sb[:]), step_first[:], ALU.subtract)
+        put_back(0, new_first)
+        for t in range(1, BLOCKS):
+            step = step_of(copy_out(t), inverses[t])
+            new = keep.tile([P, S], F32, name="new%d" % t)
+            nc.gpsimd.tensor_tensor(new[:], old_par[t][:], step[:], ALU.subtract)
+            put_back(t, new)

@@ -25,6 +25,8 @@ HALF = S // 2
 ALIGN = 64
 VECTOR_COLS = 80
 SLOT = U * 4
+LAST = BLOCKS - 1
+TINY = 2.0**-126
 
 
 def tile_picked_adagr8_none_p_kernel(tc, x_words, x_scales, w1, par, ssq, offs, ent, out):
@@ -100,10 +102,12 @@ def tile_picked_adagr8_none_p_kernel(tc, x_words, x_scales, w1, par, ssq, offs, 
                 word_table[:].bitcast(U32).indirect(offs_sb[:, start // GROUP : (start + HALF) // GROUP]),
             )
 
-        for t in range(1, BLOCKS):
-            ssq_sb[t] = load_block(ssq_rows, t, "ssq", 1 + t)
-        for slot, t in ((5, 2), (6, 3), (7, 0)):
-            par_sb[t] = load_block(par_rows, t, "par", slot)
+        ssq_sb[1] = load_block(ssq_rows, 1, "ssq", 2)
+        par_sb[2] = load_block(par_rows, 2, "par", 3)
+        ssq_sb[2] = load_block(ssq_rows, 2, "ssq", 4)
+        par_sb[0] = load_block(par_rows, 0, "par", 5)
+        ssq_sb[LAST] = load_block(ssq_rows, LAST, "ssq", 6)
+        par_sb[LAST] = load_block(par_rows, LAST, "par", 7)
 
         def product(t):
             cols = slice(t * P, (t + 1) * P)
@@ -133,7 +137,7 @@ def tile_picked_adagr8_none_p_kernel(tc, x_words, x_scales, w1, par, ssq, offs, 
             return y_sq
 
         def copy_out(t):
-            y_sb = keep.tile([P, S], F32, name="y_sb%d" % t)
+            y_sb = keep.tile([P, S], F32, name="y_sb%d" % t, tag=("y_first", "total0", "total1", "y_sq1")[t])
             for picked, bank in y[t]:
                 nc.scalar.copy(y_sb[:, picked], bank[:])
             return y_sb
@@ -151,7 +155,7 @@ def tile_picked_adagr8_none_p_kernel(tc, x_words, x_scales, w1, par, ssq, offs, 
             return inv
 
         def step_of(y_sb, inv):
-            step = keep.tile([P, S], F32, name="step", tag="y_sq%d" % (BLOCKS - 1))
+            step = keep.tile([P, S], F32, name="step")
             nc.gpsimd.tensor_tensor(step[:], y_sb[:], inv[:], ALU.mult)
             return step
 
@@ -162,7 +166,8 @@ def tile_picked_adagr8_none_p_kernel(tc, x_words, x_scales, w1, par, ssq, offs, 
         old_par = {1: fetch_par(1)}
         squares = [square(t) for t in range(BLOCKS)]
         y_first = copy_out(0)
-        inverses = [inverse_root(t, squares[t]) for t in range(BLOCKS)]
+        inverses = [inverse_root(t, squares[t]) for t in range(LAST)]
+        y_rest = {t: copy_out(t) for t in range(1, BLOCKS)}
         for t in range(2, BLOCKS):
             old_par[t] = fetch_par(t)
 
@@ -170,8 +175,29 @@ def tile_picked_adagr8_none_p_kernel(tc, x_words, x_scales, w1, par, ssq, offs, 
         step_first = step_of(y_first, inverses[0])
         nc.vector.tensor_tensor(new_first[:], par_sb[0][:].indirect(ent_sb[:]), step_first[:], ALU.subtract)
         put_back(0, new_first)
-        for t in range(1, BLOCKS):
-            step = step_of(copy_out(t), inverses[t])
+        for t in range(1, LAST):
+            step = step_of(y_rest[t], inverses[t])
             new = keep.tile([P, S], F32, name="new%d" % t)
             nc.gpsimd.tensor_tensor(new[:], old_par[t][:], step[:], ALU.subtract)
             put_back(t, new)
+
+        root = keep.tile([P, U], F32, name="root")
+        nc.scalar.activation(root[:], ssq_sb[LAST][:], ACT.Abs_reciprocal_sqrt, bias=TINY)
+        log_root = keep.tile([P, U], F32, name="log_root")
+        nc.scalar.activation(log_root[:], root[:], ACT.Ln)
+        halves = [slice(start, start + HALF) for start in range(0, S, HALF)]
+        entries = [ent_sb[:, h.start // GROUP : h.stop // GROUP] for h in halves]
+        totals = keep.tile([P, S], F32, name="totals", tag="step")
+        sums = keep.tile([P, S], F32, name="sums")
+        for h, offsets in zip(halves, entries):
+            nc.scalar.activation(sums[:, h], log_root[:].indirect(offsets), ACT.Exp, scale=-2.0)
+            nc.gpsimd.tensor_tensor(totals[:, h], sums[:, h], squares[LAST][:, h], ALU.add)
+        inv = keep.tile([P, S], F32, name="inv_last")
+        step = keep.tile([P, S], F32, name="step_last")
+        new = keep.tile([P, S], F32, name="new_last")
+        for h, offsets in zip(halves, entries):
+            nc.scalar.activation(inv[:, h], totals[:, h], ACT.Abs_reciprocal_sqrt)
+            nc.gpsimd.tensor_tensor(step[:, h], y_rest[LAST][:, h], inv[:, h], ALU.mult)
+            nc.gpsimd.tensor_tensor(new[:, h], old_par[LAST][:, h], step[:, h], ALU.subtract)
+            nc.vector.tensor_copy(par_sb[LAST][:].indirect(offsets), new[:, h])
+        nc.sync.dma_start(out_rows[LAST], par_sb[LAST][:])

@@ -139,7 +139,10 @@ def tile_picked_adagr8_none_p_kernel(tc, x_words, x_scales, w1, par, ssq, offs, 
         def copy_out(t):
             y_sb = keep.tile([P, S], F32, name="y_sb%d" % t, tag=("y_first", "total0", "total1", "y_sq1")[t])
             for picked, bank in y[t]:
-                nc.scalar.copy(y_sb[:, picked], bank[:])
+                if t == LAST:
+                    nc.scalar.activation(y_sb[:, picked], bank[:], ACT.Copy, scale=-1.0)
+                else:
+                    nc.scalar.copy(y_sb[:, picked], bank[:])
             return y_sb
 
         def fetch_par(t):
@@ -185,19 +188,14 @@ def tile_picked_adagr8_none_p_kernel(tc, x_words, x_scales, w1, par, ssq, offs, 
         nc.scalar.activation(root[:], ssq_sb[LAST][:], ACT.Abs_reciprocal_sqrt, bias=TINY)
         log_root = keep.tile([P, U], F32, name="log_root")
         nc.scalar.activation(log_root[:], root[:], ACT.Ln)
-        halves = [slice(start, start + HALF) for start in range(0, S, HALF)]
-        entries = [ent_sb[:, h.start // GROUP : h.stop // GROUP] for h in halves]
-        totals = keep.tile([P, S], F32, name="totals", tag="step")
         sums = keep.tile([P, S], F32, name="sums")
-        for h, offsets in zip(halves, entries):
-            nc.scalar.activation(sums[:, h], log_root[:].indirect(offsets), ACT.Exp, scale=-2.0)
-            nc.gpsimd.tensor_tensor(totals[:, h], sums[:, h], squares[LAST][:, h], ALU.add)
+        nc.scalar.activation(sums[:], log_root[:].indirect(ent_sb[:]), ACT.Exp, scale=-2.0)
+        warm_again = keep.tile([P, 1], F32, name="warm_again")
+        nc.scalar.activation(warm_again[:], sums[:, S - 1 : S], ACT.Abs_reciprocal_sqrt)
+        total = keep.tile([P, S], F32, name="total_last", tag="step")
+        nc.gpsimd.tensor_tensor(total[:], sums[:], squares[LAST][:], ALU.add)
         inv = keep.tile([P, S], F32, name="inv_last")
-        step = keep.tile([P, S], F32, name="step_last")
-        new = keep.tile([P, S], F32, name="new_last")
-        for h, offsets in zip(halves, entries):
-            nc.scalar.activation(inv[:, h], totals[:, h], ACT.Abs_reciprocal_sqrt)
-            nc.gpsimd.tensor_tensor(step[:, h], y_rest[LAST][:, h], inv[:, h], ALU.mult)
-            nc.gpsimd.tensor_tensor(new[:, h], old_par[LAST][:, h], step[:, h], ALU.subtract)
-            nc.vector.tensor_copy(par_sb[LAST][:].indirect(offsets), new[:, h])
+        nc.scalar.activation(inv[:], total[:], ACT.Abs_reciprocal_sqrt)
+        minus_step = step_of(y_rest[LAST], inv)
+        nc.vector.tensor_tensor(par_sb[LAST][:].indirect(ent_sb[:]), old_par[LAST][:], minus_step[:], ALU.add)
         nc.sync.dma_start(out_rows[LAST], par_sb[LAST][:])

@@ -130,14 +130,17 @@ def tile_picked_adagr8_none_p_kernel(tc, x_words, x_scales, w1, par, ssq, offs, 
 
         y = [product(t) for t in range(BLOCKS)]
 
+        def work_tile(name, place):
+            return staged.tile([P, S], F32, name=name, align_bytes=ALIGN, offset=8 * SLOT + place * HALF * 4)
+
         def square(t):
-            y_sq = keep.tile([P, S], F32, name="y_sq%d" % t)
+            y_sq = work_tile("y_sq%d" % t, (1, 5, 10, 0)[t])
             for picked, bank in y[t]:
                 nc.scalar.activation(y_sq[:, picked], bank[:], ACT.Square)
             return y_sq
 
         def copy_out(t):
-            y_sb = keep.tile([P, S], F32, name="y_sb%d" % t, tag=("y_first", "total0", "total1", "y_sq1")[t])
+            y_sb = work_tile("y_sb%d" % t, (8, 4, 6, 2)[t])
             for picked, bank in y[t]:
                 if t == LAST:
                     nc.scalar.activation(y_sb[:, picked], bank[:], ACT.Copy, scale=-1.0)
@@ -167,10 +170,11 @@ def tile_picked_adagr8_none_p_kernel(tc, x_words, x_scales, w1, par, ssq, offs, 
             nc.sync.dma_start(out_rows[t], par_sb[t][:])
 
         old_par = {1: fetch_par(1)}
-        squares = [square(t) for t in range(BLOCKS)]
+        squares = [square(t) for t in range(LAST)]
         y_first = copy_out(0)
         inverses = [inverse_root(t, squares[t]) for t in range(LAST)]
-        y_rest = {t: copy_out(t) for t in range(1, BLOCKS)}
+        squares.append(square(LAST))
+        y_rest = {t: copy_out(t) for t in (LAST, 1, 2)}
         for t in range(2, BLOCKS):
             old_par[t] = fetch_par(t)
 

@@ -53,7 +53,7 @@ def tile_picked_adagr8_none_p_kernel(tc, x_words, x_scales, w1, par, ssq, offs, 
             nc.sync.dma_start(tile[:], rows[t])
             return tile
 
-        nc.sync.dma_start(w_raw[:, 0:1, :], w_rows[:, 0:1, :])
+        nc.sync.dma_start(w_raw[:, 0:2, :], w_rows[:, 0:2, :])
         nc.sync.dma_start(offs_sb[:], offs)
         nc.vector.memset(scale_table[:].bitcast(I32), 0)
         nc.sync.dma_start(scale_table[0:P:BLOCK_ROWS, :].bitcast(I32), x_scales[0].bitcast(I32))
@@ -65,9 +65,10 @@ def tile_picked_adagr8_none_p_kernel(tc, x_words, x_scales, w1, par, ssq, offs, 
         nc.gpsimd.memset(warm_in[:], 1.0)
         nc.scalar.activation(warm_out[:], warm_in[:], ACT.Abs_reciprocal_sqrt)
 
-        nc.sync.dma_start(w_raw[:, 1:PACK, :], w_rows[:, 1:PACK, :])
+        nc.sync.dma_start(w_raw[:, 2:PACK, :], w_rows[:, 2:PACK, :])
         nc.sync.dma_start(word_table[:], x_words[0].rearrange("p c r -> p (c r)").bitcast(I32))
         nc.sync.dma_start(ent_sb[:], ent)
+        par_sb = {1: load_block(par_rows, 1, "par", 11)}
 
         picked_scales = keep.tile([P, S], U8, name="picked_scales", align_bytes=ALIGN)
         nc.vector.tensor_copy(picked_scales[:], scale_table[:].indirect(offs_sb[:]))
@@ -77,7 +78,6 @@ def tile_picked_adagr8_none_p_kernel(tc, x_words, x_scales, w1, par, ssq, offs, 
                 picked_scales[BLOCK_ROWS * i : P : QUADRANT, :].bitcast(I32),
             )
 
-        par_sb = {1: load_block(par_rows, 1, "par", 0)}
         ssq_sb = {0: load_block(ssq_rows, 0, "ssq", 1)}
 
         w_bf = keep.tile([P, BLOCKS, P, PACK], BF16, name="w_bf", align_bytes=ALIGN)
@@ -154,10 +154,12 @@ def tile_picked_adagr8_none_p_kernel(tc, x_words, x_scales, w1, par, ssq, offs, 
             return old
 
         def inverse_root(t, y_sq):
-            total = keep.tile([P, S], F32, name="total%d" % t)
-            nc.vector.tensor_tensor(total[:], ssq_sb[t][:].indirect(ent_sb[:]), y_sq[:], ALU.add)
+            total = work_tile("total%d" % t, (10, 16, 18)[t])
             inv = keep.tile([P, S], F32, name="inv%d" % t)
-            nc.scalar.activation(inv[:], total[:], ACT.Abs_reciprocal_sqrt)
+            for picked, bank in y[t]:
+                offsets = ent_sb[:, picked.start // GROUP : picked.stop // GROUP]
+                nc.vector.tensor_tensor(total[:, picked], ssq_sb[t][:].indirect(offsets), y_sq[:, picked], ALU.add)
+                nc.scalar.activation(inv[:, picked], total[:, picked], ACT.Abs_reciprocal_sqrt)
             return inv
 
         def step_of(y_sb, inv):
@@ -170,10 +172,11 @@ def tile_picked_adagr8_none_p_kernel(tc, x_words, x_scales, w1, par, ssq, offs, 
             nc.sync.dma_start(out_rows[t], par_sb[t][:])
 
         old_par = {1: fetch_par(1)}
-        squares = [square(t) for t in range(LAST)]
+        squares = [square(0), square(1)]
         y_first = copy_out(0)
-        inverses = [inverse_root(t, squares[t]) for t in range(LAST)]
-        squares.append(square(LAST))
+        inverses = [inverse_root(0, squares[0])]
+        squares.extend([square(2), square(LAST)])
+        inverses.extend([inverse_root(1, squares[1]), inverse_root(2, squares[2])])
         y_rest = {t: copy_out(t) for t in (LAST, 1, 2)}
         for t in range(2, BLOCKS):
             old_par[t] = fetch_par(t)

@@ -19,44 +19,48 @@ P = 128
 PACK = 4
 GROUP = 16
 QUADRANT = 32
-BLOCK_ROWS = 8
-BLOCKS = N // P
-HALF = S // 2
+SCALE_STEP = 8
+PANELS = N // P
+LAST = PANELS - 1
 ALIGN = 64
+WHOLE = slice(0, S)
+HALVES = (slice(0, S // 2), slice(S // 2, S))
 VECTOR_COLS = 80
-SLOT = U * 4
-LAST = BLOCKS - 1
 TINY = 2.0**-126
+HALF_TILE = S * 4 // 2
 
 
 def tile_picked_adagr8_none_p_kernel(tc, x_words, x_scales, w1, par, ssq, offs, ent, out):
     nc = tc.nc
-    par_rows = par.rearrange("(p t) u -> t p u", t=BLOCKS)
-    ssq_rows = ssq.rearrange("(p t) u -> t p u", t=BLOCKS)
-    out_rows = out.rearrange("(p t) u -> t p u", t=BLOCKS)
+    par_rows = par.rearrange("(p t) u -> t p u", t=PANELS)
+    ssq_rows = ssq.rearrange("(p t) u -> t p u", t=PANELS)
+    out_rows = out.rearrange("(p t) u -> t p u", t=PANELS)
     w_rows = w1.rearrange("(p r) c -> p r c", r=PACK)
 
     with ExitStack() as ctx:
         lists = ctx.enter_context(tc.tile_pool(name="lists", bufs=1))
-        staged = ctx.enter_context(tc.tile_pool(name="staged", bufs=1))
         keep = ctx.enter_context(tc.tile_pool(name="keep", bufs=1))
+        shared = ctx.enter_context(tc.tile_pool(name="shared", bufs=1))
         psum = ctx.enter_context(tc.psum_pool(name="psum", bufs=1))
 
-        scale_table = staged.tile([P, T], U8, name="scale_table", align_bytes=ALIGN, offset=SLOT - T // 2)
-        w_raw = staged.tile([P, PACK, N], F32, name="w_raw", align_bytes=ALIGN, offset=2 * SLOT + SLOT // 2)
-        word_table = staged.tile([P, T], I32, name="word_table", align_bytes=ALIGN, offset=5 * SLOT + SLOT // 2)
         offs_sb = lists.tile([P, S // GROUP], U16, name="offs_sb")
         ent_sb = lists.tile([P, S // GROUP], U16, name="ent_sb")
+        scale_table = keep.tile([P, T], U8, name="scale_table", align_bytes=ALIGN)
+        word_table = keep.tile([P, T], I32, name="word_table", align_bytes=ALIGN)
+        w_raw = keep.tile([P, PACK, N], F32, name="w_raw", align_bytes=ALIGN)
 
-        def load_block(rows, t, name, slot):
-            tile = staged.tile([P, U], F32, name="%s%d" % (name, t), align_bytes=ALIGN, offset=slot * SLOT)
+        def offsets(list_sb, picked):
+            return list_sb[:, picked.start // GROUP : picked.stop // GROUP]
+
+        def load_panel(rows, t, name):
+            tile = keep.tile([P, U], F32, name="%s%d" % (name, t), align_bytes=ALIGN)
             nc.sync.dma_start(tile[:], rows[t])
             return tile
 
-        nc.sync.dma_start(w_raw[:, 0:2, :], w_rows[:, 0:2, :])
+        nc.sync.dma_start(w_raw[:, 0 : PACK // 2, :], w_rows[:, 0 : PACK // 2, :])
         nc.sync.dma_start(offs_sb[:], offs)
         nc.vector.memset(scale_table[:].bitcast(I32), 0)
-        nc.sync.dma_start(scale_table[0:P:BLOCK_ROWS, :].bitcast(I32), x_scales[0].bitcast(I32))
+        nc.sync.dma_start(scale_table[0:P:SCALE_STEP, :].bitcast(I32), x_scales[0].bitcast(I32))
         x_plane = keep.tile([P, S], U8, name="x_plane", align_bytes=ALIGN)
         nc.vector.memset(x_plane[:].bitcast(I32), 0)
 
@@ -65,29 +69,34 @@ def tile_picked_adagr8_none_p_kernel(tc, x_words, x_scales, w1, par, ssq, offs, 
         nc.gpsimd.memset(warm_in[:], 1.0)
         nc.scalar.activation(warm_out[:], warm_in[:], ACT.Abs_reciprocal_sqrt)
 
-        nc.sync.dma_start(w_raw[:, 2:PACK, :], w_rows[:, 2:PACK, :])
+        nc.sync.dma_start(w_raw[:, PACK // 2 : PACK, :], w_rows[:, PACK // 2 : PACK, :])
         nc.sync.dma_start(word_table[:], x_words[0].rearrange("p c r -> p (c r)").bitcast(I32))
         nc.sync.dma_start(ent_sb[:], ent)
-        par_sb = {1: load_block(par_rows, 1, "par", 11)}
+        par_sb = {1: load_panel(par_rows, 1, "par")}
 
         picked_scales = keep.tile([P, S], U8, name="picked_scales", align_bytes=ALIGN)
         nc.vector.tensor_copy(picked_scales[:], scale_table[:].indirect(offs_sb[:]))
-        for i in range(QUADRANT // BLOCK_ROWS):
+        for i in range(QUADRANT // SCALE_STEP):
             nc.sync.dma_start(
                 x_plane[i:P:QUADRANT, :].bitcast(I32),
-                picked_scales[BLOCK_ROWS * i : P : QUADRANT, :].bitcast(I32),
+                picked_scales[SCALE_STEP * i : P : QUADRANT, :].bitcast(I32),
             )
 
-        ssq_sb = {0: load_block(ssq_rows, 0, "ssq", 1)}
+        ssq_sb = {0: load_panel(ssq_rows, 0, "ssq"), 1: load_panel(ssq_rows, 1, "ssq")}
+        par_sb[2] = load_panel(par_rows, 2, "par")
+        ssq_sb[2] = load_panel(ssq_rows, 2, "ssq")
+        par_sb[0] = load_panel(par_rows, 0, "par")
+        ssq_sb[LAST] = load_panel(ssq_rows, LAST, "ssq")
+        par_sb[LAST] = load_panel(par_rows, LAST, "par")
 
-        w_bf = keep.tile([P, BLOCKS, P, PACK], BF16, name="w_bf", align_bytes=ALIGN)
-        w_from = w_raw[:].rearrange("p r (m t) -> p m t r", t=BLOCKS)
+        w_bf = keep.tile([P, PANELS, P, PACK], BF16, name="w_bf", align_bytes=ALIGN)
+        w_from = w_raw[:].rearrange("p r (m t) -> p m t r", t=PANELS)
         w_to = w_bf[:].rearrange("p t m r -> p m t r")
         nc.vector.tensor_copy(w_to[:, 0:VECTOR_COLS], w_from[:, 0:VECTOR_COLS])
         nc.scalar.copy(w_to[:, VECTOR_COLS:P], w_from[:, VECTOR_COLS:P])
         w_codes = keep.tile([P, N], U32, name="w_codes", align_bytes=ALIGN)
         w_plane = keep.tile([P, N], U8, name="w_plane", align_bytes=ALIGN)
-        for t in range(0, BLOCKS, 2):
+        for t in range(0, PANELS, 2):
             cols = slice(t * P, (t + 2) * P)
             nc.vector.quantize_mx(
                 out=w_codes[:, cols].bitcast(FP8X4),
@@ -96,26 +105,14 @@ def tile_picked_adagr8_none_p_kernel(tc, x_words, x_scales, w1, par, ssq, offs, 
             )
 
         x_codes = keep.tile([P, S], U32, name="x_codes", align_bytes=ALIGN)
-        for start in range(0, S, HALF):
-            nc.vector.tensor_copy(
-                x_codes[:, start : start + HALF],
-                word_table[:].bitcast(U32).indirect(offs_sb[:, start // GROUP : (start + HALF) // GROUP]),
-            )
-
-        ssq_sb[1] = load_block(ssq_rows, 1, "ssq", 2)
-        par_sb[2] = load_block(par_rows, 2, "par", 3)
-        ssq_sb[2] = load_block(ssq_rows, 2, "ssq", 4)
-        par_sb[0] = load_block(par_rows, 0, "par", 5)
-        ssq_sb[LAST] = load_block(ssq_rows, LAST, "ssq", 6)
-        par_sb[LAST] = load_block(par_rows, LAST, "par", 7)
+        for picked in HALVES:
+            nc.vector.tensor_copy(x_codes[:, picked], word_table[:].bitcast(U32).indirect(offsets(offs_sb, picked)))
 
         def product(t):
             cols = slice(t * P, (t + 1) * P)
-            width = HALF if t == 0 else S
             pieces = []
-            for start in range(0, S, width):
-                picked = slice(start, start + width)
-                bank = psum.tile([P, width], F32, name="y%d_%d" % (t, start))
+            for picked in HALVES if t == 0 else (WHOLE,):
+                bank = psum.tile([P, picked.stop - picked.start], F32, name="y%d_%d" % (t, picked.start))
                 nc.tensor.matmul_mx(
                     out=bank[:],
                     lhsT=w_codes[:, cols].bitcast(FP8X4),
@@ -128,19 +125,22 @@ def tile_picked_adagr8_none_p_kernel(tc, x_words, x_scales, w1, par, ssq, offs, 
                 pieces.append((picked, bank))
             return pieces
 
-        y = [product(t) for t in range(BLOCKS)]
+        y = [product(t) for t in range(PANELS)]
 
-        def work_tile(name, place):
-            return staged.tile([P, S], F32, name=name, align_bytes=ALIGN, offset=8 * SLOT + place * HALF * 4)
+        places = {"y_sq3": 0, "y_sq0": 1, "y_sb3": 2, "y_sb1": 4, "y_sq1": 5, "y_sb2": 6}
+        places.update({"y_sb0": 8, "total0": 10, "y_sq2": 10, "total1": 12, "total2": 14})
+
+        def placed(name):
+            return shared.tile([P, S], F32, name=name, align_bytes=ALIGN, offset=places[name] * HALF_TILE)
 
         def square(t):
-            y_sq = work_tile("y_sq%d" % t, (1, 5, 10, 0)[t])
+            y_sq = placed("y_sq%d" % t)
             for picked, bank in y[t]:
                 nc.scalar.activation(y_sq[:, picked], bank[:], ACT.Square)
             return y_sq
 
         def copy_out(t):
-            y_sb = work_tile("y_sb%d" % t, (8, 4, 6, 2)[t])
+            y_sb = placed("y_sb%d" % t)
             for picked, bank in y[t]:
                 if t == LAST:
                     nc.scalar.activation(y_sb[:, picked], bank[:], ACT.Copy, scale=-1.0)
@@ -154,16 +154,19 @@ def tile_picked_adagr8_none_p_kernel(tc, x_words, x_scales, w1, par, ssq, offs, 
             return old
 
         def inverse_root(t, y_sq):
-            total = work_tile("total%d" % t, (10, 16, 18)[t])
+            total = placed("total%d" % t)
             inv = keep.tile([P, S], F32, name="inv%d" % t)
             for picked, bank in y[t]:
-                offsets = ent_sb[:, picked.start // GROUP : picked.stop // GROUP]
-                nc.vector.tensor_tensor(total[:, picked], ssq_sb[t][:].indirect(offsets), y_sq[:, picked], ALU.add)
+                looked_up = ssq_sb[t][:].indirect(offsets(ent_sb, picked))
+                nc.vector.tensor_tensor(total[:, picked], looked_up, y_sq[:, picked], ALU.add)
                 nc.scalar.activation(inv[:, picked], total[:, picked], ACT.Abs_reciprocal_sqrt)
             return inv
 
-        def step_of(y_sb, inv):
-            step = keep.tile([P, S], F32, name="step")
+        def step_buffer(name):
+            return keep.tile([P, S], F32, name=name, tag="step")
+
+        def step_of(t, y_sb, inv):
+            step = step_buffer("step%d" % t)
             nc.gpsimd.tensor_tensor(step[:], y_sb[:], inv[:], ALU.mult)
             return step
 
@@ -173,20 +176,19 @@ def tile_picked_adagr8_none_p_kernel(tc, x_words, x_scales, w1, par, ssq, offs, 
 
         old_par = {1: fetch_par(1)}
         squares = [square(0), square(1)]
-        y_first = copy_out(0)
+        y_sb = {0: copy_out(0)}
         inverses = [inverse_root(0, squares[0])]
         squares.extend([square(2), square(LAST)])
         inverses.extend([inverse_root(1, squares[1]), inverse_root(2, squares[2])])
-        y_rest = {t: copy_out(t) for t in (LAST, 1, 2)}
-        for t in range(2, BLOCKS):
-            old_par[t] = fetch_par(t)
+        y_sb.update({t: copy_out(t) for t in (LAST, 1, 2)})
+        old_par.update({t: fetch_par(t) for t in (2, LAST)})
 
         new_first = keep.tile([P, S], F32, name="new0")
-        step_first = step_of(y_first, inverses[0])
+        step_first = step_of(0, y_sb[0], inverses[0])
         nc.vector.tensor_tensor(new_first[:], par_sb[0][:].indirect(ent_sb[:]), step_first[:], ALU.subtract)
         put_back(0, new_first)
         for t in range(1, LAST):
-            step = step_of(y_rest[t], inverses[t])
+            step = step_of(t, y_sb[t], inverses[t])
             new = keep.tile([P, S], F32, name="new%d" % t)
             nc.gpsimd.tensor_tensor(new[:], old_par[t][:], step[:], ALU.subtract)
             put_back(t, new)
@@ -199,10 +201,12 @@ def tile_picked_adagr8_none_p_kernel(tc, x_words, x_scales, w1, par, ssq, offs, 
         nc.scalar.activation(sums[:], log_root[:].indirect(ent_sb[:]), ACT.Exp, scale=-2.0)
         warm_again = keep.tile([P, 1], F32, name="warm_again")
         nc.scalar.activation(warm_again[:], sums[:, S - 1 : S], ACT.Abs_reciprocal_sqrt)
-        total = keep.tile([P, S], F32, name="total_last", tag="step")
-        nc.gpsimd.tensor_tensor(total[:], sums[:], squares[LAST][:], ALU.add)
-        inv = keep.tile([P, S], F32, name="inv_last")
-        nc.scalar.activation(inv[:], total[:], ACT.Abs_reciprocal_sqrt)
-        minus_step = step_of(y_rest[LAST], inv)
+        total_last = step_buffer("total_last")
+        nc.gpsimd.tensor_tensor(total_last[:], sums[:], squares[LAST][:], ALU.add)
+        inv_last = keep.tile([P, S], F32, name="inv_last")
+        minus_step = keep.tile([P, S], F32, name="minus_step")
+        for picked in HALVES:
+            nc.scalar.activation(inv_last[:, picked], total_last[:, picked], ACT.Abs_reciprocal_sqrt)
+            nc.gpsimd.tensor_tensor(minus_step[:, picked], y_sb[LAST][:, picked], inv_last[:, picked], ALU.mult)
         nc.vector.tensor_tensor(par_sb[LAST][:].indirect(ent_sb[:]), old_par[LAST][:], minus_step[:], ALU.add)
         nc.sync.dma_start(out_rows[LAST], par_sb[LAST][:])

@@ -199,8 +199,6 @@ def tile_picked_adagr8_none_p_kernel(tc, x_words, x_scales, w1, par, ssq, offs, 
         nc.scalar.activation(log_root[:], root[:], ACT.Ln)
         sums = keep.tile([P, S], F32, name="sums")
         nc.scalar.activation(sums[:], log_root[:].indirect(ent_sb[:]), ACT.Exp, scale=-2.0)
-        warm_again = keep.tile([P, 1], F32, name="warm_again")
-        nc.scalar.activation(warm_again[:], sums[:, S - 1 : S], ACT.Abs_reciprocal_sqrt)
         total_last = step_buffer("total_last")
         nc.gpsimd.tensor_tensor(total_last[:], sums[:], squares[LAST][:], ALU.add)
         inv_last = keep.tile([P, S], F32, name="inv_last")

@@ -25,7 +25,7 @@ LAST = PANELS - 1
 ALIGN = 64
 WHOLE = slice(0, S)
 HALVES = (slice(0, S // 2), slice(S // 2, S))
-VECTOR_COLS = 80
+VECTOR_COLS = 64
 TINY = 2.0**-126
 HALF_TILE = S * 4 // 2
 
@@ -70,9 +70,10 @@ def tile_picked_adagr8_none_p_kernel(tc, x_words, x_scales, w1, par, ssq, offs, 
         nc.scalar.activation(warm_out[:], warm_in[:], ACT.Abs_reciprocal_sqrt)
 
         nc.sync.dma_start(w_raw[:, PACK // 2 : PACK, :], w_rows[:, PACK // 2 : PACK, :])
-        nc.sync.dma_start(word_table[:], x_words[0].rearrange("p c r -> p (c r)").bitcast(I32))
         nc.sync.dma_start(ent_sb[:], ent)
-        par_sb = {1: load_panel(par_rows, 1, "par")}
+        nc.sync.dma_start(word_table[:], x_words[0].rearrange("p c r -> p (c r)").bitcast(I32))
+        par_sb = {1: keep.tile([P, U], F32, name="par1", align_bytes=ALIGN)}
+        nc.sync.dma_start(par_sb[1][:, 0 : U // 2], par_rows[1][:, 0 : U // 2])
 
         picked_scales = keep.tile([P, S], U8, name="picked_scales", align_bytes=ALIGN)
         nc.vector.tensor_copy(picked_scales[:], scale_table[:].indirect(offs_sb[:]))
@@ -82,6 +83,7 @@ def tile_picked_adagr8_none_p_kernel(tc, x_words, x_scales, w1, par, ssq, offs, 
                 picked_scales[SCALE_STEP * i : P : QUADRANT, :].bitcast(I32),
             )
 
+        nc.sync.dma_start(par_sb[1][:, U // 2 : U], par_rows[1][:, U // 2 : U])
         ssq_sb = {0: load_panel(ssq_rows, 0, "ssq"), 1: load_panel(ssq_rows, 1, "ssq")}
         par_sb[2] = load_panel(par_rows, 2, "par")
         ssq_sb[2] = load_panel(ssq_rows, 2, "ssq")

@@ -25,7 +25,7 @@ LAST = PANELS - 1
 ALIGN = 64
 WHOLE = slice(0, S)
 HALVES = (slice(0, S // 2), slice(S // 2, S))
-VECTOR_COLS = 64
+VECTOR_COLS = 72
 TINY = 2.0**-126
 HALF_TILE = S * 4 // 2
 

@@ -23,11 +23,11 @@ SCALE_STEP = 8
 PANELS = N // P
 LAST = PANELS - 1
 ALIGN = 64
+H = S // 2
 WHOLE = slice(0, S)
-HALVES = (slice(0, S // 2), slice(S // 2, S))
+HALVES = (slice(0, H), slice(H, S))
+PIECES = 2 * PANELS
 VECTOR_COLS = 72
-TINY = 2.0**-126
-HALF_TILE = S * 4 // 2
 
 
 def tile_picked_adagr8_none_p_kernel(tc, x_words, x_scales, w1, par, ssq, offs, ent, out):
@@ -48,14 +48,11 @@ def tile_picked_adagr8_none_p_kernel(tc, x_words, x_scales, w1, par, ssq, offs, 
         scale_table = keep.tile([P, T], U8, name="scale_table", align_bytes=ALIGN)
         word_table = keep.tile([P, T], I32, name="word_table", align_bytes=ALIGN)
         w_raw = keep.tile([P, PACK, N], F32, name="w_raw", align_bytes=ALIGN)
+        par_sb = [keep.tile([P, U], F32, name="par%d" % t, align_bytes=ALIGN) for t in range(PANELS)]
+        ssq_sb = [shared.tile([P, U], F32, name="ssq%d" % t, align_bytes=ALIGN, offset=t * U * 4) for t in range(PANELS)]
 
         def offsets(list_sb, picked):
             return list_sb[:, picked.start // GROUP : picked.stop // GROUP]
-
-        def load_panel(rows, t, name):
-            tile = keep.tile([P, U], F32, name="%s%d" % (name, t), align_bytes=ALIGN)
-            nc.sync.dma_start(tile[:], rows[t])
-            return tile
 
         nc.sync.dma_start(w_raw[:, 0 : PACK // 2, :], w_rows[:, 0 : PACK // 2, :])
         nc.sync.dma_start(offs_sb[:], offs)
@@ -72,8 +69,7 @@ def tile_picked_adagr8_none_p_kernel(tc, x_words, x_scales, w1, par, ssq, offs, 
         nc.sync.dma_start(w_raw[:, PACK // 2 : PACK, :], w_rows[:, PACK // 2 : PACK, :])
         nc.sync.dma_start(ent_sb[:], ent)
         nc.sync.dma_start(word_table[:], x_words[0].rearrange("p c r -> p (c r)").bitcast(I32))
-        par_sb = {1: keep.tile([P, U], F32, name="par1", align_bytes=ALIGN)}
-        nc.sync.dma_start(par_sb[1][:, 0 : U // 2], par_rows[1][:, 0 : U // 2])
+        nc.sync.dma_start(par_sb[0][:, 0 : U // 2], par_rows[0][:, 0 : U // 2])
 
         picked_scales = keep.tile([P, S], U8, name="picked_scales", align_bytes=ALIGN)
         nc.vector.tensor_copy(picked_scales[:], scale_table[:].indirect(offs_sb[:]))
@@ -83,13 +79,11 @@ def tile_picked_adagr8_none_p_kernel(tc, x_words, x_scales, w1, par, ssq, offs, 
                 picked_scales[SCALE_STEP * i : P : QUADRANT, :].bitcast(I32),
             )
 
-        nc.sync.dma_start(par_sb[1][:, U // 2 : U], par_rows[1][:, U // 2 : U])
-        ssq_sb = {0: load_panel(ssq_rows, 0, "ssq"), 1: load_panel(ssq_rows, 1, "ssq")}
-        par_sb[2] = load_panel(par_rows, 2, "par")
-        ssq_sb[2] = load_panel(ssq_rows, 2, "ssq")
-        par_sb[0] = load_panel(par_rows, 0, "par")
-        ssq_sb[LAST] = load_panel(ssq_rows, LAST, "ssq")
-        par_sb[LAST] = load_panel(par_rows, LAST, "par")
+        nc.sync.dma_start(par_sb[0][:, U // 2 : U], par_rows[0][:, U // 2 : U])
+        nc.sync.dma_start(ssq_sb[0][:], ssq_rows[0])
+        for t in range(1, PANELS):
+            nc.sync.dma_start(ssq_sb[t][:], ssq_rows[t])
+            nc.sync.dma_start(par_sb[t][:], par_rows[t])
 
         w_bf = keep.tile([P, PANELS, P, PACK], BF16, name="w_bf", align_bytes=ALIGN)
         w_from = w_raw[:].rearrange("p r (m t) -> p m t r", t=PANELS)
@@ -110,103 +104,122 @@ def tile_picked_adagr8_none_p_kernel(tc, x_words, x_scales, w1, par, ssq, offs, 
         for picked in HALVES:
             nc.vector.tensor_copy(x_codes[:, picked], word_table[:].bitcast(U32).indirect(offsets(offs_sb, picked)))
 
-        def product(t):
+        def multiply(t, picked):
             cols = slice(t * P, (t + 1) * P)
-            pieces = []
-            for picked in HALVES if t == 0 else (WHOLE,):
-                bank = psum.tile([P, picked.stop - picked.start], F32, name="y%d_%d" % (t, picked.start))
-                nc.tensor.matmul_mx(
-                    out=bank[:],
-                    lhsT=w_codes[:, cols].bitcast(FP8X4),
-                    lhsT_scale=w_plane[:, cols],
-                    rhs=x_codes[:, picked].bitcast(FP8X4),
-                    rhs_scale=x_plane[:, picked],
-                    start=True,
-                    stop=True,
-                )
-                pieces.append((picked, bank))
-            return pieces
+            bank = psum.tile([P, picked.stop - picked.start], F32, name="y%d_%d" % (t, picked.start))
+            nc.tensor.matmul_mx(
+                out=bank[:],
+                lhsT=w_codes[:, cols].bitcast(FP8X4),
+                lhsT_scale=w_plane[:, cols],
+                rhs=x_codes[:, picked].bitcast(FP8X4),
+                rhs_scale=x_plane[:, picked],
+                start=True,
+                stop=True,
+            )
+            return bank
 
-        y = [product(t) for t in range(PANELS)]
+        y = [multiply(t, picked)[:] for t in (0, 1) for picked in HALVES]
+        y_whole = {t: multiply(t, WHOLE) for t in (2, 3)}
+        y.extend(y_whole[t][:, picked] for t in (2, 3) for picked in HALVES)
 
-        places = {"y_sq3": 0, "y_sq0": 1, "y_sb3": 2, "y_sb1": 4, "y_sq1": 5, "y_sb2": 6}
-        places.update({"y_sb0": 8, "total0": 10, "y_sq2": 10, "total1": 12, "total2": 14})
+        def piece(name):
+            return keep.tile([P, H], F32, name=name)[:]
 
-        def placed(name):
-            return shared.tile([P, S], F32, name=name, align_bytes=ALIGN, offset=places[name] * HALF_TILE)
-
-        def square(t):
-            y_sq = placed("y_sq%d" % t)
-            for picked, bank in y[t]:
-                nc.scalar.activation(y_sq[:, picked], bank[:], ACT.Square)
-            return y_sq
-
-        def copy_out(t):
-            y_sb = placed("y_sb%d" % t)
-            for picked, bank in y[t]:
-                if t == LAST:
-                    nc.scalar.activation(y_sb[:, picked], bank[:], ACT.Copy, scale=-1.0)
-                else:
-                    nc.scalar.copy(y_sb[:, picked], bank[:])
-            return y_sb
-
-        def fetch_par(t):
-            old = keep.tile([P, S], F32, name="old%d" % t)
-            nc.vector.tensor_copy(old[:], par_sb[t][:].indirect(ent_sb[:]))
-            return old
-
-        def inverse_root(t, y_sq):
-            total = placed("total%d" % t)
-            inv = keep.tile([P, S], F32, name="inv%d" % t)
-            for picked, bank in y[t]:
-                looked_up = ssq_sb[t][:].indirect(offsets(ent_sb, picked))
-                nc.vector.tensor_tensor(total[:, picked], looked_up, y_sq[:, picked], ALU.add)
-                nc.scalar.activation(inv[:, picked], total[:, picked], ACT.Abs_reciprocal_sqrt)
-            return inv
-
-        def step_buffer(name):
-            return keep.tile([P, S], F32, name=name, tag="step")
-
-        def step_of(t, y_sb, inv):
-            step = step_buffer("step%d" % t)
-            nc.gpsimd.tensor_tensor(step[:], y_sb[:], inv[:], ALU.mult)
-            return step
-
-        def put_back(t, new):
-            nc.vector.tensor_copy(par_sb[t][:].indirect(ent_sb[:]), new[:])
-            nc.sync.dma_start(out_rows[t], par_sb[t][:])
-
-        old_par = {1: fetch_par(1)}
-        squares = [square(0), square(1)]
-        y_sb = {0: copy_out(0)}
-        inverses = [inverse_root(0, squares[0])]
-        squares.extend([square(2), square(LAST)])
-        inverses.extend([inverse_root(1, squares[1]), inverse_root(2, squares[2])])
-        y_sb.update({t: copy_out(t) for t in (LAST, 1, 2)})
-        old_par.update({t: fetch_par(t) for t in (2, LAST)})
-
-        new_first = keep.tile([P, S], F32, name="new0")
-        step_first = step_of(0, y_sb[0], inverses[0])
-        nc.vector.tensor_tensor(new_first[:], par_sb[0][:].indirect(ent_sb[:]), step_first[:], ALU.subtract)
-        put_back(0, new_first)
-        for t in range(1, LAST):
-            step = step_of(t, y_sb[t], inverses[t])
-            new = keep.tile([P, S], F32, name="new%d" % t)
-            nc.gpsimd.tensor_tensor(new[:], old_par[t][:], step[:], ALU.subtract)
-            put_back(t, new)
-
-        root = keep.tile([P, U], F32, name="root")
-        nc.scalar.activation(root[:], ssq_sb[LAST][:], ACT.Abs_reciprocal_sqrt, bias=TINY)
-        log_root = keep.tile([P, U], F32, name="log_root")
-        nc.scalar.activation(log_root[:], root[:], ACT.Ln)
-        sums = keep.tile([P, S], F32, name="sums")
-        nc.scalar.activation(sums[:], log_root[:].indirect(ent_sb[:]), ACT.Exp, scale=-2.0)
-        total_last = step_buffer("total_last")
-        nc.gpsimd.tensor_tensor(total_last[:], sums[:], squares[LAST][:], ALU.add)
-        inv_last = keep.tile([P, S], F32, name="inv_last")
+        work = keep.tile([P, (PIECES + 1) * S], F32, name="work")
+        middle = [work[:, k * S + H // 2 : k * S + H // 2 + H] for k in range(PIECES)]
+        left = [work[:, k * S : k * S + H] for k in range(PIECES)]
+        right = [work[:, k * S + H : (k + 1) * S] for k in range(PIECES)]
+        tail = {t: right[2 * t + 2] for t in range(1, LAST)}
+        tail[LAST] = None
+        sq_whole = {t: shared.tile([P, S], F32, name="y_sq%d" % t, align_bytes=ALIGN, offset=(t - 1) * U * 4) for t in (2, 3)}
+        y_sq = [piece("y_sq%d" % u) for u in range(4)]
+        y_last = shared.tile([P, S], F32, name="y_last", align_bytes=ALIGN, offset=LAST * U * 4)
         minus_step = keep.tile([P, S], F32, name="minus_step")
-        for picked in HALVES:
-            nc.scalar.activation(inv_last[:, picked], total_last[:, picked], ACT.Abs_reciprocal_sqrt)
-            nc.gpsimd.tensor_tensor(minus_step[:, picked], y_sb[LAST][:, picked], inv_last[:, picked], ALU.mult)
-        nc.vector.tensor_tensor(par_sb[LAST][:].indirect(ent_sb[:]), old_par[LAST][:], minus_step[:], ALU.add)
-        nc.sync.dma_start(out_rows[LAST], par_sb[LAST][:])
+        y_sq.extend(sq_whole[t][:, picked] for t in (2, 3) for picked in HALVES)
+        total = [middle[u] if u % 2 else piece("total0") if u == 0 else left[u] for u in range(PIECES)]
+        step = [piece("step%d" % u) for u in range(PIECES)]
+        old_first = keep.tile([P, S], F32, name="old_first")
+        old = [old_first[:, picked] for picked in HALVES]
+        sums = [None, None, piece("old2"), piece("sums3")]
+        late = {t: shared.tile([P, H], F32, name="late%d" % t, align_bytes=ALIGN, offset=(t + 1) * U * 4 + S * 4)[:] for t in (1, 2)}
+        late[LAST] = piece("old7")
+        for t in range(1, PANELS):
+            old.extend([sums[2 * t], late[t]])
+            sums.extend([y_sq[2 * t + 1], tail[t]])
+        new = [middle[u + 1] if u % 2 else piece("new%d" % u) for u in range(PIECES - 2)]
+        inv_last = keep.tile([P, S], F32, name="inv_last")
+        inv = [piece("inv%d" % u) for u in range(PIECES - 2)] + [inv_last[:, picked] for picked in HALVES]
+
+        def looked_up(table, u):
+            return table[u // 2][:].indirect(offsets(ent_sb, HALVES[u % 2]))
+
+        def square(u):
+            nc.scalar.activation(y_sq[u], y[u], ACT.Square)
+
+        def fetch_ssq(u):
+            nc.scalar.activation(sums[u], looked_up(ssq_sb, u), ACT.Copy)
+
+        def fetch_par(u):
+            nc.scalar.activation(old[u], looked_up(par_sb, u), ACT.Copy)
+
+        def add(u):
+            nc.gpsimd.tensor_tensor(total[u], sums[u], y_sq[u], ALU.add)
+
+        def root(u):
+            nc.scalar.activation(inv[u], total[u], ACT.Abs_reciprocal_sqrt)
+
+        def product(u):
+            nc.vector.tensor_tensor(step[u], y[u], inv[u], ALU.mult)
+
+        def subtract(u):
+            nc.gpsimd.tensor_tensor(new[u], old[u], step[u], ALU.subtract)
+
+        def put_back(u):
+            if u // 2 == LAST:
+                nc.vector.tensor_tensor(looked_up(par_sb, u), old[u], minus_step[:, HALVES[u % 2]], ALU.add)
+            else:
+                nc.vector.tensor_copy(looked_up(par_sb, u), new[u])
+            if u % 2:
+                nc.sync.dma_start(out_rows[u // 2], par_sb[u // 2][:])
+
+        nc.vector.tensor_copy(old_first[:], par_sb[0][:].indirect(ent_sb[:]))
+        for u in range(4):
+            square(u)
+        for u in range(3):
+            nc.vector.tensor_tensor(total[u], looked_up(ssq_sb, u), y_sq[u], ALU.add)
+        root(0)
+        root(1)
+        product(0)
+        product(1)
+        subtract(0)
+        put_back(0)
+        fetch_ssq(3)
+        for t in range(1, PANELS):
+            first, second = 2 * t, 2 * t + 1
+            if t > 1:
+                add(first)
+            root(first)
+            if t == 1:
+                nc.scalar.activation(sq_whole[2][:], y_whole[2][:], ACT.Square)
+            fetch_par(first)
+            add(second)
+            root(second)
+            if t < LAST:
+                fetch_ssq(first + 2)
+                fetch_ssq(second + 2)
+            fetch_par(second)
+            if t + 2 < PANELS:
+                nc.scalar.activation(sq_whole[t + 2][:], y_whole[t + 2][:], ACT.Square)
+            if t + 1 == LAST:
+                nc.scalar.activation(y_last[:], y_whole[LAST][:], ACT.Copy, scale=-1.0)
+            subtract(first - 1)
+            if t < LAST:
+                product(first)
+            put_back(first - 1)
+            if t < LAST:
+                subtract(first)
+                product(second)
+            else:
+                nc.gpsimd.tensor_tensor(minus_step[:], y_last[:], inv_last[:], ALU.mult)
+            put_back(first)
+        put_back(PIECES - 1)

@@ -146,6 +146,8 @@ def tile_picked_adagr8_none_p_kernel(tc, x_words, x_scales, w1, par, ssq, offs, 
         for t in range(1, PANELS):
             old.extend([sums[2 * t], late[t]])
             sums.extend([y_sq[2 * t + 1], tail[t]])
+        old_last = keep.tile([P, S], F32, name="old_last")
+        old[PIECES - 2 :] = [old_last[:, picked] for picked in HALVES]
         new = [middle[u + 1] if u % 2 else piece("new%d" % u) for u in range(PIECES - 2)]
         inv_last = keep.tile([P, S], F32, name="inv_last")
         inv = [piece("inv%d" % u) for u in range(PIECES - 2)] + [inv_last[:, picked] for picked in HALVES]
@@ -175,10 +177,7 @@ def tile_picked_adagr8_none_p_kernel(tc, x_words, x_scales, w1, par, ssq, offs, 
             nc.gpsimd.tensor_tensor(new[u], old[u], step[u], ALU.subtract)
 
         def put_back(u):
-            if u // 2 == LAST:
-                nc.vector.tensor_tensor(looked_up(par_sb, u), old[u], minus_step[:, HALVES[u % 2]], ALU.add)
-            else:
-                nc.vector.tensor_copy(looked_up(par_sb, u), new[u])
+            nc.vector.tensor_copy(looked_up(par_sb, u), new[u])
             if u % 2:
                 nc.sync.dma_start(out_rows[u // 2], par_sb[u // 2][:])
 
@@ -211,15 +210,17 @@ def tile_picked_adagr8_none_p_kernel(tc, x_words, x_scales, w1, par, ssq, offs, 
             if t + 2 < PANELS:
                 nc.scalar.activation(sq_whole[t + 2][:], y_whole[t + 2][:], ACT.Square)
             if t + 1 == LAST:
-                nc.scalar.activation(y_last[:], y_whole[LAST][:], ACT.Copy, scale=-1.0)
+                nc.scalar.activation(y_last[:, HALVES[1]], y[PIECES - 1], ACT.Copy, scale=-1.0)
             subtract(first - 1)
             if t < LAST:
                 product(first)
+            else:
+                nc.vector.scalar_tensor_tensor(minus_step[:, HALVES[0]], y[first], -1.0, inv[first], ALU.mult, ALU.mult)
             put_back(first - 1)
             if t < LAST:
                 subtract(first)
                 product(second)
-            else:
-                nc.gpsimd.tensor_tensor(minus_step[:], y_last[:], inv_last[:], ALU.mult)
-            put_back(first)
-        put_back(PIECES - 1)
+                put_back(first)
+        nc.gpsimd.tensor_tensor(minus_step[:, HALVES[1]], y_last[:, HALVES[1]], inv[PIECES - 1], ALU.mult)
+        nc.vector.tensor_tensor(par_sb[LAST][:].indirect(ent_sb[:]), old_last[:], minus_step[:], ALU.add)
+        nc.sync.dma_start(out_rows[LAST], par_sb[LAST][:])

@@ -28,6 +28,7 @@ WHOLE = slice(0, S)
 HALVES = (slice(0, H), slice(H, S))
 PIECES = 2 * PANELS
 VECTOR_COLS = 72
+LEAD = 224
 
 
 def tile_picked_adagr8_none_p_kernel(tc, x_words, x_scales, w1, par, ssq, offs, ent, out):
@@ -81,9 +82,12 @@ def tile_picked_adagr8_none_p_kernel(tc, x_words, x_scales, w1, par, ssq, offs, 
 
         nc.sync.dma_start(par_sb[0][:, U // 2 : U], par_rows[0][:, U // 2 : U])
         nc.sync.dma_start(ssq_sb[0][:], ssq_rows[0])
-        for t in range(1, PANELS):
+        for t in range(1, LAST):
             nc.sync.dma_start(ssq_sb[t][:], ssq_rows[t])
             nc.sync.dma_start(par_sb[t][:], par_rows[t])
+        nc.sync.dma_start(par_sb[LAST][:, 0 : U // 2], par_rows[LAST][:, 0 : U // 2])
+        nc.sync.dma_start(ssq_sb[LAST][:], ssq_rows[LAST])
+        nc.sync.dma_start(par_sb[LAST][:, U // 2 : U], par_rows[LAST][:, U // 2 : U])
 
         w_bf = keep.tile([P, PANELS, P, PACK], BF16, name="w_bf", align_bytes=ALIGN)
         w_from = w_raw[:].rearrange("p r (m t) -> p m t r", t=PANELS)
@@ -118,45 +122,54 @@ def tile_picked_adagr8_none_p_kernel(tc, x_words, x_scales, w1, par, ssq, offs, 
             )
             return bank
 
-        y = [multiply(t, picked)[:] for t in (0, 1) for picked in HALVES]
-        y_whole = {t: multiply(t, WHOLE) for t in (2, 3)}
-        y.extend(y_whole[t][:, picked] for t in (2, 3) for picked in HALVES)
+        y = [multiply(t, picked)[:] for t in range(LAST) for picked in HALVES]
+        y_whole = multiply(LAST, WHOLE)
+        y.extend(y_whole[:, picked] for picked in HALVES)
 
         def piece(name):
             return keep.tile([P, H], F32, name=name)[:]
 
-        work = keep.tile([P, (PIECES + 1) * S], F32, name="work")
-        middle = [work[:, k * S + H // 2 : k * S + H // 2 + H] for k in range(PIECES)]
-        left = [work[:, k * S : k * S + H] for k in range(PIECES)]
-        right = [work[:, k * S + H : (k + 1) * S] for k in range(PIECES)]
-        tail = {t: right[2 * t + 2] for t in range(1, LAST)}
-        tail[LAST] = None
-        sq_whole = {t: shared.tile([P, S], F32, name="y_sq%d" % t, align_bytes=ALIGN, offset=(t - 1) * U * 4) for t in (2, 3)}
-        y_sq = [piece("y_sq%d" % u) for u in range(4)]
-        y_last = shared.tile([P, S], F32, name="y_last", align_bytes=ALIGN, offset=LAST * U * 4)
-        minus_step = keep.tile([P, S], F32, name="minus_step")
-        y_sq.extend(sq_whole[t][:, picked] for t in (2, 3) for picked in HALVES)
-        total = [middle[u] if u % 2 else piece("total0") if u == 0 else left[u] for u in range(PIECES)]
-        step = [piece("step%d" % u) for u in range(PIECES)]
-        old_first = keep.tile([P, S], F32, name="old_first")
-        old = [old_first[:, picked] for picked in HALVES]
-        sums = [None, None, piece("old2"), piece("sums3")]
-        late = {t: shared.tile([P, H], F32, name="late%d" % t, align_bytes=ALIGN, offset=(t + 1) * U * 4 + S * 4)[:] for t in (1, 2)}
-        late[LAST] = piece("old7")
-        for t in range(1, PANELS):
-            old.extend([sums[2 * t], late[t]])
-            sums.extend([y_sq[2 * t + 1], tail[t]])
-        old_last = keep.tile([P, S], F32, name="old_last")
-        old[PIECES - 2 :] = [old_last[:, picked] for picked in HALVES]
-        new = [middle[u + 1] if u % 2 else piece("new%d" % u) for u in range(PIECES - 2)]
-        inv_last = keep.tile([P, S], F32, name="inv_last")
-        inv = [piece("inv%d" % u) for u in range(PIECES - 2)] + [inv_last[:, picked] for picked in HALVES]
+        def over_ssq(name, t, quarter):
+            return shared.tile([P, H], F32, name=name, align_bytes=ALIGN, offset=(t * U + quarter * H) * 4)[:]
+
+        def regions(name):
+            tile = keep.tile([P, S], F32, name=name)
+            return tile[:, 0:H], tile[:, H // 2 : H // 2 + H], tile[:, H:S]
+
+        def halves(name):
+            tile = keep.tile([P, S], F32, name=name)
+            return tile[:], [tile[:, picked] for picked in HALVES]
+
+        y_sq = {u: piece("y_sq%d" % u) for u in range(5)}
+        sums = {u: piece("sums%d" % u) for u in (3, 4, 6, 7)}
+        total = {u: piece("total%d" % u) for u in (0, 1, 3, 6, 7)}
+        inv = {u: piece("inv%d" % u) for u in (0, 1, 2, 4, 5, 6, 7)}
+        step = {u: piece("step%d" % u) for u in (2, 3)}
+        old = {u: piece("old%d" % u) for u in (2,)}
+        old_whole, step_whole = {}, {}
+        for t in (0, 2, LAST):
+            old_whole[t], (old[2 * t], old[2 * t + 1]) = halves("old_whole%d" % t)
+            step_whole[t], (step[2 * t], step[2 * t + 1]) = halves("step_whole%d" % t)
+        y_sq[5] = y_sq[0]
+        rest_tile = keep.tile([P, S], F32, name="rest_tile")
+        total[2], new_rest = rest_tile[:, 0:H], rest_tile[:, H // 2 : H // 2 + S - LEAD]
+        y_sq[6], inv[3], old[3] = over_ssq("y_sq6", 2, 0), over_ssq("inv3", 2, 1), over_ssq("old3", 2, 2)
+        y_sb = {5: over_ssq("y_sb5", 2, 3), 6: over_ssq("y_sb6", LAST, 0)}
+        new = {2: sums[4]}
+        total[5] = step[2]
+        total[4], new[3], sums[5] = regions("after_root4")
+        y_sq[7] = total[5]
+        y_sb[7] = total[6]
+        new_whole = keep.tile([P, S], F32, name="new_whole")
 
         def looked_up(table, u):
             return table[u // 2][:].indirect(offsets(ent_sb, HALVES[u % 2]))
 
         def square(u):
             nc.scalar.activation(y_sq[u], y[u], ACT.Square)
+
+        def copy_out(u):
+            nc.scalar.activation(y_sb[u], y[u], ACT.Copy, scale=-1.0 if u // 2 == LAST else 1.0)
 
         def fetch_ssq(u):
             nc.scalar.activation(sums[u], looked_up(ssq_sb, u), ACT.Copy)
@@ -171,56 +184,78 @@ def tile_picked_adagr8_none_p_kernel(tc, x_words, x_scales, w1, par, ssq, offs, 
             nc.scalar.activation(inv[u], total[u], ACT.Abs_reciprocal_sqrt)
 
         def product(u):
-            nc.vector.tensor_tensor(step[u], y[u], inv[u], ALU.mult)
+            if u in y_sb:
+                nc.gpsimd.tensor_tensor(step[u], y_sb[u], inv[u], ALU.mult)
+            else:
+                nc.vector.tensor_tensor(step[u], y[u], inv[u], ALU.mult)
 
         def subtract(u):
             nc.gpsimd.tensor_tensor(new[u], old[u], step[u], ALU.subtract)
 
-        def put_back(u):
-            nc.vector.tensor_copy(looked_up(par_sb, u), new[u])
-            if u % 2:
-                nc.sync.dma_start(out_rows[u // 2], par_sb[u // 2][:])
+        def put_back(t, picked, values):
+            nc.vector.tensor_copy(par_sb[t][:].indirect(offsets(ent_sb, picked)), values)
+            if picked.stop == S:
+                nc.sync.dma_start(out_rows[t], par_sb[t][:])
 
-        nc.vector.tensor_copy(old_first[:], par_sb[0][:].indirect(ent_sb[:]))
-        for u in range(4):
+        nc.vector.tensor_copy(old_whole[0], par_sb[0][:].indirect(ent_sb[:]))
+        for u in range(5):
             square(u)
         for u in range(3):
             nc.vector.tensor_tensor(total[u], looked_up(ssq_sb, u), y_sq[u], ALU.add)
-        root(0)
+        lead, rest = slice(0, LEAD), slice(LEAD, S)
+        for picked in (lead, slice(LEAD, H)):
+            nc.scalar.activation(inv[0][:, picked], total[0][:, picked], ACT.Abs_reciprocal_sqrt)
+        square(5)
         root(1)
-        product(0)
+        for picked in (lead, slice(LEAD, H)):
+            nc.vector.tensor_tensor(step[0][:, picked], y[0][:, picked], inv[0][:, picked], ALU.mult)
         product(1)
-        subtract(0)
-        put_back(0)
+        new_lead = keep.tile([P, LEAD], F32, name="new_lead")
+        nc.gpsimd.tensor_tensor(new_lead[:], old_whole[0][:, lead], step_whole[0][:, lead], ALU.subtract)
+        put_back(0, lead, new_lead[:])
+        root(2)
         fetch_ssq(3)
-        for t in range(1, PANELS):
-            first, second = 2 * t, 2 * t + 1
-            if t > 1:
-                add(first)
-            root(first)
-            if t == 1:
-                nc.scalar.activation(sq_whole[2][:], y_whole[2][:], ACT.Square)
-            fetch_par(first)
-            add(second)
-            root(second)
-            if t < LAST:
-                fetch_ssq(first + 2)
-                fetch_ssq(second + 2)
-            fetch_par(second)
-            if t + 2 < PANELS:
-                nc.scalar.activation(sq_whole[t + 2][:], y_whole[t + 2][:], ACT.Square)
-            if t + 1 == LAST:
-                nc.scalar.activation(y_last[:, HALVES[1]], y[PIECES - 1], ACT.Copy, scale=-1.0)
-            subtract(first - 1)
-            if t < LAST:
-                product(first)
-            else:
-                nc.vector.scalar_tensor_tensor(minus_step[:, HALVES[0]], y[first], -1.0, inv[first], ALU.mult, ALU.mult)
-            put_back(first - 1)
-            if t < LAST:
-                subtract(first)
-                product(second)
-                put_back(first)
-        nc.gpsimd.tensor_tensor(minus_step[:, HALVES[1]], y_last[:, HALVES[1]], inv[PIECES - 1], ALU.mult)
-        nc.vector.tensor_tensor(par_sb[LAST][:].indirect(ent_sb[:]), old_last[:], minus_step[:], ALU.add)
+        add(3)
+        nc.gpsimd.tensor_tensor(new_rest, old_whole[0][:, rest], step_whole[0][:, rest], ALU.subtract)
+        product(2)
+        put_back(0, rest, new_rest)
+
+        fetch_par(2)
+        fetch_ssq(4)
+        fetch_ssq(5)
+        square(6)
+        root(3)
+        fetch_par(3)
+        copy_out(5)
+        add(4)
+        root(4)
+        subtract(2)
+        product(3)
+        put_back(1, HALVES[0], new[2])
+        add(5)
+        fetch_par(4)
+        root(5)
+        fetch_par(5)
+        subtract(3)
+        product(4)
+        put_back(1, HALVES[1], new[3])
+
+        product(5)
+        nc.gpsimd.tensor_tensor(new_whole[:], old_whole[2], step_whole[2], ALU.subtract)
+        put_back(2, WHOLE, new_whole[:])
+
+        square(7)
+        fetch_ssq(6)
+        fetch_ssq(7)
+        copy_out(6)
+        fetch_par(6)
+        add(6)
+        root(6)
+        copy_out(7)
+        add(7)
+        root(7)
+        fetch_par(7)
+        product(6)
+        product(7)
+        nc.vector.tensor_tensor(par_sb[LAST][:].indirect(ent_sb[:]), old_whole[LAST], step_whole[LAST], ALU.add)
         nc.sync.dma_start(out_rows[LAST], par_sb[LAST][:])

@@ -207,11 +207,12 @@ def tile_picked_adagr8_none_p_kernel(tc, x_words, x_scales, w1, par, ssq, offs, 
             nc.scalar.activation(inv[0][:, picked], total[0][:, picked], ACT.Abs_reciprocal_sqrt)
         square(5)
         root(1)
-        for picked in (lead, slice(LEAD, H)):
-            nc.vector.tensor_tensor(step[0][:, picked], y[0][:, picked], inv[0][:, picked], ALU.mult)
-        product(1)
+        step_lead = total[3][:, lead]
+        nc.vector.tensor_tensor(step_lead, y[0][:, lead], inv[0][:, lead], ALU.mult)
+        nc.vector.tensor_tensor(step[0][:, LEAD:H], y[0][:, LEAD:H], inv[0][:, LEAD:H], ALU.mult)
         new_lead = keep.tile([P, LEAD], F32, name="new_lead")
-        nc.gpsimd.tensor_tensor(new_lead[:], old_whole[0][:, lead], step_whole[0][:, lead], ALU.subtract)
+        nc.vector.tensor_tensor(new_lead[:], old_whole[0][:, lead], step_lead, ALU.subtract)
+        product(1)
         put_back(0, lead, new_lead[:])
         root(2)
         fetch_ssq(3)

@@ -28,7 +28,7 @@ WHOLE = slice(0, S)
 HALVES = (slice(0, H), slice(H, S))
 PIECES = 2 * PANELS
 VECTOR_COLS = 72
-LEAD = 224
+CUT = 192
 
 
 def tile_picked_adagr8_none_p_kernel(tc, x_words, x_scales, w1, par, ssq, offs, ent, out):
@@ -122,9 +122,9 @@ def tile_picked_adagr8_none_p_kernel(tc, x_words, x_scales, w1, par, ssq, offs, 
             )
             return bank
 
-        y = [multiply(t, picked)[:] for t in range(LAST) for picked in HALVES]
+        y = {u: multiply(u // 2, HALVES[u % 2])[:] for u in (0, 2, 1, 3, 4, 5)}
         y_whole = multiply(LAST, WHOLE)
-        y.extend(y_whole[:, picked] for picked in HALVES)
+        y.update({2 * LAST + h: y_whole[:, picked] for h, picked in enumerate(HALVES)})
 
         def piece(name):
             return keep.tile([P, H], F32, name=name)[:]
@@ -132,16 +132,12 @@ def tile_picked_adagr8_none_p_kernel(tc, x_words, x_scales, w1, par, ssq, offs, 
         def over_ssq(name, t, quarter):
             return shared.tile([P, H], F32, name=name, align_bytes=ALIGN, offset=(t * U + quarter * H) * 4)[:]
 
-        def regions(name):
-            tile = keep.tile([P, S], F32, name=name)
-            return tile[:, 0:H], tile[:, H // 2 : H // 2 + H], tile[:, H:S]
-
         def halves(name):
             tile = keep.tile([P, S], F32, name=name)
             return tile[:], [tile[:, picked] for picked in HALVES]
 
         y_sq = {u: piece("y_sq%d" % u) for u in range(5)}
-        sums = {u: piece("sums%d" % u) for u in (3, 4, 6, 7)}
+        sums = {u: piece("sums%d" % u) for u in (3, 6, 7)}
         total = {u: piece("total%d" % u) for u in (0, 1, 3, 6, 7)}
         inv = {u: piece("inv%d" % u) for u in (0, 1, 2, 4, 5, 6, 7)}
         step = {u: piece("step%d" % u) for u in (2, 3)}
@@ -152,13 +148,17 @@ def tile_picked_adagr8_none_p_kernel(tc, x_words, x_scales, w1, par, ssq, offs, 
             step_whole[t], (step[2 * t], step[2 * t + 1]) = halves("step_whole%d" % t)
         y_sq[5] = y_sq[0]
         rest_tile = keep.tile([P, S], F32, name="rest_tile")
-        total[2], new_rest = rest_tile[:, 0:H], rest_tile[:, H // 2 : H // 2 + S - LEAD]
-        y_sq[6], inv[3], old[3] = over_ssq("y_sq6", 2, 0), over_ssq("inv3", 2, 1), over_ssq("old3", 2, 2)
+        total[2], new_rest = rest_tile[:, 0:H], rest_tile[:, H // 2 : H // 2 + H]
+        inv[3], old[3] = over_ssq("inv3", 2, 1), over_ssq("old3", 2, 2)
         y_sb = {5: over_ssq("y_sb5", 2, 3), 6: over_ssq("y_sb6", LAST, 0)}
-        new = {2: sums[4]}
-        total[5] = step[2]
-        total[4], new[3], sums[5] = regions("after_root4")
-        y_sq[7] = total[5]
+        second_new = keep.tile([P, S + H // 2], F32, name="second_new")
+        sums[4], sums[5] = second_new[:, 0:H], piece("sums5")
+        new = {0: piece("new0"), 1: new_rest, 2: sums[4], 3: second_new[:, H:S]}
+        step[0], step[1], total[3] = total[3], piece("step1"), total[3]
+        chain = keep.tile([P, S], F32, name="chain")
+        step[2] = total[5] = chain[:, 0:H]
+        y_sq[6], y_sq[7] = (chain[:, picked] for picked in HALVES)
+        total[4] = second_new[:, H + H // 2 : S + H // 2]
         y_sb[7] = total[6]
         new_whole = keep.tile([P, S], F32, name="new_whole")
 
@@ -198,33 +198,30 @@ def tile_picked_adagr8_none_p_kernel(tc, x_words, x_scales, w1, par, ssq, offs, 
                 nc.sync.dma_start(out_rows[t], par_sb[t][:])
 
         nc.vector.tensor_copy(old_whole[0], par_sb[0][:].indirect(ent_sb[:]))
-        for u in range(5):
+        for u in (0, 2, 1, 3, 4):
             square(u)
         for u in range(3):
             nc.vector.tensor_tensor(total[u], looked_up(ssq_sb, u), y_sq[u], ALU.add)
-        lead, rest = slice(0, LEAD), slice(LEAD, S)
-        for picked in (lead, slice(LEAD, H)):
+        quarters = (slice(0, H // 2), slice(H // 2, H))
+        for picked in quarters:
             nc.scalar.activation(inv[0][:, picked], total[0][:, picked], ACT.Abs_reciprocal_sqrt)
         square(5)
         root(1)
-        step_lead = total[3][:, lead]
-        nc.vector.tensor_tensor(step_lead, y[0][:, lead], inv[0][:, lead], ALU.mult)
-        nc.vector.tensor_tensor(step[0][:, LEAD:H], y[0][:, LEAD:H], inv[0][:, LEAD:H], ALU.mult)
-        new_lead = keep.tile([P, LEAD], F32, name="new_lead")
-        nc.vector.tensor_tensor(new_lead[:], old_whole[0][:, lead], step_lead, ALU.subtract)
+        for picked in quarters:
+            nc.vector.tensor_tensor(step[0][:, picked], y[0][:, picked], inv[0][:, picked], ALU.mult)
+        nc.vector.tensor_tensor(new[0], old[0], step[0], ALU.subtract)
         product(1)
-        put_back(0, lead, new_lead[:])
+        put_back(0, HALVES[0], new[0])
         root(2)
         fetch_ssq(3)
         add(3)
-        nc.gpsimd.tensor_tensor(new_rest, old_whole[0][:, rest], step_whole[0][:, rest], ALU.subtract)
+        subtract(1)
         product(2)
-        put_back(0, rest, new_rest)
+        put_back(0, HALVES[1], new[1])
 
         fetch_par(2)
         fetch_ssq(4)
         fetch_ssq(5)
-        square(6)
         root(3)
         fetch_par(3)
         copy_out(5)
@@ -232,20 +229,20 @@ def tile_picked_adagr8_none_p_kernel(tc, x_words, x_scales, w1, par, ssq, offs, 
         root(4)
         subtract(2)
         product(3)
-        put_back(1, HALVES[0], new[2])
+        put_back(1, slice(0, CUT), second_new[:, 0:CUT])
         add(5)
         fetch_par(4)
         root(5)
         fetch_par(5)
         subtract(3)
         product(4)
-        put_back(1, HALVES[1], new[3])
+        put_back(1, slice(CUT, S), second_new[:, CUT:S])
 
         product(5)
         nc.gpsimd.tensor_tensor(new_whole[:], old_whole[2], step_whole[2], ALU.subtract)
         put_back(2, WHOLE, new_whole[:])
 
-        square(7)
+        nc.scalar.activation(chain[:], y_whole[:], ACT.Square)
         fetch_ssq(6)
         fetch_ssq(7)
         copy_out(6)

@@ -224,9 +224,9 @@ def tile_picked_adagr8_none_p_kernel(tc, x_words, x_scales, w1, par, ssq, offs, 
         fetch_ssq(5)
         root(3)
         fetch_par(3)
-        copy_out(5)
         add(4)
         root(4)
+        copy_out(5)
         subtract(2)
         product(3)
         put_back(1, slice(0, CUT), second_new[:, 0:CUT])

@@ -20,13 +20,14 @@ PACK = 4
 GROUP = 16
 QUADRANT = 32
 SCALE_STEP = 8
+F32_BYTES = 4
 PANELS = N // P
 LAST = PANELS - 1
 ALIGN = 64
 H = S // 2
 WHOLE = slice(0, S)
 HALVES = (slice(0, H), slice(H, S))
-PIECES = 2 * PANELS
+QUARTERS = (slice(0, H // 2), slice(H // 2, H))
 VECTOR_COLS = 72
 CUT = 192
 
@@ -41,7 +42,7 @@ def tile_picked_adagr8_none_p_kernel(tc, x_words, x_scales, w1, par, ssq, offs, 
     with ExitStack() as ctx:
         lists = ctx.enter_context(tc.tile_pool(name="lists", bufs=1))
         keep = ctx.enter_context(tc.tile_pool(name="keep", bufs=1))
-        shared = ctx.enter_context(tc.tile_pool(name="shared", bufs=1))
+        placed = ctx.enter_context(tc.tile_pool(name="placed", bufs=1))
         psum = ctx.enter_context(tc.psum_pool(name="psum", bufs=1))
 
         offs_sb = lists.tile([P, S // GROUP], U16, name="offs_sb")
@@ -50,10 +51,17 @@ def tile_picked_adagr8_none_p_kernel(tc, x_words, x_scales, w1, par, ssq, offs, 
         word_table = keep.tile([P, T], I32, name="word_table", align_bytes=ALIGN)
         w_raw = keep.tile([P, PACK, N], F32, name="w_raw", align_bytes=ALIGN)
         par_sb = [keep.tile([P, U], F32, name="par%d" % t, align_bytes=ALIGN) for t in range(PANELS)]
-        ssq_sb = [shared.tile([P, U], F32, name="ssq%d" % t, align_bytes=ALIGN, offset=t * U * 4) for t in range(PANELS)]
+        ssq_sb = [
+            placed.tile([P, U], F32, name="ssq%d" % t, align_bytes=ALIGN, offset=t * U * F32_BYTES)
+            for t in range(PANELS)
+        ]
 
         def offsets(list_sb, picked):
             return list_sb[:, picked.start // GROUP : picked.stop // GROUP]
+
+        def load_par_half(t, half):
+            cols = slice(half * U // 2, (half + 1) * U // 2)
+            nc.sync.dma_start(par_sb[t][:, cols], par_rows[t][:, cols])
 
         nc.sync.dma_start(w_raw[:, 0 : PACK // 2, :], w_rows[:, 0 : PACK // 2, :])
         nc.sync.dma_start(offs_sb[:], offs)
@@ -70,7 +78,7 @@ def tile_picked_adagr8_none_p_kernel(tc, x_words, x_scales, w1, par, ssq, offs, 
         nc.sync.dma_start(w_raw[:, PACK // 2 : PACK, :], w_rows[:, PACK // 2 : PACK, :])
         nc.sync.dma_start(ent_sb[:], ent)
         nc.sync.dma_start(word_table[:], x_words[0].rearrange("p c r -> p (c r)").bitcast(I32))
-        nc.sync.dma_start(par_sb[0][:, 0 : U // 2], par_rows[0][:, 0 : U // 2])
+        load_par_half(0, 0)
 
         picked_scales = keep.tile([P, S], U8, name="picked_scales", align_bytes=ALIGN)
         nc.vector.tensor_copy(picked_scales[:], scale_table[:].indirect(offs_sb[:]))
@@ -80,14 +88,14 @@ def tile_picked_adagr8_none_p_kernel(tc, x_words, x_scales, w1, par, ssq, offs, 
                 picked_scales[SCALE_STEP * i : P : QUADRANT, :].bitcast(I32),
             )
 
-        nc.sync.dma_start(par_sb[0][:, U // 2 : U], par_rows[0][:, U // 2 : U])
+        load_par_half(0, 1)
         nc.sync.dma_start(ssq_sb[0][:], ssq_rows[0])
         for t in range(1, LAST):
             nc.sync.dma_start(ssq_sb[t][:], ssq_rows[t])
             nc.sync.dma_start(par_sb[t][:], par_rows[t])
-        nc.sync.dma_start(par_sb[LAST][:, 0 : U // 2], par_rows[LAST][:, 0 : U // 2])
+        load_par_half(LAST, 0)
         nc.sync.dma_start(ssq_sb[LAST][:], ssq_rows[LAST])
-        nc.sync.dma_start(par_sb[LAST][:, U // 2 : U], par_rows[LAST][:, U // 2 : U])
+        load_par_half(LAST, 1)
 
         w_bf = keep.tile([P, PANELS, P, PACK], BF16, name="w_bf", align_bytes=ALIGN)
         w_from = w_raw[:].rearrange("p r (m t) -> p m t r", t=PANELS)
@@ -120,47 +128,48 @@ def tile_picked_adagr8_none_p_kernel(tc, x_words, x_scales, w1, par, ssq, offs, 
                 start=True,
                 stop=True,
             )
-            return bank
+            return bank[:]
 
-        y = {u: multiply(u // 2, HALVES[u % 2])[:] for u in (0, 2, 1, 3, 4, 5)}
-        y_whole = multiply(LAST, WHOLE)
-        y.update({2 * LAST + h: y_whole[:, picked] for h, picked in enumerate(HALVES)})
+        y = {u: multiply(u // 2, HALVES[u % 2]) for u in (0, 2, 1, 3, 4, 5)}
+        y_last = multiply(LAST, WHOLE)
+        y[6], y[7] = (y_last[:, picked] for picked in HALVES)
 
-        def piece(name):
-            return keep.tile([P, H], F32, name=name)[:]
+        def buffer(name, columns=H):
+            return keep.tile([P, columns], F32, name=name)[:]
+
+        def buffers(name, pieces):
+            return {u: buffer("%s%d" % (name, u)) for u in pieces}
 
         def over_ssq(name, t, quarter):
-            return shared.tile([P, H], F32, name=name, align_bytes=ALIGN, offset=(t * U + quarter * H) * 4)[:]
+            return placed.tile([P, H], F32, name=name, align_bytes=ALIGN, offset=(t * U + quarter * H) * F32_BYTES)[:]
 
-        def halves(name):
-            tile = keep.tile([P, S], F32, name=name)
-            return tile[:], [tile[:, picked] for picked in HALVES]
+        y_sq = buffers("y_sq", range(5))
+        sums = buffers("sums", (3, 5, 6, 7))
+        total = buffers("total", (0, 1, 6, 7))
+        inv = buffers("inv", (0, 1, 2, 4, 5, 6, 7))
+        step = buffers("step", (0, 1, 3))
+        old = buffers("old", (2,))
+        new = buffers("new", (0,))
+        old_panel = {t: buffer("old_panel%d" % t, S) for t in (0, 2, LAST)}
+        step_panel = {t: buffer("step_panel%d" % t, S) for t in (2, LAST)}
+        for pieces, panels in ((old, old_panel), (step, step_panel)):
+            for t in panels:
+                pieces[2 * t], pieces[2 * t + 1] = (panels[t][:, picked] for picked in HALVES)
+        new_panel2 = buffer("new_panel2", S)
 
-        y_sq = {u: piece("y_sq%d" % u) for u in range(5)}
-        sums = {u: piece("sums%d" % u) for u in (3, 6, 7)}
-        total = {u: piece("total%d" % u) for u in (0, 1, 3, 6, 7)}
-        inv = {u: piece("inv%d" % u) for u in (0, 1, 2, 4, 5, 6, 7)}
-        step = {u: piece("step%d" % u) for u in (2, 3)}
-        old = {u: piece("old%d" % u) for u in (2,)}
-        old_whole, step_whole = {}, {}
-        for t in (0, 2, LAST):
-            old_whole[t], (old[2 * t], old[2 * t + 1]) = halves("old_whole%d" % t)
-            step_whole[t], (step[2 * t], step[2 * t + 1]) = halves("step_whole%d" % t)
         y_sq[5] = y_sq[0]
-        rest_tile = keep.tile([P, S], F32, name="rest_tile")
-        total[2], new_rest = rest_tile[:, 0:H], rest_tile[:, H // 2 : H // 2 + H]
+        total[3] = step[0]
+        after_root2 = buffer("after_root2", H + H // 2)
+        total[2], new[1] = after_root2[:, 0:H], after_root2[:, H // 2 :]
         inv[3], old[3] = over_ssq("inv3", 2, 1), over_ssq("old3", 2, 2)
         y_sb = {5: over_ssq("y_sb5", 2, 3), 6: over_ssq("y_sb6", LAST, 0)}
-        second_new = keep.tile([P, S + H // 2], F32, name="second_new")
-        sums[4], sums[5] = second_new[:, 0:H], piece("sums5")
-        new = {0: piece("new0"), 1: new_rest, 2: sums[4], 3: second_new[:, H:S]}
-        step[0], step[1], total[3] = total[3], piece("step1"), total[3]
-        chain = keep.tile([P, S], F32, name="chain")
-        step[2] = total[5] = chain[:, 0:H]
-        y_sq[6], y_sq[7] = (chain[:, picked] for picked in HALVES)
-        total[4] = second_new[:, H + H // 2 : S + H // 2]
+        new_panel1 = buffer("new_panel1", S + H // 2)
+        new[2], new[3] = (new_panel1[:, picked] for picked in HALVES)
+        sums[4], total[4] = new[2], new_panel1[:, H + H // 2 :]
+        y_sq_last = buffer("y_sq_last", S)
+        y_sq[6], y_sq[7] = (y_sq_last[:, picked] for picked in HALVES)
+        step[2] = total[5] = y_sq[6]
         y_sb[7] = total[6]
-        new_whole = keep.tile([P, S], F32, name="new_whole")
 
         def looked_up(table, u):
             return table[u // 2][:].indirect(offsets(ent_sb, HALVES[u % 2]))
@@ -180,14 +189,14 @@ def tile_picked_adagr8_none_p_kernel(tc, x_words, x_scales, w1, par, ssq, offs, 
         def add(u):
             nc.gpsimd.tensor_tensor(total[u], sums[u], y_sq[u], ALU.add)
 
-        def root(u):
-            nc.scalar.activation(inv[u], total[u], ACT.Abs_reciprocal_sqrt)
+        def root(u, part=HALVES[0]):
+            nc.scalar.activation(inv[u][:, part], total[u][:, part], ACT.Abs_reciprocal_sqrt)
 
-        def product(u):
+        def product(u, part=HALVES[0]):
             if u in y_sb:
                 nc.gpsimd.tensor_tensor(step[u], y_sb[u], inv[u], ALU.mult)
             else:
-                nc.vector.tensor_tensor(step[u], y[u], inv[u], ALU.mult)
+                nc.vector.tensor_tensor(step[u][:, part], y[u][:, part], inv[u][:, part], ALU.mult)
 
         def subtract(u):
             nc.gpsimd.tensor_tensor(new[u], old[u], step[u], ALU.subtract)
@@ -197,18 +206,17 @@ def tile_picked_adagr8_none_p_kernel(tc, x_words, x_scales, w1, par, ssq, offs, 
             if picked.stop == S:
                 nc.sync.dma_start(out_rows[t], par_sb[t][:])
 
-        nc.vector.tensor_copy(old_whole[0], par_sb[0][:].indirect(ent_sb[:]))
+        nc.vector.tensor_copy(old_panel[0], par_sb[0][:].indirect(ent_sb[:]))
         for u in (0, 2, 1, 3, 4):
             square(u)
         for u in range(3):
             nc.vector.tensor_tensor(total[u], looked_up(ssq_sb, u), y_sq[u], ALU.add)
-        quarters = (slice(0, H // 2), slice(H // 2, H))
-        for picked in quarters:
-            nc.scalar.activation(inv[0][:, picked], total[0][:, picked], ACT.Abs_reciprocal_sqrt)
+        for part in QUARTERS:
+            root(0, part)
         square(5)
         root(1)
-        for picked in quarters:
-            nc.vector.tensor_tensor(step[0][:, picked], y[0][:, picked], inv[0][:, picked], ALU.mult)
+        for part in QUARTERS:
+            product(0, part)
         nc.vector.tensor_tensor(new[0], old[0], step[0], ALU.subtract)
         product(1)
         put_back(0, HALVES[0], new[0])
@@ -229,20 +237,20 @@ def tile_picked_adagr8_none_p_kernel(tc, x_words, x_scales, w1, par, ssq, offs, 
         copy_out(5)
         subtract(2)
         product(3)
-        put_back(1, slice(0, CUT), second_new[:, 0:CUT])
+        put_back(1, slice(0, CUT), new_panel1[:, 0:CUT])
         add(5)
         fetch_par(4)
         root(5)
         fetch_par(5)
         subtract(3)
         product(4)
-        put_back(1, slice(CUT, S), second_new[:, CUT:S])
+        put_back(1, slice(CUT, S), new_panel1[:, CUT:S])
 
         product(5)
-        nc.gpsimd.tensor_tensor(new_whole[:], old_whole[2], step_whole[2], ALU.subtract)
-        put_back(2, WHOLE, new_whole[:])
+        nc.gpsimd.tensor_tensor(new_panel2, old_panel[2], step_panel[2], ALU.subtract)
+        put_back(2, WHOLE, new_panel2)
 
-        nc.scalar.activation(chain[:], y_whole[:], ACT.Square)
+        nc.scalar.activation(y_sq_last, y_last, ACT.Square)
         fetch_ssq(6)
         fetch_ssq(7)
         copy_out(6)
@@ -255,5 +263,5 @@ def tile_picked_adagr8_none_p_kernel(tc, x_words, x_scales, w1, par, ssq, offs, 
         fetch_par(7)
         product(6)
         product(7)
-        nc.vector.tensor_tensor(par_sb[LAST][:].indirect(ent_sb[:]), old_whole[LAST], step_whole[LAST], ALU.add)
+        nc.vector.tensor_tensor(par_sb[LAST][:].indirect(ent_sb[:]), old_panel[LAST], step_panel[LAST], ALU.add)
         nc.sync.dma_start(out_rows[LAST], par_sb[LAST][:])

@@ -59,10 +59,6 @@ def tile_picked_adagr8_none_p_kernel(tc, x_words, x_scales, w1, par, ssq, offs, 
         def offsets(list_sb, picked):
             return list_sb[:, picked.start // GROUP : picked.stop // GROUP]
 
-        def load_par_half(t, half):
-            cols = slice(half * U // 2, (half + 1) * U // 2)
-            nc.sync.dma_start(par_sb[t][:, cols], par_rows[t][:, cols])
-
         nc.sync.dma_start(w_raw[:, 0 : PACK // 2, :], w_rows[:, 0 : PACK // 2, :])
         nc.sync.dma_start(offs_sb[:], offs)
         nc.vector.memset(scale_table[:].bitcast(I32), 0)
@@ -78,7 +74,7 @@ def tile_picked_adagr8_none_p_kernel(tc, x_words, x_scales, w1, par, ssq, offs, 
         nc.sync.dma_start(w_raw[:, PACK // 2 : PACK, :], w_rows[:, PACK // 2 : PACK, :])
         nc.sync.dma_start(ent_sb[:], ent)
         nc.sync.dma_start(word_table[:], x_words[0].rearrange("p c r -> p (c r)").bitcast(I32))
-        load_par_half(0, 0)
+        nc.sync.dma_start(par_sb[0][:, 0 : U // 2], par_rows[0][:, 0 : U // 2])
 
         picked_scales = keep.tile([P, S], U8, name="picked_scales", align_bytes=ALIGN)
         nc.vector.tensor_copy(picked_scales[:], scale_table[:].indirect(offs_sb[:]))
@@ -88,14 +84,11 @@ def tile_picked_adagr8_none_p_kernel(tc, x_words, x_scales, w1, par, ssq, offs, 
                 picked_scales[SCALE_STEP * i : P : QUADRANT, :].bitcast(I32),
             )
 
-        load_par_half(0, 1)
+        nc.sync.dma_start(par_sb[0][:, U // 2 : U], par_rows[0][:, U // 2 : U])
         nc.sync.dma_start(ssq_sb[0][:], ssq_rows[0])
-        for t in range(1, LAST):
+        for t in range(1, PANELS):
             nc.sync.dma_start(ssq_sb[t][:], ssq_rows[t])
             nc.sync.dma_start(par_sb[t][:], par_rows[t])
-        load_par_half(LAST, 0)
-        nc.sync.dma_start(ssq_sb[LAST][:], ssq_rows[LAST])
-        load_par_half(LAST, 1)
 
         w_bf = keep.tile([P, PANELS, P, PACK], BF16, name="w_bf", align_bytes=ALIGN)
         w_from = w_raw[:].rearrange("p r (m t) -> p m t r", t=PANELS)

@@ -1,6 +1,7 @@
 from contextlib import ExitStack
 
 import concourse.mybir as mybir
+from concourse.masks import make_identity
 
 K, T, S, N, U = 512, 2048, 512, 512, 1024
 FLOPS = 2 * K * N * S
@@ -52,7 +53,7 @@ def tile_picked_adagr8_none_p_kernel(tc, x_words, x_scales, w1, par, ssq, offs, 
         w_raw = keep.tile([P, PACK, N], F32, name="w_raw", align_bytes=ALIGN)
         par_sb = [keep.tile([P, U], F32, name="par%d" % t, align_bytes=ALIGN) for t in range(PANELS)]
         ssq_sb = [
-            placed.tile([P, U], F32, name="ssq%d" % t, align_bytes=ALIGN, offset=t * U * F32_BYTES)
+            placed.tile([P, U], F32, name="ssq%d" % t, align_bytes=ALIGN, offset=(H + t * (U + H)) * F32_BYTES)
             for t in range(PANELS)
         ]
 
@@ -86,9 +87,15 @@ def tile_picked_adagr8_none_p_kernel(tc, x_words, x_scales, w1, par, ssq, offs, 
 
         nc.sync.dma_start(par_sb[0][:, U // 2 : U], par_rows[0][:, U // 2 : U])
         nc.sync.dma_start(ssq_sb[0][:], ssq_rows[0])
-        for t in range(1, PANELS):
-            nc.sync.dma_start(ssq_sb[t][:], ssq_rows[t])
-            nc.sync.dma_start(par_sb[t][:], par_rows[t])
+        nc.sync.dma_start(ssq_sb[1][:], ssq_rows[1])
+        nc.sync.dma_start(par_sb[1][:, 0 : U // 2], par_rows[1][:, 0 : U // 2])
+        nc.sync.dma_start(ssq_sb[2][:], ssq_rows[2])
+        nc.sync.dma_start(par_sb[1][:, U // 2 : U], par_rows[1][:, U // 2 : U])
+        nc.sync.dma_start(par_sb[2][:, 0 : U // 2], par_rows[2][:, 0 : U // 2])
+        nc.sync.dma_start(par_sb[3][:, 0 : U // 2], par_rows[3][:, 0 : U // 2])
+        nc.sync.dma_start(ssq_sb[3][:], ssq_rows[3])
+        nc.sync.dma_start(par_sb[2][:, U // 2 : U], par_rows[2][:, U // 2 : U])
+        nc.sync.dma_start(par_sb[3][:, U // 2 : U], par_rows[3][:, U // 2 : U])
 
         w_bf = keep.tile([P, PANELS, P, PACK], BF16, name="w_bf", align_bytes=ALIGN)
         w_from = w_raw[:].rearrange("p r (m t) -> p m t r", t=PANELS)
@@ -127,134 +134,192 @@ def tile_picked_adagr8_none_p_kernel(tc, x_words, x_scales, w1, par, ssq, offs, 
         y_last = multiply(LAST, WHOLE)
         y[6], y[7] = (y_last[:, picked] for picked in HALVES)
 
+
+        ident = keep.tile([P, P], F32, name="ident")
+        make_identity(nc, ident[:])
+
         def buffer(name, columns=H):
             return keep.tile([P, columns], F32, name=name)[:]
-
-        def buffers(name, pieces):
-            return {u: buffer("%s%d" % (name, u)) for u in pieces}
 
         def over_ssq(name, t, quarter):
             return placed.tile([P, H], F32, name=name, align_bytes=ALIGN, offset=(t * U + quarter * H) * F32_BYTES)[:]
 
-        y_sq = buffers("y_sq", range(5))
-        sums = buffers("sums", (3, 5, 6, 7))
-        total = buffers("total", (0, 1, 6, 7))
-        inv = buffers("inv", (0, 1, 2, 4, 5, 6, 7))
-        step = buffers("step", (0, 1, 3))
-        old = buffers("old", (2,))
-        new = buffers("new", (0,))
-        old_panel = {t: buffer("old_panel%d" % t, S) for t in (0, 2, LAST)}
-        step_panel = {t: buffer("step_panel%d" % t, S) for t in (2, LAST)}
-        for pieces, panels in ((old, old_panel), (step, step_panel)):
-            for t in panels:
-                pieces[2 * t], pieces[2 * t + 1] = (panels[t][:, picked] for picked in HALVES)
-        new_panel2 = buffer("new_panel2", S)
+        y_sq, sums, total, inv, step, old, new, y_sb, turned = {}, {}, {}, {}, {}, {}, {}, {}, {}
+        NEG = (7,)
+        ARENA = (H + PANELS * (U + H)) * F32_BYTES
+        spots = {}
 
-        y_sq[5] = y_sq[0]
-        total[3] = step[0]
+        def slot(name, index):
+            spots[name] = ARENA + (3 * index + 1) * H * F32_BYTES
+            return placed.tile([P, H], F32, name=name, align_bytes=ALIGN, offset=spots[name])[:]
+
+        def beside(name, other, side):
+            return placed.tile([P, H], F32, name=name, align_bytes=ALIGN, offset=spots[other] + side * (H // 2) * F32_BYTES)[:]
+
+        def on_ssq(name, t, fifth):
+            return placed.tile([P, H], F32, name=name, align_bytes=ALIGN, offset=(H // 2 + t * (U + H) + fifth * H) * F32_BYTES)[:]
+
+        old_panel0 = buffer("old_panel0", S)
+        old[0], old[1] = old_panel0[:, HALVES[0]], old_panel0[:, HALVES[1]]
+        for u in range(3):
+            y_sq[u] = buffer("y_sq%d" % u)
+        y_sq[5], y_sb[3], y_sq[6] = y_sq[0], y_sq[1], y_sq[2]
         after_root2 = buffer("after_root2", H + H // 2)
         total[2], new[1] = after_root2[:, 0:H], after_root2[:, H // 2 :]
-        inv[3], old[3] = over_ssq("inv3", 2, 1), over_ssq("old3", 2, 2)
-        y_sb = {5: over_ssq("y_sb5", 2, 3), 6: over_ssq("y_sb6", LAST, 0)}
-        new_panel1 = buffer("new_panel1", S + H // 2)
-        new[2], new[3] = (new_panel1[:, picked] for picked in HALVES)
-        sums[4], total[4] = new[2], new_panel1[:, H + H // 2 :]
-        y_sq_last = buffer("y_sq_last", S)
-        y_sq[6], y_sq[7] = (y_sq_last[:, picked] for picked in HALVES)
-        step[2] = total[5] = y_sq[6]
-        y_sb[7] = total[6]
+        step[0] = buffer("step0")
+        total[3] = step[0]
+        after_root4 = buffer("after_root4", H + H // 2)
+        total[4], new[3] = after_root4[:, 0:H], after_root4[:, H // 2 :]
+        inv[3], y_sb[6] = on_ssq("inv3", 2, 0), on_ssq("y_sb6", 2, 1)
+        inv[5], y_sb[5], y_sb[7], y_sq[7] = (on_ssq(name, 3, i) for i, name in enumerate(("inv5", "y_sb5", "y_sb7", "y_sq7")))
+        step[5], total[7] = buffer("step5"), buffer("total7")
+        old[7], step[7] = total[7], step[5]
+        spare = psum.tile([P, H], F32, name="spare")[:]
+        for group, label in ((y_sq, "y_sq"), (sums, "sums"), (total, "total"), (inv, "inv"), (step, "step"), (old, "old"), (new, "new"), (y_sb, "y_sb")):
+            for u in range(8):
+                if u not in group:
+                    group[u] = buffer("%s%d" % (label, u))
 
         def looked_up(table, u):
             return table[u // 2][:].indirect(offsets(ent_sb, HALVES[u % 2]))
 
-        def square(u):
+        def Q(u):
             nc.scalar.activation(y_sq[u], y[u], ACT.Square)
 
-        def copy_out(u):
-            nc.scalar.activation(y_sb[u], y[u], ACT.Copy, scale=-1.0 if u // 2 == LAST else 1.0)
+        def C(u):
+            nc.scalar.activation(y_sb[u], y[u], ACT.Copy, scale=-1.0 if u in NEG else 1.0)
 
-        def fetch_ssq(u):
+        def F(u):
             nc.scalar.activation(sums[u], looked_up(ssq_sb, u), ACT.Copy)
 
-        def fetch_par(u):
+        def Pp(u):
             nc.scalar.activation(old[u], looked_up(par_sb, u), ACT.Copy)
 
-        def add(u):
+        def vF(u):
+            nc.vector.tensor_copy(sums[u], looked_up(ssq_sb, u))
+
+        def vP(u):
+            nc.vector.tensor_copy(old[u], looked_up(par_sb, u))
+
+        def FA(u):
+            nc.vector.tensor_tensor(total[u], looked_up(ssq_sb, u), y_sq[u], ALU.add)
+
+        def A(u):
             nc.gpsimd.tensor_tensor(total[u], sums[u], y_sq[u], ALU.add)
 
-        def root(u, part=HALVES[0]):
+        def vA(u, part=HALVES[0]):
+            nc.vector.tensor_tensor(total[u][:, part], sums[u][:, part], y_sq[u][:, part], ALU.add)
+
+        def R(u, part=HALVES[0]):
             nc.scalar.activation(inv[u][:, part], total[u][:, part], ACT.Abs_reciprocal_sqrt)
 
-        def product(u, part=HALVES[0]):
-            if u in y_sb:
-                nc.gpsimd.tensor_tensor(step[u], y_sb[u], inv[u], ALU.mult)
-            else:
-                nc.vector.tensor_tensor(step[u][:, part], y[u][:, part], inv[u][:, part], ALU.mult)
+        def vM(u, part=HALVES[0]):
+            nc.vector.tensor_tensor(step[u][:, part], y[u][:, part], inv[u][:, part], ALU.mult)
 
-        def subtract(u):
+        def M(u):
+            nc.gpsimd.tensor_tensor(step[u], y_sb[u], inv[u], ALU.mult)
+
+        def D(u):
             nc.gpsimd.tensor_tensor(new[u], old[u], step[u], ALU.subtract)
 
-        def put_back(t, picked, values):
-            nc.vector.tensor_copy(par_sb[t][:].indirect(offsets(ent_sb, picked)), values)
-            if picked.stop == S:
-                nc.sync.dma_start(out_rows[t], par_sb[t][:])
+        def vD(u, part=HALVES[0]):
+            nc.vector.tensor_tensor(new[u][:, part], old[u][:, part], step[u][:, part], ALU.subtract)
 
-        nc.vector.tensor_copy(old_panel[0], par_sb[0][:].indirect(ent_sb[:]))
+        def store(t):
+            nc.sync.dma_start(out_rows[t], par_sb[t][:])
+
+        def X(u):
+            nc.vector.tensor_copy(looked_up(par_sb, u), new[u])
+
+        def Xf(u):
+            nc.vector.tensor_tensor(looked_up(par_sb, u), old[u], step[u], ALU.add)
+
+        def T1(u, bank):
+            passes = [(term, part) for term in (sums[u], y_sq[u]) for part in QUARTERS]
+            for i, (term, part) in enumerate(passes):
+                nc.tensor.matmul(bank[:, part], term[:, part], ident[:], start=i == 0, stop=i == len(passes) - 1, is_transpose=True)
+
+        def RT(u, bank):
+            nc.scalar.activation(total[u], bank, ACT.Abs_reciprocal_sqrt)
+
+        def T2(u, bank):
+            for part in QUARTERS:
+                nc.tensor.transpose(bank[:, part], total[u][:, part], ident[:])
+
+        def CI(u, bank):
+            nc.scalar.copy(inv[u], bank)
+
+        def clock(ap, name):
+            nc.tensor.transpose(spare[:, 0:P], ap[:, 0:P], ident[:])
+
+        nc.vector.tensor_copy(old_panel0, par_sb[0][:].indirect(ent_sb[:]))
         for u in (0, 2, 1, 3, 4):
-            square(u)
+            Q(u)
         for u in range(3):
-            nc.vector.tensor_tensor(total[u], looked_up(ssq_sb, u), y_sq[u], ALU.add)
+            FA(u)
         for part in QUARTERS:
-            root(0, part)
-        square(5)
-        root(1)
+            R(0, part)
+        Q(5)
+        R(1)
+        C(3)
         for part in QUARTERS:
-            product(0, part)
-        nc.vector.tensor_tensor(new[0], old[0], step[0], ALU.subtract)
-        product(1)
-        put_back(0, HALVES[0], new[0])
-        root(2)
-        fetch_ssq(3)
-        add(3)
-        subtract(1)
-        product(2)
-        put_back(0, HALVES[1], new[1])
-
-        fetch_par(2)
-        fetch_ssq(4)
-        fetch_ssq(5)
-        root(3)
-        fetch_par(3)
-        add(4)
-        root(4)
-        copy_out(5)
-        subtract(2)
-        product(3)
-        put_back(1, slice(0, CUT), new_panel1[:, 0:CUT])
-        add(5)
-        fetch_par(4)
-        root(5)
-        fetch_par(5)
-        subtract(3)
-        product(4)
-        put_back(1, slice(CUT, S), new_panel1[:, CUT:S])
-
-        product(5)
-        nc.gpsimd.tensor_tensor(new_panel2, old_panel[2], step_panel[2], ALU.subtract)
-        put_back(2, WHOLE, new_panel2)
-
-        nc.scalar.activation(y_sq_last, y_last, ACT.Square)
-        fetch_ssq(6)
-        fetch_ssq(7)
-        copy_out(6)
-        fetch_par(6)
-        add(6)
-        root(6)
-        copy_out(7)
-        add(7)
-        root(7)
-        fetch_par(7)
-        product(6)
-        product(7)
-        nc.vector.tensor_tensor(par_sb[LAST][:].indirect(ent_sb[:]), old_panel[LAST], step_panel[LAST], ALU.add)
-        nc.sync.dma_start(out_rows[LAST], par_sb[LAST][:])
+            vM(0, part)
+        vD(0)
+        vM(1)
+        X(0)
+        F(3)
+        R(2)
+        Q(6)
+        A(3)
+        D(1)
+        vM(2)
+        X(1)
+        for c in range(0, U, U // 4):
+            nc.sync.dma_start(out_rows[0][:, c : c + U // 4], par_sb[0][:, c : c + U // 4])
+        F(4)
+        F(5)
+        T1(5, spare)
+        A(4)
+        Pp(2)
+        D(2)
+        R(3)
+        Pp(3)
+        X(2)
+        R(4)
+        RT(5, spare)
+        T2(5, y[0])
+        C(6)
+        M(3)
+        D(3)
+        vM(4)
+        X(3)
+        for c in range(0, U, U // 4):
+            nc.sync.dma_start(out_rows[1][:, c : c + U // 4], par_sb[1][:, c : c + U // 4])
+        F(6)
+        F(7)
+        A(6)
+        Pp(4)
+        D(4)
+        Pp(5)
+        R(6)
+        X(4)
+        M(6)
+        Pp(6)
+        D(6)
+        X(6)
+        C(5)
+        CI(5, y[0])
+        Q(7)
+        T1(7, y[1])
+        M(5)
+        D(5)
+        X(5)
+        store(2)
+        C(7)
+        RT(7, y[1])
+        T2(7, y[2])
+        CI(7, y[2])
+        M(7)
+        Pp(7)
+        Xf(7)
+        store(3)

@@ -29,8 +29,10 @@ H = S // 2
 WHOLE = slice(0, S)
 HALVES = (slice(0, H), slice(H, S))
 QUARTERS = (slice(0, H // 2), slice(H // 2, H))
+COLUMN_HALVES = (slice(0, U // 2), slice(U // 2, U))
+SSQ_STEP = U + H
 VECTOR_COLS = 72
-CUT = 192
+STORE_PARTS = 4
 
 
 def tile_picked_adagr8_none_p_kernel(tc, x_words, x_scales, w1, par, ssq, offs, ent, out):
@@ -53,12 +55,18 @@ def tile_picked_adagr8_none_p_kernel(tc, x_words, x_scales, w1, par, ssq, offs, 
         w_raw = keep.tile([P, PACK, N], F32, name="w_raw", align_bytes=ALIGN)
         par_sb = [keep.tile([P, U], F32, name="par%d" % t, align_bytes=ALIGN) for t in range(PANELS)]
         ssq_sb = [
-            placed.tile([P, U], F32, name="ssq%d" % t, align_bytes=ALIGN, offset=(H + t * (U + H)) * F32_BYTES)
+            placed.tile([P, U], F32, name="ssq%d" % t, align_bytes=ALIGN, offset=(H + t * SSQ_STEP) * F32_BYTES)
             for t in range(PANELS)
         ]
 
         def offsets(list_sb, picked):
             return list_sb[:, picked.start // GROUP : picked.stop // GROUP]
+
+        def load_ssq(t):
+            nc.sync.dma_start(ssq_sb[t][:], ssq_rows[t])
+
+        def load_par(t, half):
+            nc.sync.dma_start(par_sb[t][:, COLUMN_HALVES[half]], par_rows[t][:, COLUMN_HALVES[half]])
 
         nc.sync.dma_start(w_raw[:, 0 : PACK // 2, :], w_rows[:, 0 : PACK // 2, :])
         nc.sync.dma_start(offs_sb[:], offs)
@@ -75,7 +83,7 @@ def tile_picked_adagr8_none_p_kernel(tc, x_words, x_scales, w1, par, ssq, offs, 
         nc.sync.dma_start(w_raw[:, PACK // 2 : PACK, :], w_rows[:, PACK // 2 : PACK, :])
         nc.sync.dma_start(ent_sb[:], ent)
         nc.sync.dma_start(word_table[:], x_words[0].rearrange("p c r -> p (c r)").bitcast(I32))
-        nc.sync.dma_start(par_sb[0][:, 0 : U // 2], par_rows[0][:, 0 : U // 2])
+        load_par(0, 0)
 
         picked_scales = keep.tile([P, S], U8, name="picked_scales", align_bytes=ALIGN)
         nc.vector.tensor_copy(picked_scales[:], scale_table[:].indirect(offs_sb[:]))
@@ -85,17 +93,17 @@ def tile_picked_adagr8_none_p_kernel(tc, x_words, x_scales, w1, par, ssq, offs, 
                 picked_scales[SCALE_STEP * i : P : QUADRANT, :].bitcast(I32),
             )
 
-        nc.sync.dma_start(par_sb[0][:, U // 2 : U], par_rows[0][:, U // 2 : U])
-        nc.sync.dma_start(ssq_sb[0][:], ssq_rows[0])
-        nc.sync.dma_start(ssq_sb[1][:], ssq_rows[1])
-        nc.sync.dma_start(par_sb[1][:, 0 : U // 2], par_rows[1][:, 0 : U // 2])
-        nc.sync.dma_start(ssq_sb[2][:], ssq_rows[2])
-        nc.sync.dma_start(par_sb[1][:, U // 2 : U], par_rows[1][:, U // 2 : U])
-        nc.sync.dma_start(par_sb[2][:, 0 : U // 2], par_rows[2][:, 0 : U // 2])
-        nc.sync.dma_start(par_sb[3][:, 0 : U // 2], par_rows[3][:, 0 : U // 2])
-        nc.sync.dma_start(ssq_sb[3][:], ssq_rows[3])
-        nc.sync.dma_start(par_sb[2][:, U // 2 : U], par_rows[2][:, U // 2 : U])
-        nc.sync.dma_start(par_sb[3][:, U // 2 : U], par_rows[3][:, U // 2 : U])
+        load_par(0, 1)
+        load_ssq(0)
+        load_ssq(1)
+        load_par(1, 0)
+        load_ssq(2)
+        load_par(1, 1)
+        load_par(2, 0)
+        load_par(LAST, 0)
+        load_ssq(LAST)
+        load_par(2, 1)
+        load_par(LAST, 1)
 
         w_bf = keep.tile([P, PANELS, P, PACK], BF16, name="w_bf", align_bytes=ALIGN)
         w_from = w_raw[:].rearrange("p r (m t) -> p m t r", t=PANELS)
@@ -134,192 +142,168 @@ def tile_picked_adagr8_none_p_kernel(tc, x_words, x_scales, w1, par, ssq, offs, 
         y_last = multiply(LAST, WHOLE)
         y[6], y[7] = (y_last[:, picked] for picked in HALVES)
 
-
-        ident = keep.tile([P, P], F32, name="ident")
-        make_identity(nc, ident[:])
+        identity = keep.tile([P, P], F32, name="identity")
+        make_identity(nc, identity[:])
 
         def buffer(name, columns=H):
             return keep.tile([P, columns], F32, name=name)[:]
 
-        def over_ssq(name, t, quarter):
-            return placed.tile([P, H], F32, name=name, align_bytes=ALIGN, offset=(t * U + quarter * H) * F32_BYTES)[:]
+        def buffers(name, pieces):
+            return {u: buffer("%s%d" % (name, u)) for u in pieces}
 
-        y_sq, sums, total, inv, step, old, new, y_sb, turned = {}, {}, {}, {}, {}, {}, {}, {}, {}
-        NEG = (7,)
-        ARENA = (H + PANELS * (U + H)) * F32_BYTES
-        spots = {}
-
-        def slot(name, index):
-            spots[name] = ARENA + (3 * index + 1) * H * F32_BYTES
-            return placed.tile([P, H], F32, name=name, align_bytes=ALIGN, offset=spots[name])[:]
-
-        def beside(name, other, side):
-            return placed.tile([P, H], F32, name=name, align_bytes=ALIGN, offset=spots[other] + side * (H // 2) * F32_BYTES)[:]
-
-        def on_ssq(name, t, fifth):
-            return placed.tile([P, H], F32, name=name, align_bytes=ALIGN, offset=(H // 2 + t * (U + H) + fifth * H) * F32_BYTES)[:]
+        def over_ssq(name, t, place):
+            column = H // 2 + t * SSQ_STEP + place * H
+            return placed.tile([P, H], F32, name=name, align_bytes=ALIGN, offset=column * F32_BYTES)[:]
 
         old_panel0 = buffer("old_panel0", S)
-        old[0], old[1] = old_panel0[:, HALVES[0]], old_panel0[:, HALVES[1]]
-        for u in range(3):
-            y_sq[u] = buffer("y_sq%d" % u)
-        y_sq[5], y_sb[3], y_sq[6] = y_sq[0], y_sq[1], y_sq[2]
-        after_root2 = buffer("after_root2", H + H // 2)
-        total[2], new[1] = after_root2[:, 0:H], after_root2[:, H // 2 :]
-        step[0] = buffer("step0")
+        y_sq = buffers("y_sq", range(5))
+        sums = buffers("sums", range(3, 8))
+        total = buffers("total", (0, 1, 6))
+        turned = buffers("turned", (5, 7))
+        inv = buffers("inv", (0, 1, 2, 4, 6, 7))
+        step = buffers("step", range(7))
+        old = buffers("old", range(2, 7))
+        old[0], old[1] = (old_panel0[:, picked] for picked in HALVES)
+        new = buffers("new", (0, 2, 4, 5, 6))
+
+        y_sb = {3: y_sq[1]}
+        y_sq[5], y_sq[6] = y_sq[0], y_sq[2]
         total[3] = step[0]
-        after_root4 = buffer("after_root4", H + H // 2)
-        total[4], new[3] = after_root4[:, 0:H], after_root4[:, H // 2 :]
-        inv[3], y_sb[6] = on_ssq("inv3", 2, 0), on_ssq("y_sb6", 2, 1)
-        inv[5], y_sb[5], y_sb[7], y_sq[7] = (on_ssq(name, 3, i) for i, name in enumerate(("inv5", "y_sb5", "y_sb7", "y_sq7")))
-        step[5], total[7] = buffer("step5"), buffer("total7")
-        old[7], step[7] = total[7], step[5]
-        spare = psum.tile([P, H], F32, name="spare")[:]
-        for group, label in ((y_sq, "y_sq"), (sums, "sums"), (total, "total"), (inv, "inv"), (step, "step"), (old, "old"), (new, "new"), (y_sb, "y_sb")):
-            for u in range(8):
-                if u not in group:
-                    group[u] = buffer("%s%d" % (label, u))
+        for u in (2, 4):
+            shared = buffer("after_root%d" % u, H + H // 2)
+            total[u], new[u - 1] = shared[:, 0:H], shared[:, H // 2 :]
+        inv[3], y_sb[6] = over_ssq("inv3", 2, 0), over_ssq("y_sb6", 2, 1)
+        inv[5], y_sb[5] = over_ssq("inv5", LAST, 0), over_ssq("y_sb5", LAST, 1)
+        y_sb[7], y_sq[7] = over_ssq("y_sb7", LAST, 2), over_ssq("y_sq7", LAST, 3)
+        old[7], step[7] = turned[7], step[5]
+
+        sum_bank = {5: psum.tile([P, H], F32, name="sum5")[:], 7: y[1]}
+        back_bank = {5: y[0], 7: y[2]}
 
         def looked_up(table, u):
             return table[u // 2][:].indirect(offsets(ent_sb, HALVES[u % 2]))
 
-        def Q(u):
+        def square(u):
             nc.scalar.activation(y_sq[u], y[u], ACT.Square)
 
-        def C(u):
-            nc.scalar.activation(y_sb[u], y[u], ACT.Copy, scale=-1.0 if u in NEG else 1.0)
+        def copy_out(u):
+            nc.scalar.activation(y_sb[u], y[u], ACT.Copy, scale=-1.0 if u == 7 else 1.0)
 
-        def F(u):
+        def fetch_ssq(u):
             nc.scalar.activation(sums[u], looked_up(ssq_sb, u), ACT.Copy)
 
-        def Pp(u):
+        def fetch_par(u):
             nc.scalar.activation(old[u], looked_up(par_sb, u), ACT.Copy)
 
-        def vF(u):
-            nc.vector.tensor_copy(sums[u], looked_up(ssq_sb, u))
-
-        def vP(u):
-            nc.vector.tensor_copy(old[u], looked_up(par_sb, u))
-
-        def FA(u):
-            nc.vector.tensor_tensor(total[u], looked_up(ssq_sb, u), y_sq[u], ALU.add)
-
-        def A(u):
+        def add(u):
             nc.gpsimd.tensor_tensor(total[u], sums[u], y_sq[u], ALU.add)
 
-        def vA(u, part=HALVES[0]):
-            nc.vector.tensor_tensor(total[u][:, part], sums[u][:, part], y_sq[u][:, part], ALU.add)
-
-        def R(u, part=HALVES[0]):
+        def root(u, part=HALVES[0]):
             nc.scalar.activation(inv[u][:, part], total[u][:, part], ACT.Abs_reciprocal_sqrt)
 
-        def vM(u, part=HALVES[0]):
-            nc.vector.tensor_tensor(step[u][:, part], y[u][:, part], inv[u][:, part], ALU.mult)
-
-        def M(u):
-            nc.gpsimd.tensor_tensor(step[u], y_sb[u], inv[u], ALU.mult)
-
-        def D(u):
-            nc.gpsimd.tensor_tensor(new[u], old[u], step[u], ALU.subtract)
-
-        def vD(u, part=HALVES[0]):
-            nc.vector.tensor_tensor(new[u][:, part], old[u][:, part], step[u][:, part], ALU.subtract)
-
-        def store(t):
-            nc.sync.dma_start(out_rows[t], par_sb[t][:])
-
-        def X(u):
-            nc.vector.tensor_copy(looked_up(par_sb, u), new[u])
-
-        def Xf(u):
-            nc.vector.tensor_tensor(looked_up(par_sb, u), old[u], step[u], ALU.add)
-
-        def T1(u, bank):
+        def add_turned(u):
             passes = [(term, part) for term in (sums[u], y_sq[u]) for part in QUARTERS]
             for i, (term, part) in enumerate(passes):
-                nc.tensor.matmul(bank[:, part], term[:, part], ident[:], start=i == 0, stop=i == len(passes) - 1, is_transpose=True)
+                nc.tensor.matmul(
+                    sum_bank[u][:, part],
+                    term[:, part],
+                    identity[:],
+                    start=i == 0,
+                    stop=i == len(passes) - 1,
+                    is_transpose=True,
+                )
 
-        def RT(u, bank):
-            nc.scalar.activation(total[u], bank, ACT.Abs_reciprocal_sqrt)
-
-        def T2(u, bank):
+        def root_turned(u):
+            nc.scalar.activation(turned[u], sum_bank[u], ACT.Abs_reciprocal_sqrt)
             for part in QUARTERS:
-                nc.tensor.transpose(bank[:, part], total[u][:, part], ident[:])
+                nc.tensor.transpose(back_bank[u][:, part], turned[u][:, part], identity[:])
 
-        def CI(u, bank):
-            nc.scalar.copy(inv[u], bank)
+        def copy_root(u):
+            nc.scalar.copy(inv[u], back_bank[u])
 
-        def clock(ap, name):
-            nc.tensor.transpose(spare[:, 0:P], ap[:, 0:P], ident[:])
+        def product(u, part=HALVES[0]):
+            if u in y_sb:
+                nc.gpsimd.tensor_tensor(step[u], y_sb[u], inv[u], ALU.mult)
+            else:
+                nc.vector.tensor_tensor(step[u][:, part], y[u][:, part], inv[u][:, part], ALU.mult)
+
+        def subtract(u):
+            nc.gpsimd.tensor_tensor(new[u], old[u], step[u], ALU.subtract)
+
+        def put_back(u):
+            nc.vector.tensor_copy(looked_up(par_sb, u), new[u])
+
+        def store(t, parts=1):
+            for c in range(0, U, U // parts):
+                nc.sync.dma_start(out_rows[t][:, c : c + U // parts], par_sb[t][:, c : c + U // parts])
 
         nc.vector.tensor_copy(old_panel0, par_sb[0][:].indirect(ent_sb[:]))
         for u in (0, 2, 1, 3, 4):
-            Q(u)
+            square(u)
         for u in range(3):
-            FA(u)
+            nc.vector.tensor_tensor(total[u], looked_up(ssq_sb, u), y_sq[u], ALU.add)
         for part in QUARTERS:
-            R(0, part)
-        Q(5)
-        R(1)
-        C(3)
+            root(0, part)
+        square(5)
+        root(1)
+        copy_out(3)
         for part in QUARTERS:
-            vM(0, part)
-        vD(0)
-        vM(1)
-        X(0)
-        F(3)
-        R(2)
-        Q(6)
-        A(3)
-        D(1)
-        vM(2)
-        X(1)
-        for c in range(0, U, U // 4):
-            nc.sync.dma_start(out_rows[0][:, c : c + U // 4], par_sb[0][:, c : c + U // 4])
-        F(4)
-        F(5)
-        T1(5, spare)
-        A(4)
-        Pp(2)
-        D(2)
-        R(3)
-        Pp(3)
-        X(2)
-        R(4)
-        RT(5, spare)
-        T2(5, y[0])
-        C(6)
-        M(3)
-        D(3)
-        vM(4)
-        X(3)
-        for c in range(0, U, U // 4):
-            nc.sync.dma_start(out_rows[1][:, c : c + U // 4], par_sb[1][:, c : c + U // 4])
-        F(6)
-        F(7)
-        A(6)
-        Pp(4)
-        D(4)
-        Pp(5)
-        R(6)
-        X(4)
-        M(6)
-        Pp(6)
-        D(6)
-        X(6)
-        C(5)
-        CI(5, y[0])
-        Q(7)
-        T1(7, y[1])
-        M(5)
-        D(5)
-        X(5)
+            product(0, part)
+        nc.vector.tensor_tensor(new[0], old[0], step[0], ALU.subtract)
+        product(1)
+        put_back(0)
+        fetch_ssq(3)
+        root(2)
+        square(6)
+        add(3)
+        subtract(1)
+        product(2)
+        put_back(1)
+        store(0, STORE_PARTS)
+
+        fetch_ssq(4)
+        fetch_ssq(5)
+        add_turned(5)
+        add(4)
+        fetch_par(2)
+        subtract(2)
+        root(3)
+        fetch_par(3)
+        put_back(2)
+        root(4)
+        root_turned(5)
+        copy_out(6)
+        product(3)
+        subtract(3)
+        product(4)
+        put_back(3)
+        store(1, STORE_PARTS)
+
+        fetch_ssq(6)
+        fetch_ssq(7)
+        add(6)
+        fetch_par(4)
+        subtract(4)
+        fetch_par(5)
+        root(6)
+        put_back(4)
+        product(6)
+        fetch_par(6)
+        subtract(6)
+        put_back(6)
+
+        copy_out(5)
+        copy_root(5)
+        square(7)
+        add_turned(7)
+        product(5)
+        subtract(5)
+        put_back(5)
         store(2)
-        C(7)
-        RT(7, y[1])
-        T2(7, y[2])
-        CI(7, y[2])
-        M(7)
-        Pp(7)
-        Xf(7)
-        store(3)
+        copy_out(7)
+        root_turned(7)
+        copy_root(7)
+        product(7)
+        fetch_par(7)
+        nc.vector.tensor_tensor(looked_up(par_sb, 7), old[7], step[7], ALU.add)
+        store(LAST)

@@ -1,7 +1,6 @@
 from contextlib import ExitStack
 
 import concourse.mybir as mybir
-from concourse.masks import make_identity
 
 K, T, S, N, U = 512, 2048, 512, 512, 1024
 FLOPS = 2 * K * N * S
@@ -21,18 +20,14 @@ PACK = 4
 GROUP = 16
 QUADRANT = 32
 SCALE_STEP = 8
-F32_BYTES = 4
 PANELS = N // P
 LAST = PANELS - 1
 ALIGN = 64
 H = S // 2
 WHOLE = slice(0, S)
 HALVES = (slice(0, H), slice(H, S))
-QUARTERS = (slice(0, H // 2), slice(H // 2, H))
 COLUMN_HALVES = (slice(0, U // 2), slice(U // 2, U))
-SSQ_STEP = U + H
 VECTOR_COLS = 72
-STORE_PARTS = 4
 
 
 def tile_picked_adagr8_none_p_kernel(tc, x_words, x_scales, w1, par, ssq, offs, ent, out):
@@ -45,7 +40,6 @@ def tile_picked_adagr8_none_p_kernel(tc, x_words, x_scales, w1, par, ssq, offs, 
     with ExitStack() as ctx:
         lists = ctx.enter_context(tc.tile_pool(name="lists", bufs=1))
         keep = ctx.enter_context(tc.tile_pool(name="keep", bufs=1))
-        placed = ctx.enter_context(tc.tile_pool(name="placed", bufs=1))
         psum = ctx.enter_context(tc.psum_pool(name="psum", bufs=1))
 
         offs_sb = lists.tile([P, S // GROUP], U16, name="offs_sb")
@@ -54,19 +48,16 @@ def tile_picked_adagr8_none_p_kernel(tc, x_words, x_scales, w1, par, ssq, offs, 
         word_table = keep.tile([P, T], I32, name="word_table", align_bytes=ALIGN)
         w_raw = keep.tile([P, PACK, N], F32, name="w_raw", align_bytes=ALIGN)
         par_sb = [keep.tile([P, U], F32, name="par%d" % t, align_bytes=ALIGN) for t in range(PANELS)]
-        ssq_sb = [
-            placed.tile([P, U], F32, name="ssq%d" % t, align_bytes=ALIGN, offset=(H + t * SSQ_STEP) * F32_BYTES)
-            for t in range(PANELS)
-        ]
+        ssq_sb = [keep.tile([P, U], F32, name="ssq%d" % t, align_bytes=ALIGN) for t in range(PANELS)]
 
         def offsets(list_sb, picked):
             return list_sb[:, picked.start // GROUP : picked.stop // GROUP]
 
-        def load_ssq(t):
-            nc.sync.dma_start(ssq_sb[t][:], ssq_rows[t])
+        def load_ssq(t, cols=slice(0, U)):
+            nc.sync.dma_start(ssq_sb[t][:, cols], ssq_rows[t][:, cols])
 
-        def load_par(t, half):
-            nc.sync.dma_start(par_sb[t][:, COLUMN_HALVES[half]], par_rows[t][:, COLUMN_HALVES[half]])
+        def load_par(t, cols=slice(0, U)):
+            nc.sync.dma_start(par_sb[t][:, cols], par_rows[t][:, cols])
 
         nc.sync.dma_start(w_raw[:, 0 : PACK // 2, :], w_rows[:, 0 : PACK // 2, :])
         nc.sync.dma_start(offs_sb[:], offs)
@@ -83,7 +74,7 @@ def tile_picked_adagr8_none_p_kernel(tc, x_words, x_scales, w1, par, ssq, offs, 
         nc.sync.dma_start(w_raw[:, PACK // 2 : PACK, :], w_rows[:, PACK // 2 : PACK, :])
         nc.sync.dma_start(ent_sb[:], ent)
         nc.sync.dma_start(word_table[:], x_words[0].rearrange("p c r -> p (c r)").bitcast(I32))
-        load_par(0, 0)
+        load_par(LAST, COLUMN_HALVES[0])
 
         picked_scales = keep.tile([P, S], U8, name="picked_scales", align_bytes=ALIGN)
         nc.vector.tensor_copy(picked_scales[:], scale_table[:].indirect(offs_sb[:]))
@@ -93,17 +84,14 @@ def tile_picked_adagr8_none_p_kernel(tc, x_words, x_scales, w1, par, ssq, offs, 
                 picked_scales[SCALE_STEP * i : P : QUADRANT, :].bitcast(I32),
             )
 
-        load_par(0, 1)
+        load_par(LAST, COLUMN_HALVES[1])
         load_ssq(0)
         load_ssq(1)
-        load_par(1, 0)
+        load_par(0)
         load_ssq(2)
-        load_par(1, 1)
-        load_par(2, 0)
-        load_par(LAST, 0)
+        load_par(1)
         load_ssq(LAST)
-        load_par(2, 1)
-        load_par(LAST, 1)
+        load_par(2)
 
         w_bf = keep.tile([P, PANELS, P, PACK], BF16, name="w_bf", align_bytes=ALIGN)
         w_from = w_raw[:].rearrange("p r (m t) -> p m t r", t=PANELS)
@@ -136,174 +124,114 @@ def tile_picked_adagr8_none_p_kernel(tc, x_words, x_scales, w1, par, ssq, offs, 
                 start=True,
                 stop=True,
             )
-            return bank[:]
+            return bank
 
-        y = {u: multiply(u // 2, HALVES[u % 2]) for u in (0, 2, 1, 3, 4, 5)}
-        y_last = multiply(LAST, WHOLE)
-        y[6], y[7] = (y_last[:, picked] for picked in HALVES)
+        A, B = HALVES
+        y = {t: [] for t in range(PANELS)}
+        for t, picked in ((0, A), (1, A), (0, B), (1, B), (2, WHOLE), (LAST, WHOLE)):
+            y[t].append((picked.start, multiply(t, picked)))
 
-        identity = keep.tile([P, P], F32, name="identity")
-        make_identity(nc, identity[:])
+        kinds = ("y_sq", "total", "inv", "step", "new")
+        shared = 3 * S
+        work = keep.tile([P, shared + len(kinds) * PANELS * S], F32, name="work")
+        place = {}
+        for i, kind in enumerate(kinds):
+            for t in range(PANELS):
+                start = shared + (i * PANELS + t) * S
+                place[kind, t] = [start, start + H]
+        place["new", LAST] = [0, H]
+        place["y_sq", 0] = [H + H // 2, 4 * H]
+        place["y_sq", 2] = [2 * H, 3 * H]
+        place["y_sq", LAST] = [4 * H, 5 * H]
+        place["step", 0][1] = 3 * H
+        place["step", 1] = [2 * H, 4 * H]
+        place["new", 0][1] = 5 * H
+        place["step", 2] = [3 * H, 4 * H]
+        place["step", LAST] = [2 * H, 3 * H]
 
-        def buffer(name, columns=H):
-            return keep.tile([P, columns], F32, name=name)[:]
+        def looked_up(table, t, part):
+            return table[t][:].indirect(offsets(ent_sb, part))
 
-        def buffers(name, pieces):
-            return {u: buffer("%s%d" % (name, u)) for u in pieces}
+        def at(kind, t, part):
+            start = place[kind, t][part.start // H] + part.start % H
+            return work[:, start : start + part.stop - part.start]
 
-        def over_ssq(name, t, place):
-            column = H // 2 + t * SSQ_STEP + place * H
-            return placed.tile([P, H], F32, name=name, align_bytes=ALIGN, offset=column * F32_BYTES)[:]
+        def y_at(t, part):
+            for first, bank in y[t]:
+                if first <= part.start and part.stop - first <= bank.shape[1]:
+                    return bank[:, part.start - first : part.stop - first]
 
-        old_panel0 = buffer("old_panel0", S)
-        y_sq = buffers("y_sq", range(5))
-        sums = buffers("sums", range(3, 8))
-        total = buffers("total", (0, 1, 6))
-        turned = buffers("turned", (5, 7))
-        inv = buffers("inv", (0, 1, 2, 4, 6, 7))
-        step = buffers("step", range(7))
-        old = buffers("old", range(2, 7))
-        old[0], old[1] = (old_panel0[:, picked] for picked in HALVES)
-        new = buffers("new", (0, 2, 4, 5, 6))
+        def square(t, part):
+            nc.scalar.activation(at("y_sq", t, part), y_at(t, part), ACT.Square)
 
-        y_sb = {3: y_sq[1]}
-        y_sq[5], y_sq[6] = y_sq[0], y_sq[2]
-        total[3] = step[0]
-        for u in (2, 4):
-            shared = buffer("after_root%d" % u, H + H // 2)
-            total[u], new[u - 1] = shared[:, 0:H], shared[:, H // 2 :]
-        inv[3], y_sb[6] = over_ssq("inv3", 2, 0), over_ssq("y_sb6", 2, 1)
-        inv[5], y_sb[5] = over_ssq("inv5", LAST, 0), over_ssq("y_sb5", LAST, 1)
-        y_sb[7], y_sq[7] = over_ssq("y_sb7", LAST, 2), over_ssq("y_sq7", LAST, 3)
-        old[7], step[7] = turned[7], step[5]
+        def add_ssq(t, part):
+            nc.vector.tensor_tensor(at("total", t, part), looked_up(ssq_sb, t, part), at("y_sq", t, part), ALU.add)
 
-        sum_bank = {5: psum.tile([P, H], F32, name="sum5")[:], 7: y[1]}
-        back_bank = {5: y[0], 7: y[2]}
+        def root(t, part):
+            nc.scalar.activation(at("inv", t, part), at("total", t, part), ACT.Abs_reciprocal_sqrt)
 
-        def looked_up(table, u):
-            return table[u // 2][:].indirect(offsets(ent_sb, HALVES[u % 2]))
-
-        def square(u):
-            nc.scalar.activation(y_sq[u], y[u], ACT.Square)
-
-        def copy_out(u):
-            nc.scalar.activation(y_sb[u], y[u], ACT.Copy, scale=-1.0 if u == 7 else 1.0)
-
-        def fetch_ssq(u):
-            nc.scalar.activation(sums[u], looked_up(ssq_sb, u), ACT.Copy)
-
-        def fetch_par(u):
-            nc.scalar.activation(old[u], looked_up(par_sb, u), ACT.Copy)
-
-        def add(u):
-            nc.gpsimd.tensor_tensor(total[u], sums[u], y_sq[u], ALU.add)
-
-        def root(u, part=HALVES[0]):
-            nc.scalar.activation(inv[u][:, part], total[u][:, part], ACT.Abs_reciprocal_sqrt)
-
-        def add_turned(u):
-            passes = [(term, part) for term in (sums[u], y_sq[u]) for part in QUARTERS]
-            for i, (term, part) in enumerate(passes):
-                nc.tensor.matmul(
-                    sum_bank[u][:, part],
-                    term[:, part],
-                    identity[:],
-                    start=i == 0,
-                    stop=i == len(passes) - 1,
-                    is_transpose=True,
+        def product(t, part):
+            if t == LAST:
+                nc.vector.scalar_tensor_tensor(
+                    at("step", t, part), y_at(t, part), -1.0, at("inv", t, part), ALU.mult, ALU.mult
                 )
-
-        def root_turned(u):
-            nc.scalar.activation(turned[u], sum_bank[u], ACT.Abs_reciprocal_sqrt)
-            for part in QUARTERS:
-                nc.tensor.transpose(back_bank[u][:, part], turned[u][:, part], identity[:])
-
-        def copy_root(u):
-            nc.scalar.copy(inv[u], back_bank[u])
-
-        def product(u, part=HALVES[0]):
-            if u in y_sb:
-                nc.gpsimd.tensor_tensor(step[u], y_sb[u], inv[u], ALU.mult)
             else:
-                nc.vector.tensor_tensor(step[u][:, part], y[u][:, part], inv[u][:, part], ALU.mult)
+                nc.vector.tensor_tensor(at("step", t, part), y_at(t, part), at("inv", t, part), ALU.mult)
 
-        def subtract(u):
-            nc.gpsimd.tensor_tensor(new[u], old[u], step[u], ALU.subtract)
+        def subtract_from_par(t, part):
+            nc.vector.tensor_tensor(at("new", t, part), looked_up(par_sb, t, part), at("step", t, part), ALU.subtract)
 
-        def put_back(u):
-            nc.vector.tensor_copy(looked_up(par_sb, u), new[u])
+        def put_back(t, part):
+            nc.scalar.activation(looked_up(par_sb, t, part), at("new", t, part), ACT.Copy)
 
         def store(t, parts=1):
             for c in range(0, U, U // parts):
                 nc.sync.dma_start(out_rows[t][:, c : c + U // parts], par_sb[t][:, c : c + U // parts])
 
-        nc.vector.tensor_copy(old_panel0, par_sb[0][:].indirect(ent_sb[:]))
-        for u in (0, 2, 1, 3, 4):
-            square(u)
-        for u in range(3):
-            nc.vector.tensor_tensor(total[u], looked_up(ssq_sb, u), y_sq[u], ALU.add)
-        for part in QUARTERS:
-            root(0, part)
-        square(5)
-        root(1)
-        copy_out(3)
-        for part in QUARTERS:
-            product(0, part)
-        nc.vector.tensor_tensor(new[0], old[0], step[0], ALU.subtract)
-        product(1)
-        put_back(0)
-        fetch_ssq(3)
-        root(2)
-        square(6)
-        add(3)
-        subtract(1)
-        product(2)
-        put_back(1)
-        store(0, STORE_PARTS)
-
-        fetch_ssq(4)
-        fetch_ssq(5)
-        add_turned(5)
-        add(4)
-        fetch_par(2)
-        subtract(2)
-        root(3)
-        fetch_par(3)
-        put_back(2)
-        root(4)
-        root_turned(5)
-        copy_out(6)
-        product(3)
-        subtract(3)
-        product(4)
-        put_back(3)
-        store(1, STORE_PARTS)
-
-        fetch_ssq(6)
-        fetch_ssq(7)
-        add(6)
-        fetch_par(4)
-        subtract(4)
-        fetch_par(5)
-        root(6)
-        put_back(4)
-        product(6)
-        fetch_par(6)
-        subtract(6)
-        put_back(6)
-
-        copy_out(5)
-        copy_root(5)
-        square(7)
-        add_turned(7)
-        product(5)
-        subtract(5)
-        put_back(5)
+        C, D = slice(H, H + H // 2), slice(H + H // 2, S)
+        nc.vector.tensor_copy(at("new", LAST, A), looked_up(par_sb, LAST, A))
+        square(0, A)
+        square(1, A)
+        square(0, B)
+        square(1, B)
+        add_ssq(0, A)
+        add_ssq(0, B)
+        root(0, A)
+        product(0, A)
+        square(2, WHOLE)
+        add_ssq(1, A)
+        add_ssq(1, B)
+        nc.scalar.activation(at("new", LAST, B), looked_up(par_sb, LAST, B), ACT.Copy)
+        root(0, B)
+        square(LAST, WHOLE)
+        root(1, A)
+        root(1, B)
+        subtract_from_par(0, A)
+        put_back(0, A)
+        add_ssq(2, A)
+        add_ssq(2, B)
+        root(2, WHOLE)
+        product(1, A)
+        product(0, B)
+        subtract_from_par(1, A)
+        put_back(1, A)
+        add_ssq(LAST, A)
+        add_ssq(LAST, B)
+        root(LAST, WHOLE)
+        product(1, B)
+        subtract_from_par(0, B)
+        put_back(0, B)
+        store(0, 2)
+        subtract_from_par(1, B)
+        put_back(1, C)
+        product(2, A)
+        product(2, B)
+        subtract_from_par(2, A)
+        subtract_from_par(2, B)
+        put_back(2, WHOLE)
+        product(LAST, WHOLE)
+        nc.vector.tensor_copy(looked_up(par_sb, 1, D), at("new", 1, D))
+        store(1)
         store(2)
-        copy_out(7)
-        root_turned(7)
-        copy_root(7)
-        product(7)
-        fetch_par(7)
-        nc.vector.tensor_tensor(looked_up(par_sb, 7), old[7], step[7], ALU.add)
+        nc.vector.tensor_tensor(looked_up(par_sb, LAST, WHOLE), at("new", LAST, WHOLE), at("step", LAST, WHOLE), ALU.add)
         store(LAST)

@@ -28,6 +28,7 @@ WHOLE = slice(0, S)
 HALVES = (slice(0, H), slice(H, S))
 COLUMN_HALVES = (slice(0, U // 2), slice(U // 2, U))
 VECTOR_COLS = 72
+SCALAR_SHARE = 352
 
 
 def tile_picked_adagr8_none_p_kernel(tc, x_words, x_scales, w1, par, ssq, offs, ent, out):
@@ -86,10 +87,11 @@ def tile_picked_adagr8_none_p_kernel(tc, x_words, x_scales, w1, par, ssq, offs, 
 
         load_par(LAST, COLUMN_HALVES[1])
         load_ssq(0)
+        load_par(0, slice(0, U // 4))
         load_ssq(1)
-        load_par(0)
-        load_ssq(2)
+        load_par(0, slice(U // 4, U))
         load_par(1)
+        load_ssq(2)
         load_ssq(LAST)
         load_par(2)
 
@@ -128,26 +130,27 @@ def tile_picked_adagr8_none_p_kernel(tc, x_words, x_scales, w1, par, ssq, offs, 
 
         A, B = HALVES
         y = {t: [] for t in range(PANELS)}
-        for t, picked in ((0, A), (1, A), (0, B), (1, B), (2, WHOLE), (LAST, WHOLE)):
+        for t, picked in ((0, A), (1, A), (0, B), (1, B), (2, A), (2, B), (LAST, WHOLE)):
             y[t].append((picked.start, multiply(t, picked)))
 
         kinds = ("y_sq", "total", "inv", "step", "new")
-        shared = 3 * S
+        shared = 8 * H
         work = keep.tile([P, shared + len(kinds) * PANELS * S], F32, name="work")
         place = {}
         for i, kind in enumerate(kinds):
             for t in range(PANELS):
                 start = shared + (i * PANELS + t) * S
                 place[kind, t] = [start, start + H]
-        place["new", LAST] = [0, H]
-        place["y_sq", 0] = [H + H // 2, 4 * H]
-        place["y_sq", 2] = [2 * H, 3 * H]
-        place["y_sq", LAST] = [4 * H, 5 * H]
-        place["step", 0][1] = 3 * H
-        place["step", 1] = [2 * H, 4 * H]
-        place["new", 0][1] = 5 * H
-        place["step", 2] = [3 * H, 4 * H]
+        place["y_sq", 0] = [H, 4 * H]
+        place["y_sq", 2] = [0, H]
+        place["new", 0][1] = 0
+        place["step", 1][1] = H
+        place["y_sq", LAST] = [3 * H, 4 * H]
+        place["step", 2] = [3 * H, H]
         place["step", LAST] = [2 * H, 3 * H]
+        place["step", 0][1] = 6 * H + H // 2
+        place["total", 1] = [7 * H, place["step", 0][0]]
+        old_0b = keep.tile([P, H], F32, name="old_0b")
 
         def looked_up(table, t, part):
             return table[t][:].indirect(offsets(ent_sb, part))
@@ -188,50 +191,50 @@ def tile_picked_adagr8_none_p_kernel(tc, x_words, x_scales, w1, par, ssq, offs, 
             for c in range(0, U, U // parts):
                 nc.sync.dma_start(out_rows[t][:, c : c + U // parts], par_sb[t][:, c : c + U // parts])
 
-        C, D = slice(H, H + H // 2), slice(H + H // 2, S)
-        nc.vector.tensor_copy(at("new", LAST, A), looked_up(par_sb, LAST, A))
+        C, D = slice(H, SCALAR_SHARE), slice(SCALAR_SHARE, S)
+        nc.vector.tensor_copy(at("new", LAST, WHOLE), looked_up(par_sb, LAST, WHOLE))
         square(0, A)
         square(1, A)
         square(0, B)
         square(1, B)
+        square(2, A)
         add_ssq(0, A)
         add_ssq(0, B)
         root(0, A)
         product(0, A)
-        square(2, WHOLE)
-        add_ssq(1, A)
-        add_ssq(1, B)
-        nc.scalar.activation(at("new", LAST, B), looked_up(par_sb, LAST, B), ACT.Copy)
+        square(2, B)
         root(0, B)
         square(LAST, WHOLE)
+        add_ssq(1, A)
         root(1, A)
-        root(1, B)
+        nc.scalar.activation(old_0b[:], looked_up(par_sb, 0, B), ACT.Copy)
         subtract_from_par(0, A)
         put_back(0, A)
+        product(1, A)
+        product(0, B)
+        add_ssq(1, B)
+        root(1, B)
+        subtract_from_par(1, A)
+        put_back(1, A)
         add_ssq(2, A)
         add_ssq(2, B)
         root(2, WHOLE)
-        product(1, A)
-        product(0, B)
-        subtract_from_par(1, A)
-        put_back(1, A)
-        add_ssq(LAST, A)
-        add_ssq(LAST, B)
-        root(LAST, WHOLE)
+        nc.vector.tensor_tensor(at("new", 0, B), old_0b[:], at("step", 0, B), ALU.subtract)
+        put_back(0, C)
         product(1, B)
-        subtract_from_par(0, B)
-        put_back(0, B)
-        store(0, 2)
+        add_ssq(LAST, WHOLE)
+        root(LAST, WHOLE)
         subtract_from_par(1, B)
-        put_back(1, C)
+        put_back(1, B)
+        store(1)
         product(2, A)
         product(2, B)
         subtract_from_par(2, A)
         subtract_from_par(2, B)
         put_back(2, WHOLE)
         product(LAST, WHOLE)
-        nc.vector.tensor_copy(looked_up(par_sb, 1, D), at("new", 1, D))
-        store(1)
+        nc.vector.tensor_copy(looked_up(par_sb, 0, D), at("new", 0, D))
+        store(0)
         store(2)
         nc.vector.tensor_tensor(looked_up(par_sb, LAST, WHOLE), at("new", LAST, WHOLE), at("step", LAST, WHOLE), ALU.add)
         store(LAST)

@@ -22,13 +22,16 @@ QUADRANT = 32
 SCALE_STEP = 8
 PANELS = N // P
 LAST = PANELS - 1
+APART = 64 * 1024
+PAR_PLACES = (0, APART, 2 * APART, 4 * U)
 ALIGN = 64
 H = S // 2
 WHOLE = slice(0, S)
 HALVES = (slice(0, H), slice(H, S))
 COLUMN_HALVES = (slice(0, U // 2), slice(U // 2, U))
 VECTOR_COLS = 72
-SCALAR_SHARE = 352
+SCALAR_SHARE = 320
+W_AHEAD = 576
 
 
 def tile_picked_adagr8_none_p_kernel(tc, x_words, x_scales, w1, par, ssq, offs, ent, out):
@@ -41,6 +44,7 @@ def tile_picked_adagr8_none_p_kernel(tc, x_words, x_scales, w1, par, ssq, offs, 
     with ExitStack() as ctx:
         lists = ctx.enter_context(tc.tile_pool(name="lists", bufs=1))
         keep = ctx.enter_context(tc.tile_pool(name="keep", bufs=1))
+        placed = ctx.enter_context(tc.tile_pool(name="placed", bufs=1))
         psum = ctx.enter_context(tc.psum_pool(name="psum", bufs=1))
 
         offs_sb = lists.tile([P, S // GROUP], U16, name="offs_sb")
@@ -48,7 +52,9 @@ def tile_picked_adagr8_none_p_kernel(tc, x_words, x_scales, w1, par, ssq, offs, 
         scale_table = keep.tile([P, T], U8, name="scale_table", align_bytes=ALIGN)
         word_table = keep.tile([P, T], I32, name="word_table", align_bytes=ALIGN)
         w_raw = keep.tile([P, PACK, N], F32, name="w_raw", align_bytes=ALIGN)
-        par_sb = [keep.tile([P, U], F32, name="par%d" % t, align_bytes=ALIGN) for t in range(PANELS)]
+        par_sb = [
+            placed.tile([P, U], F32, name="par%d" % t, align_bytes=ALIGN, offset=PAR_PLACES[t]) for t in range(PANELS)
+        ]
         ssq_sb = [keep.tile([P, U], F32, name="ssq%d" % t, align_bytes=ALIGN) for t in range(PANELS)]
 
         def offsets(list_sb, picked):
@@ -60,9 +66,11 @@ def tile_picked_adagr8_none_p_kernel(tc, x_words, x_scales, w1, par, ssq, offs, 
         def load_par(t, cols=slice(0, U)):
             nc.sync.dma_start(par_sb[t][:, cols], par_rows[t][:, cols])
 
-        nc.sync.dma_start(w_raw[:, 0 : PACK // 2, :], w_rows[:, 0 : PACK // 2, :])
+        w_flat, w_rows_flat = (w.rearrange("p r c -> p (r c)") for w in (w_raw[:], w_rows))
+        nc.sync.dma_start(w_flat[:, 0:W_AHEAD], w_rows_flat[:, 0:W_AHEAD])
         nc.sync.dma_start(offs_sb[:], offs)
-        nc.vector.memset(scale_table[:].bitcast(I32), 0)
+        nc.vector.memset(scale_table[:, 0 : T // 2].bitcast(I32), 0)
+        nc.gpsimd.memset(scale_table[:, T // 2 : T].bitcast(I32), 0)
         nc.sync.dma_start(scale_table[0:P:SCALE_STEP, :].bitcast(I32), x_scales[0].bitcast(I32))
         x_plane = keep.tile([P, S], U8, name="x_plane", align_bytes=ALIGN)
         nc.vector.memset(x_plane[:].bitcast(I32), 0)
@@ -72,10 +80,9 @@ def tile_picked_adagr8_none_p_kernel(tc, x_words, x_scales, w1, par, ssq, offs, 
         nc.gpsimd.memset(warm_in[:], 1.0)
         nc.scalar.activation(warm_out[:], warm_in[:], ACT.Abs_reciprocal_sqrt)
 
-        nc.sync.dma_start(w_raw[:, PACK // 2 : PACK, :], w_rows[:, PACK // 2 : PACK, :])
+        nc.sync.dma_start(w_flat[:, W_AHEAD:], w_rows_flat[:, W_AHEAD:])
         nc.sync.dma_start(ent_sb[:], ent)
         nc.sync.dma_start(word_table[:], x_words[0].rearrange("p c r -> p (c r)").bitcast(I32))
-        load_par(LAST, COLUMN_HALVES[0])
 
         picked_scales = keep.tile([P, S], U8, name="picked_scales", align_bytes=ALIGN)
         nc.vector.tensor_copy(picked_scales[:], scale_table[:].indirect(offs_sb[:]))
@@ -85,11 +92,11 @@ def tile_picked_adagr8_none_p_kernel(tc, x_words, x_scales, w1, par, ssq, offs, 
                 picked_scales[SCALE_STEP * i : P : QUADRANT, :].bitcast(I32),
             )
 
-        load_par(LAST, COLUMN_HALVES[1])
+        load_par(LAST)
         load_ssq(0)
-        load_par(0, slice(0, U // 4))
+        load_par(0, COLUMN_HALVES[0])
         load_ssq(1)
-        load_par(0, slice(U // 4, U))
+        load_par(0, COLUMN_HALVES[1])
         load_par(1)
         load_ssq(2)
         load_ssq(LAST)
@@ -130,26 +137,30 @@ def tile_picked_adagr8_none_p_kernel(tc, x_words, x_scales, w1, par, ssq, offs, 
 
         A, B = HALVES
         y = {t: [] for t in range(PANELS)}
-        for t, picked in ((0, A), (1, A), (0, B), (1, B), (2, A), (2, B), (LAST, WHOLE)):
+        for t, picked in ((0, A), (1, A), (0, B), (1, B), (2, A), (2, B), (LAST, A), (LAST, B)):
             y[t].append((picked.start, multiply(t, picked)))
 
         kinds = ("y_sq", "total", "inv", "step", "new")
-        shared = 8 * H
+        shared = 12 * H
         work = keep.tile([P, shared + len(kinds) * PANELS * S], F32, name="work")
         place = {}
         for i, kind in enumerate(kinds):
             for t in range(PANELS):
                 start = shared + (i * PANELS + t) * S
                 place[kind, t] = [start, start + H]
-        place["y_sq", 0] = [H, 4 * H]
-        place["y_sq", 2] = [0, H]
-        place["new", 0][1] = 0
-        place["step", 1][1] = H
-        place["y_sq", LAST] = [3 * H, 4 * H]
-        place["step", 2] = [3 * H, H]
-        place["step", LAST] = [2 * H, 3 * H]
-        place["step", 0][1] = 6 * H + H // 2
-        place["total", 1] = [7 * H, place["step", 0][0]]
+        Q = H // 2
+        place["y_sq", 0] = [0, 22 * Q]
+        place["y_sq", 2] = [20 * Q, 0]
+        place["new", 0][1] = 20 * Q
+        place["step", 1][1] = 0
+        place["y_sq", 1][0] = 4 * Q
+        place["y_sq", LAST] = [3 * Q, 5 * Q]
+        place["new", 1][1] = 3 * Q
+        place["step", 2] = [6 * Q, 0]
+        place["step", LAST] = [5 * Q, 7 * Q]
+        place["step", 0][1] = 11 * Q
+        place["total", 1] = [12 * Q, place["step", 0][0]]
+        minus_y = work[:, 22 * Q : 24 * Q]
         old_0b = keep.tile([P, H], F32, name="old_0b")
 
         def looked_up(table, t, part):
@@ -174,12 +185,15 @@ def tile_picked_adagr8_none_p_kernel(tc, x_words, x_scales, w1, par, ssq, offs, 
             nc.scalar.activation(at("inv", t, part), at("total", t, part), ACT.Abs_reciprocal_sqrt)
 
         def product(t, part):
-            if t == LAST:
-                nc.vector.scalar_tensor_tensor(
-                    at("step", t, part), y_at(t, part), -1.0, at("inv", t, part), ALU.mult, ALU.mult
-                )
-            else:
-                nc.vector.tensor_tensor(at("step", t, part), y_at(t, part), at("inv", t, part), ALU.mult)
+            nc.vector.tensor_tensor(at("step", t, part), y_at(t, part), at("inv", t, part), ALU.mult)
+
+        def negated_product(t, part):
+            nc.vector.scalar_tensor_tensor(
+                at("step", t, part), y_at(t, part), -1.0, at("inv", t, part), ALU.mult, ALU.mult
+            )
+
+        def add_back(t, part):
+            nc.vector.tensor_tensor(looked_up(par_sb, t, part), at("new", t, part), at("step", t, part), ALU.add)
 
         def subtract_from_par(t, part):
             nc.vector.tensor_tensor(at("new", t, part), looked_up(par_sb, t, part), at("step", t, part), ALU.subtract)
@@ -204,9 +218,11 @@ def tile_picked_adagr8_none_p_kernel(tc, x_words, x_scales, w1, par, ssq, offs, 
         product(0, A)
         square(2, B)
         root(0, B)
-        square(LAST, WHOLE)
+        nc.scalar.activation(minus_y, y_at(LAST, A), ACT.Copy, scale=-1.0)
         add_ssq(1, A)
+        nc.gpsimd.tensor_tensor(at("y_sq", LAST, A), minus_y, minus_y, ALU.mult)
         root(1, A)
+        square(LAST, B)
         nc.scalar.activation(old_0b[:], looked_up(par_sb, 0, B), ACT.Copy)
         subtract_from_par(0, A)
         put_back(0, A)
@@ -222,19 +238,21 @@ def tile_picked_adagr8_none_p_kernel(tc, x_words, x_scales, w1, par, ssq, offs, 
         nc.vector.tensor_tensor(at("new", 0, B), old_0b[:], at("step", 0, B), ALU.subtract)
         put_back(0, C)
         product(1, B)
-        add_ssq(LAST, WHOLE)
+        add_ssq(LAST, A)
+        add_ssq(LAST, B)
         root(LAST, WHOLE)
         subtract_from_par(1, B)
         put_back(1, B)
-        store(1)
+        store(1, 2)
         product(2, A)
         product(2, B)
         subtract_from_par(2, A)
+        nc.gpsimd.tensor_tensor(at("step", LAST, A), minus_y, at("inv", LAST, A), ALU.mult)
         subtract_from_par(2, B)
         put_back(2, WHOLE)
-        product(LAST, WHOLE)
+        negated_product(LAST, B)
         nc.vector.tensor_copy(looked_up(par_sb, 0, D), at("new", 0, D))
         store(0)
-        store(2)
-        nc.vector.tensor_tensor(looked_up(par_sb, LAST, WHOLE), at("new", LAST, WHOLE), at("step", LAST, WHOLE), ALU.add)
+        nc.scalar.dma_start(out_rows[2], par_sb[2][:])
+        add_back(LAST, WHOLE)
         store(LAST)

@@ -30,7 +30,8 @@ WHOLE = slice(0, S)
 HALVES = (slice(0, H), slice(H, S))
 COLUMN_HALVES = (slice(0, U // 2), slice(U // 2, U))
 VECTOR_COLS = 72
-SCALAR_SHARE = 320
+SCALAR_SHARE = 288
+FIRST = 224
 W_AHEAD = 576
 
 
@@ -94,9 +95,8 @@ def tile_picked_adagr8_none_p_kernel(tc, x_words, x_scales, w1, par, ssq, offs, 
 
         load_par(LAST)
         load_ssq(0)
-        load_par(0, COLUMN_HALVES[0])
         load_ssq(1)
-        load_par(0, COLUMN_HALVES[1])
+        load_par(0)
         load_par(1)
         load_ssq(2)
         load_ssq(LAST)
@@ -137,11 +137,11 @@ def tile_picked_adagr8_none_p_kernel(tc, x_words, x_scales, w1, par, ssq, offs, 
 
         A, B = HALVES
         y = {t: [] for t in range(PANELS)}
-        for t, picked in ((0, A), (1, A), (0, B), (1, B), (2, A), (2, B), (LAST, A), (LAST, B)):
+        for t, picked in ((0, A), (1, A), (0, B), (1, B), (LAST, WHOLE), (2, WHOLE)):
             y[t].append((picked.start, multiply(t, picked)))
 
         kinds = ("y_sq", "total", "inv", "step", "new")
-        shared = 12 * H
+        shared = 10 * H
         work = keep.tile([P, shared + len(kinds) * PANELS * S], F32, name="work")
         place = {}
         for i, kind in enumerate(kinds):
@@ -149,18 +149,17 @@ def tile_picked_adagr8_none_p_kernel(tc, x_words, x_scales, w1, par, ssq, offs, 
                 start = shared + (i * PANELS + t) * S
                 place[kind, t] = [start, start + H]
         Q = H // 2
-        place["y_sq", 0] = [0, 22 * Q]
-        place["y_sq", 2] = [20 * Q, 0]
-        place["new", 0][1] = 20 * Q
-        place["step", 1][1] = 0
-        place["y_sq", 1][0] = 4 * Q
-        place["y_sq", LAST] = [3 * Q, 5 * Q]
-        place["new", 1][1] = 3 * Q
-        place["step", 2] = [6 * Q, 0]
-        place["step", LAST] = [5 * Q, 7 * Q]
-        place["step", 0][1] = 11 * Q
-        place["total", 1] = [12 * Q, place["step", 0][0]]
-        minus_y = work[:, 22 * Q : 24 * Q]
+        place["y_sq", 1][0] = Q
+        place["step", 0] = [0, place["y_sq", 1][1]]
+        place["step", 1] = [6 * Q, 0]
+        place["inv", 0] = [5 * Q, 7 * Q]
+        place["y_sq", LAST] = [2 * Q, 8 * Q]
+        place["new", 1][1] = 2 * Q
+        place["new", 0] = [12 * Q, 14 * Q]
+        place["y_sq", 2] = [14 * Q, 16 * Q]
+        place["step", 2] = [8 * Q, 0]
+        place["step", LAST] = [8 * Q, 10 * Q]
+        minus_y = keep.tile([P, S], F32, name="minus_y")
         old_0b = keep.tile([P, H], F32, name="old_0b")
 
         def looked_up(table, t, part):
@@ -205,31 +204,29 @@ def tile_picked_adagr8_none_p_kernel(tc, x_words, x_scales, w1, par, ssq, offs, 
             for c in range(0, U, U // parts):
                 nc.sync.dma_start(out_rows[t][:, c : c + U // parts], par_sb[t][:, c : c + U // parts])
 
-        C, D = slice(H, SCALAR_SHARE), slice(SCALAR_SHARE, S)
+        first, C, D = slice(0, FIRST), slice(FIRST, SCALAR_SHARE), slice(SCALAR_SHARE, S)
         nc.vector.tensor_copy(at("new", LAST, WHOLE), looked_up(par_sb, LAST, WHOLE))
         square(0, A)
         square(1, A)
         square(0, B)
         square(1, B)
-        square(2, A)
+        nc.scalar.activation(minus_y[:], y_at(LAST, WHOLE), ACT.Copy, scale=-1.0)
+        square(2, WHOLE)
         add_ssq(0, A)
         add_ssq(0, B)
-        root(0, A)
-        product(0, A)
-        square(2, B)
-        root(0, B)
-        nc.scalar.activation(minus_y, y_at(LAST, A), ACT.Copy, scale=-1.0)
+        root(0, WHOLE)
         add_ssq(1, A)
-        nc.gpsimd.tensor_tensor(at("y_sq", LAST, A), minus_y, minus_y, ALU.mult)
-        root(1, A)
-        square(LAST, B)
-        nc.scalar.activation(old_0b[:], looked_up(par_sb, 0, B), ACT.Copy)
-        subtract_from_par(0, A)
-        put_back(0, A)
-        product(1, A)
-        product(0, B)
+        nc.gpsimd.tensor_tensor(at("y_sq", LAST, A), minus_y[:, A], minus_y[:, A], ALU.mult)
         add_ssq(1, B)
-        root(1, B)
+        root(1, WHOLE)
+        nc.scalar.activation(old_0b[:], looked_up(par_sb, 0, B), ACT.Copy)
+        product(0, A)
+        product(0, B)
+        nc.gpsimd.tensor_tensor(at("y_sq", LAST, B), minus_y[:, B], minus_y[:, B], ALU.mult)
+        subtract_from_par(0, A)
+        put_back(0, first)
+        product(1, A)
+        product(1, B)
         subtract_from_par(1, A)
         put_back(1, A)
         add_ssq(2, A)
@@ -237,7 +234,6 @@ def tile_picked_adagr8_none_p_kernel(tc, x_words, x_scales, w1, par, ssq, offs, 
         root(2, WHOLE)
         nc.vector.tensor_tensor(at("new", 0, B), old_0b[:], at("step", 0, B), ALU.subtract)
         put_back(0, C)
-        product(1, B)
         add_ssq(LAST, A)
         add_ssq(LAST, B)
         root(LAST, WHOLE)
@@ -247,12 +243,12 @@ def tile_picked_adagr8_none_p_kernel(tc, x_words, x_scales, w1, par, ssq, offs, 
         product(2, A)
         product(2, B)
         subtract_from_par(2, A)
-        nc.gpsimd.tensor_tensor(at("step", LAST, A), minus_y, at("inv", LAST, A), ALU.mult)
+        for part in HALVES:
+            nc.gpsimd.tensor_tensor(at("step", LAST, part), minus_y[:, part], at("inv", LAST, part), ALU.mult)
         subtract_from_par(2, B)
         put_back(2, WHOLE)
-        negated_product(LAST, B)
         nc.vector.tensor_copy(looked_up(par_sb, 0, D), at("new", 0, D))
-        store(0)
+        store(0, 2)
         nc.scalar.dma_start(out_rows[2], par_sb[2][:])
         add_back(LAST, WHOLE)
         store(LAST)

@@ -20,19 +20,20 @@ PACK = 4
 GROUP = 16
 QUADRANT = 32
 SCALE_STEP = 8
+F32_BYTES = 4
 PANELS = N // P
 LAST = PANELS - 1
-APART = 64 * 1024
-PAR_PLACES = (0, APART, 2 * APART, 4 * U)
 ALIGN = 64
 H = S // 2
 WHOLE = slice(0, S)
-HALVES = (slice(0, H), slice(H, S))
-COLUMN_HALVES = (slice(0, U // 2), slice(U // 2, U))
+A, B = slice(0, H), slice(H, S)
 VECTOR_COLS = 72
+W_AHEAD = 576
 SCALAR_SHARE = 288
 FIRST = 224
-W_AHEAD = 576
+APART = 64 * 1024
+PAR_PLACES = (0, APART, 2 * APART, U * F32_BYTES)
+STORE_PARTS = 2
 
 
 def tile_picked_adagr8_none_p_kernel(tc, x_words, x_scales, w1, par, ssq, offs, ent, out):
@@ -40,7 +41,7 @@ def tile_picked_adagr8_none_p_kernel(tc, x_words, x_scales, w1, par, ssq, offs, 
     par_rows = par.rearrange("(p t) u -> t p u", t=PANELS)
     ssq_rows = ssq.rearrange("(p t) u -> t p u", t=PANELS)
     out_rows = out.rearrange("(p t) u -> t p u", t=PANELS)
-    w_rows = w1.rearrange("(p r) c -> p r c", r=PACK)
+    w_rows = w1.rearrange("(p r) c -> p (r c)", r=PACK)
 
     with ExitStack() as ctx:
         lists = ctx.enter_context(tc.tile_pool(name="lists", bufs=1))
@@ -52,23 +53,16 @@ def tile_picked_adagr8_none_p_kernel(tc, x_words, x_scales, w1, par, ssq, offs, 
         ent_sb = lists.tile([P, S // GROUP], U16, name="ent_sb")
         scale_table = keep.tile([P, T], U8, name="scale_table", align_bytes=ALIGN)
         word_table = keep.tile([P, T], I32, name="word_table", align_bytes=ALIGN)
-        w_raw = keep.tile([P, PACK, N], F32, name="w_raw", align_bytes=ALIGN)
+        w_raw = keep.tile([P, PACK * N], F32, name="w_raw", align_bytes=ALIGN)
+        ssq_sb = [keep.tile([P, U], F32, name="ssq%d" % t, align_bytes=ALIGN) for t in range(PANELS)]
         par_sb = [
             placed.tile([P, U], F32, name="par%d" % t, align_bytes=ALIGN, offset=PAR_PLACES[t]) for t in range(PANELS)
         ]
-        ssq_sb = [keep.tile([P, U], F32, name="ssq%d" % t, align_bytes=ALIGN) for t in range(PANELS)]
 
-        def offsets(list_sb, picked):
-            return list_sb[:, picked.start // GROUP : picked.stop // GROUP]
+        def offsets(list_sb, part):
+            return list_sb[:, part.start // GROUP : part.stop // GROUP]
 
-        def load_ssq(t, cols=slice(0, U)):
-            nc.sync.dma_start(ssq_sb[t][:, cols], ssq_rows[t][:, cols])
-
-        def load_par(t, cols=slice(0, U)):
-            nc.sync.dma_start(par_sb[t][:, cols], par_rows[t][:, cols])
-
-        w_flat, w_rows_flat = (w.rearrange("p r c -> p (r c)") for w in (w_raw[:], w_rows))
-        nc.sync.dma_start(w_flat[:, 0:W_AHEAD], w_rows_flat[:, 0:W_AHEAD])
+        nc.sync.dma_start(w_raw[:, 0:W_AHEAD], w_rows[:, 0:W_AHEAD])
         nc.sync.dma_start(offs_sb[:], offs)
         nc.vector.memset(scale_table[:, 0 : T // 2].bitcast(I32), 0)
         nc.gpsimd.memset(scale_table[:, T // 2 : T].bitcast(I32), 0)
@@ -81,7 +75,7 @@ def tile_picked_adagr8_none_p_kernel(tc, x_words, x_scales, w1, par, ssq, offs, 
         nc.gpsimd.memset(warm_in[:], 1.0)
         nc.scalar.activation(warm_out[:], warm_in[:], ACT.Abs_reciprocal_sqrt)
 
-        nc.sync.dma_start(w_flat[:, W_AHEAD:], w_rows_flat[:, W_AHEAD:])
+        nc.sync.dma_start(w_raw[:, W_AHEAD:], w_rows[:, W_AHEAD:])
         nc.sync.dma_start(ent_sb[:], ent)
         nc.sync.dma_start(word_table[:], x_words[0].rearrange("p c r -> p (c r)").bitcast(I32))
 
@@ -93,17 +87,18 @@ def tile_picked_adagr8_none_p_kernel(tc, x_words, x_scales, w1, par, ssq, offs, 
                 picked_scales[SCALE_STEP * i : P : QUADRANT, :].bitcast(I32),
             )
 
-        load_par(LAST)
-        load_ssq(0)
-        load_ssq(1)
-        load_par(0)
-        load_par(1)
-        load_ssq(2)
-        load_ssq(LAST)
-        load_par(2)
+        for tiles, rows, order in (
+            (par_sb, par_rows, (LAST,)),
+            (ssq_sb, ssq_rows, (0, 1)),
+            (par_sb, par_rows, (0, 1)),
+            (ssq_sb, ssq_rows, (2, LAST)),
+            (par_sb, par_rows, (2,)),
+        ):
+            for t in order:
+                nc.sync.dma_start(tiles[t][:], rows[t])
 
         w_bf = keep.tile([P, PANELS, P, PACK], BF16, name="w_bf", align_bytes=ALIGN)
-        w_from = w_raw[:].rearrange("p r (m t) -> p m t r", t=PANELS)
+        w_from = w_raw[:].rearrange("p (r m t) -> p m t r", r=PACK, t=PANELS)
         w_to = w_bf[:].rearrange("p t m r -> p m t r")
         nc.vector.tensor_copy(w_to[:, 0:VECTOR_COLS], w_from[:, 0:VECTOR_COLS])
         nc.scalar.copy(w_to[:, VECTOR_COLS:P], w_from[:, VECTOR_COLS:P])
@@ -118,137 +113,124 @@ def tile_picked_adagr8_none_p_kernel(tc, x_words, x_scales, w1, par, ssq, offs, 
             )
 
         x_codes = keep.tile([P, S], U32, name="x_codes", align_bytes=ALIGN)
-        for picked in HALVES:
-            nc.vector.tensor_copy(x_codes[:, picked], word_table[:].bitcast(U32).indirect(offsets(offs_sb, picked)))
+        for part in (A, B):
+            nc.vector.tensor_copy(x_codes[:, part], word_table[:].bitcast(U32).indirect(offsets(offs_sb, part)))
 
-        def multiply(t, picked):
+        def multiply(t, part):
             cols = slice(t * P, (t + 1) * P)
-            bank = psum.tile([P, picked.stop - picked.start], F32, name="y%d_%d" % (t, picked.start))
+            bank = psum.tile([P, part.stop - part.start], F32, name="y%d_%d" % (t, part.start))
             nc.tensor.matmul_mx(
                 out=bank[:],
                 lhsT=w_codes[:, cols].bitcast(FP8X4),
                 lhsT_scale=w_plane[:, cols],
-                rhs=x_codes[:, picked].bitcast(FP8X4),
-                rhs_scale=x_plane[:, picked],
+                rhs=x_codes[:, part].bitcast(FP8X4),
+                rhs_scale=x_plane[:, part],
                 start=True,
                 stop=True,
             )
-            return bank
+            return bank[:]
 
-        A, B = HALVES
-        y = {t: [] for t in range(PANELS)}
-        for t, picked in ((0, A), (1, A), (0, B), (1, B), (LAST, WHOLE), (2, WHOLE)):
-            y[t].append((picked.start, multiply(t, picked)))
+        y = {t: [multiply(t, A)] for t in (0, 1)}
+        for t in (0, 1):
+            y[t].append(multiply(t, B))
+        for t in (2, LAST):
+            y[t] = [multiply(t, WHOLE)]
 
-        kinds = ("y_sq", "total", "inv", "step", "new")
-        shared = 10 * H
-        work = keep.tile([P, shared + len(kinds) * PANELS * S], F32, name="work")
-        place = {}
-        for i, kind in enumerate(kinds):
-            for t in range(PANELS):
-                start = shared + (i * PANELS + t) * S
-                place[kind, t] = [start, start + H]
-        Q = H // 2
-        place["y_sq", 1][0] = Q
-        place["step", 0] = [0, place["y_sq", 1][1]]
-        place["step", 1] = [6 * Q, 0]
-        place["inv", 0] = [5 * Q, 7 * Q]
-        place["y_sq", LAST] = [2 * Q, 8 * Q]
-        place["new", 1][1] = 2 * Q
-        place["new", 0] = [12 * Q, 14 * Q]
-        place["y_sq", 2] = [14 * Q, 16 * Q]
-        place["step", 2] = [8 * Q, 0]
-        place["step", LAST] = [8 * Q, 10 * Q]
-        minus_y = keep.tile([P, S], F32, name="minus_y")
-        old_0b = keep.tile([P, H], F32, name="old_0b")
+        def at(values, t, part):
+            if len(values[t]) == 1:
+                return values[t][0][:, part]
+            return values[t][part.start // H]
+
+        def buffer(name, columns=S):
+            return keep.tile([P, columns], F32, name=name)[:]
+
+        total = {t: [buffer("total%d" % t)] for t in range(PANELS)}
+        inv = {t: [buffer("inv%d" % t)] for t in range(PANELS)}
+        y_sq = {1: [buffer("y_sq1")]}
+        new = {2: [buffer("new2")]}
+        old_0b = buffer("old_0b", H)
+        old_last = buffer("old_last")
+
+        step = {}
+        step[0] = y_sq[1]
+        step[1] = [inv[0][0][:, B], step[0][0][:, A]]
+        shared = buffer("new0_and_y_sq2", S + H)
+        new[0], y_sq[2] = [shared[:, 0:S]], [shared[:, H:]]
+        shared = buffer("y_sq3_and_step3", S + H)
+        y_sq[LAST], step[LAST] = [shared[:, 0:S]], [shared[:, H:]]
+        new[1] = [buffer("new1a", H), shared[:, A]]
+        step[2] = [shared[:, B], step[1][1]]
+        y_sq[0] = [buffer("y_sq0a", H), shared[:, A]]
 
         def looked_up(table, t, part):
             return table[t][:].indirect(offsets(ent_sb, part))
 
-        def at(kind, t, part):
-            start = place[kind, t][part.start // H] + part.start % H
-            return work[:, start : start + part.stop - part.start]
-
-        def y_at(t, part):
-            for first, bank in y[t]:
-                if first <= part.start and part.stop - first <= bank.shape[1]:
-                    return bank[:, part.start - first : part.stop - first]
-
         def square(t, part):
-            nc.scalar.activation(at("y_sq", t, part), y_at(t, part), ACT.Square)
+            nc.scalar.activation(at(y_sq, t, part), at(y, t, part), ACT.Square)
 
         def add_ssq(t, part):
-            nc.vector.tensor_tensor(at("total", t, part), looked_up(ssq_sb, t, part), at("y_sq", t, part), ALU.add)
+            nc.vector.tensor_tensor(at(total, t, part), looked_up(ssq_sb, t, part), at(y_sq, t, part), ALU.add)
 
-        def root(t, part):
-            nc.scalar.activation(at("inv", t, part), at("total", t, part), ACT.Abs_reciprocal_sqrt)
+        def root(t):
+            nc.scalar.activation(at(inv, t, WHOLE), at(total, t, WHOLE), ACT.Abs_reciprocal_sqrt)
 
         def product(t, part):
-            nc.vector.tensor_tensor(at("step", t, part), y_at(t, part), at("inv", t, part), ALU.mult)
-
-        def negated_product(t, part):
-            nc.vector.scalar_tensor_tensor(
-                at("step", t, part), y_at(t, part), -1.0, at("inv", t, part), ALU.mult, ALU.mult
-            )
-
-        def add_back(t, part):
-            nc.vector.tensor_tensor(looked_up(par_sb, t, part), at("new", t, part), at("step", t, part), ALU.add)
+            nc.vector.tensor_tensor(at(step, t, part), at(y, t, part), at(inv, t, part), ALU.mult)
 
         def subtract_from_par(t, part):
-            nc.vector.tensor_tensor(at("new", t, part), looked_up(par_sb, t, part), at("step", t, part), ALU.subtract)
+            nc.vector.tensor_tensor(at(new, t, part), looked_up(par_sb, t, part), at(step, t, part), ALU.subtract)
 
         def put_back(t, part):
-            nc.scalar.activation(looked_up(par_sb, t, part), at("new", t, part), ACT.Copy)
+            nc.scalar.activation(looked_up(par_sb, t, part), at(new, t, part), ACT.Copy)
 
-        def store(t, parts=1):
-            for c in range(0, U, U // parts):
-                nc.sync.dma_start(out_rows[t][:, c : c + U // parts], par_sb[t][:, c : c + U // parts])
+        def store_in_parts(t):
+            for c in range(0, U, U // STORE_PARTS):
+                cols = slice(c, c + U // STORE_PARTS)
+                nc.sync.dma_start(out_rows[t][:, cols], par_sb[t][:, cols])
 
-        first, C, D = slice(0, FIRST), slice(FIRST, SCALAR_SHARE), slice(SCALAR_SHARE, S)
-        nc.vector.tensor_copy(at("new", LAST, WHOLE), looked_up(par_sb, LAST, WHOLE))
-        square(0, A)
-        square(1, A)
-        square(0, B)
-        square(1, B)
-        nc.scalar.activation(minus_y[:], y_at(LAST, WHOLE), ACT.Copy, scale=-1.0)
+        nc.vector.tensor_copy(old_last, looked_up(par_sb, LAST, WHOLE))
+        for part in (A, B):
+            for t in (0, 1):
+                square(t, part)
         square(2, WHOLE)
-        add_ssq(0, A)
-        add_ssq(0, B)
-        root(0, WHOLE)
-        add_ssq(1, A)
-        nc.gpsimd.tensor_tensor(at("y_sq", LAST, A), minus_y[:, A], minus_y[:, A], ALU.mult)
-        add_ssq(1, B)
-        root(1, WHOLE)
-        nc.scalar.activation(old_0b[:], looked_up(par_sb, 0, B), ACT.Copy)
-        product(0, A)
-        product(0, B)
-        nc.gpsimd.tensor_tensor(at("y_sq", LAST, B), minus_y[:, B], minus_y[:, B], ALU.mult)
-        subtract_from_par(0, A)
-        put_back(0, first)
-        product(1, A)
-        product(1, B)
-        subtract_from_par(1, A)
-        put_back(1, A)
-        add_ssq(2, A)
-        add_ssq(2, B)
-        root(2, WHOLE)
-        nc.vector.tensor_tensor(at("new", 0, B), old_0b[:], at("step", 0, B), ALU.subtract)
-        put_back(0, C)
-        add_ssq(LAST, A)
-        add_ssq(LAST, B)
-        root(LAST, WHOLE)
+
+        for part in (A, B):
+            add_ssq(0, part)
+        root(0)
+        square(LAST, WHOLE)
+        for part in (A, B):
+            add_ssq(1, part)
+        root(1)
+        nc.scalar.activation(old_0b, looked_up(par_sb, 0, B), ACT.Copy)
+        for t, scattered in ((0, slice(0, FIRST)), (1, A)):
+            for part in (A, B):
+                product(t, part)
+            subtract_from_par(t, A)
+            put_back(t, scattered)
+
+        for part in (A, B):
+            add_ssq(2, part)
+        root(2)
+        nc.vector.tensor_tensor(at(new, 0, B), old_0b, at(step, 0, B), ALU.subtract)
+        put_back(0, slice(FIRST, SCALAR_SHARE))
+        for part in (A, B):
+            add_ssq(LAST, part)
+        root(LAST)
         subtract_from_par(1, B)
         put_back(1, B)
-        store(1, 2)
-        product(2, A)
-        product(2, B)
-        subtract_from_par(2, A)
-        for part in HALVES:
-            nc.gpsimd.tensor_tensor(at("step", LAST, part), minus_y[:, part], at("inv", LAST, part), ALU.mult)
-        subtract_from_par(2, B)
+        store_in_parts(1)
+
+        for part in (A, B):
+            product(2, part)
+        for part in (A, B):
+            subtract_from_par(2, part)
         put_back(2, WHOLE)
-        nc.vector.tensor_copy(looked_up(par_sb, 0, D), at("new", 0, D))
-        store(0, 2)
+        nc.vector.scalar_tensor_tensor(
+            at(step, LAST, WHOLE), at(y, LAST, WHOLE), -1.0, at(inv, LAST, WHOLE), ALU.mult, ALU.mult
+        )
+        rest = slice(SCALAR_SHARE, S)
+        nc.vector.tensor_copy(looked_up(par_sb, 0, rest), at(new, 0, rest))
+        store_in_parts(0)
         nc.scalar.dma_start(out_rows[2], par_sb[2][:])
-        add_back(LAST, WHOLE)
-        store(LAST)
+        nc.vector.tensor_tensor(looked_up(par_sb, LAST, WHOLE), old_last, at(step, LAST, WHOLE), ALU.add)
+        nc.sync.dma_start(out_rows[LAST], par_sb[LAST][:])

@@ -20,7 +20,6 @@ PACK = 4
 GROUP = 16
 QUADRANT = 32
 SCALE_STEP = 8
-F32_BYTES = 4
 PANELS = N // P
 LAST = PANELS - 1
 ALIGN = 64
@@ -31,8 +30,6 @@ VECTOR_COLS = 72
 W_AHEAD = 576
 SCALAR_SHARE = 288
 FIRST = 224
-APART = 64 * 1024
-PAR_PLACES = (0, APART, 2 * APART, U * F32_BYTES)
 STORE_PARTS = 2
 
 
@@ -46,7 +43,6 @@ def tile_picked_adagr8_none_p_kernel(tc, x_words, x_scales, w1, par, ssq, offs, 
     with ExitStack() as ctx:
         lists = ctx.enter_context(tc.tile_pool(name="lists", bufs=1))
         keep = ctx.enter_context(tc.tile_pool(name="keep", bufs=1))
-        placed = ctx.enter_context(tc.tile_pool(name="placed", bufs=1))
         psum = ctx.enter_context(tc.psum_pool(name="psum", bufs=1))
 
         offs_sb = lists.tile([P, S // GROUP], U16, name="offs_sb")
@@ -55,9 +51,7 @@ def tile_picked_adagr8_none_p_kernel(tc, x_words, x_scales, w1, par, ssq, offs, 
         word_table = keep.tile([P, T], I32, name="word_table", align_bytes=ALIGN)
         w_raw = keep.tile([P, PACK * N], F32, name="w_raw", align_bytes=ALIGN)
         ssq_sb = [keep.tile([P, U], F32, name="ssq%d" % t, align_bytes=ALIGN) for t in range(PANELS)]
-        par_sb = [
-            placed.tile([P, U], F32, name="par%d" % t, align_bytes=ALIGN, offset=PAR_PLACES[t]) for t in range(PANELS)
-        ]
+        par_sb = [keep.tile([P, U], F32, name="par%d" % t, align_bytes=ALIGN) for t in range(PANELS)]
 
         def offsets(list_sb, part):
             return list_sb[:, part.start // GROUP : part.stop // GROUP]

from contextlib import ExitStack

import concourse.mybir as mybir

K, T, S, N, U = 512, 2048, 512, 512, 1024
FLOPS = 2 * K * N * S

F32 = mybir.dt.float32
BF16 = mybir.dt.bfloat16
I32 = mybir.dt.int32
U32 = mybir.dt.uint32
U16 = mybir.dt.uint16
U8 = mybir.dt.uint8
FP8X4 = mybir.dt.float8_e4m3fn_x4
ALU = mybir.AluOpType
ACT = mybir.ActivationFunctionType

P = 128
PACK = 4
GROUP = 16
QUADRANT = 32
SCALE_STEP = 8
PANELS = N // P
LAST = PANELS - 1
ALIGN = 64
H = S // 2
WHOLE = slice(0, S)
A, B = slice(0, H), slice(H, S)
VECTOR_COLS = 72
W_AHEAD = 576
SCALAR_SHARE = 288
FIRST = 224
STORE_PARTS = 2


def tile_picked_adagr8_none_p_kernel(tc, x_words, x_scales, w1, par, ssq, offs, ent, out):
    nc = tc.nc
    par_rows = par.rearrange("(p t) u -> t p u", t=PANELS)
    ssq_rows = ssq.rearrange("(p t) u -> t p u", t=PANELS)
    out_rows = out.rearrange("(p t) u -> t p u", t=PANELS)
    w_rows = w1.rearrange("(p r) c -> p (r c)", r=PACK)

    with ExitStack() as ctx:
        lists = ctx.enter_context(tc.tile_pool(name="lists", bufs=1))
        keep = ctx.enter_context(tc.tile_pool(name="keep", bufs=1))
        psum = ctx.enter_context(tc.psum_pool(name="psum", bufs=1))

        offs_sb = lists.tile([P, S // GROUP], U16, name="offs_sb")
        ent_sb = lists.tile([P, S // GROUP], U16, name="ent_sb")
        scale_table = keep.tile([P, T], U8, name="scale_table", align_bytes=ALIGN)
        word_table = keep.tile([P, T], I32, name="word_table", align_bytes=ALIGN)
        w_raw = keep.tile([P, PACK * N], F32, name="w_raw", align_bytes=ALIGN)
        ssq_sb = [keep.tile([P, U], F32, name="ssq%d" % t, align_bytes=ALIGN) for t in range(PANELS)]
        par_sb = [keep.tile([P, U], F32, name="par%d" % t, align_bytes=ALIGN) for t in range(PANELS)]

        def offsets(list_sb, part):
            return list_sb[:, part.start // GROUP : part.stop // GROUP]

        nc.sync.dma_start(w_raw[:, 0:W_AHEAD], w_rows[:, 0:W_AHEAD])
        nc.sync.dma_start(offs_sb[:], offs)
        nc.vector.memset(scale_table[:, 0 : T // 2].bitcast(I32), 0)
        nc.gpsimd.memset(scale_table[:, T // 2 : T].bitcast(I32), 0)
        nc.sync.dma_start(scale_table[0:P:SCALE_STEP, :].bitcast(I32), x_scales[0].bitcast(I32))
        x_plane = keep.tile([P, S], U8, name="x_plane", align_bytes=ALIGN)
        nc.vector.memset(x_plane[:].bitcast(I32), 0)

        warm_in = keep.tile([P, 1], F32, name="warm_in")
        warm_out = keep.tile([P, 1], F32, name="warm_out")
        nc.gpsimd.memset(warm_in[:], 1.0)
        nc.scalar.activation(warm_out[:], warm_in[:], ACT.Abs_reciprocal_sqrt)

        nc.sync.dma_start(w_raw[:, W_AHEAD:], w_rows[:, W_AHEAD:])
        nc.sync.dma_start(ent_sb[:], ent)
        nc.sync.dma_start(word_table[:], x_words[0].rearrange("p c r -> p (c r)").bitcast(I32))

        picked_scales = keep.tile([P, S], U8, name="picked_scales", align_bytes=ALIGN)
        nc.vector.tensor_copy(picked_scales[:], scale_table[:].indirect(offs_sb[:]))
        for i in range(QUADRANT // SCALE_STEP):
            nc.sync.dma_start(
                x_plane[i:P:QUADRANT, :].bitcast(I32),
                picked_scales[SCALE_STEP * i : P : QUADRANT, :].bitcast(I32),
            )

        for tiles, rows, order in (
            (par_sb, par_rows, (LAST,)),
            (ssq_sb, ssq_rows, (0, 1)),
            (par_sb, par_rows, (0, 1)),
            (ssq_sb, ssq_rows, (2, LAST)),
            (par_sb, par_rows, (2,)),
        ):
            for t in order:
                nc.sync.dma_start(tiles[t][:], rows[t])

        w_bf = keep.tile([P, PANELS, P, PACK], BF16, name="w_bf", align_bytes=ALIGN)
        w_from = w_raw[:].rearrange("p (r m t) -> p m t r", r=PACK, t=PANELS)
        w_to = w_bf[:].rearrange("p t m r -> p m t r")
        nc.vector.tensor_copy(w_to[:, 0:VECTOR_COLS], w_from[:, 0:VECTOR_COLS])
        nc.scalar.copy(w_to[:, VECTOR_COLS:P], w_from[:, VECTOR_COLS:P])
        w_codes = keep.tile([P, N], U32, name="w_codes", align_bytes=ALIGN)
        w_plane = keep.tile([P, N], U8, name="w_plane", align_bytes=ALIGN)
        for t in range(0, PANELS, 2):
            cols = slice(t * P, (t + 2) * P)
            nc.vector.quantize_mx(
                out=w_codes[:, cols].bitcast(FP8X4),
                scales=w_plane[:, cols],
                in_=w_bf[:, t : t + 2].rearrange("p t m r -> p (t m r)"),
            )

        x_codes = keep.tile([P, S], U32, name="x_codes", align_bytes=ALIGN)
        for part in (A, B):
            nc.vector.tensor_copy(x_codes[:, part], word_table[:].bitcast(U32).indirect(offsets(offs_sb, part)))

        def multiply(t, part):
            cols = slice(t * P, (t + 1) * P)
            bank = psum.tile([P, part.stop - part.start], F32, name="y%d_%d" % (t, part.start))
            nc.tensor.matmul_mx(
                out=bank[:],
                lhsT=w_codes[:, cols].bitcast(FP8X4),
                lhsT_scale=w_plane[:, cols],
                rhs=x_codes[:, part].bitcast(FP8X4),
                rhs_scale=x_plane[:, part],
                start=True,
                stop=True,
            )
            return bank[:]

        y = {t: [multiply(t, A)] for t in (0, 1)}
        for t in (0, 1):
            y[t].append(multiply(t, B))
        for t in (2, LAST):
            y[t] = [multiply(t, WHOLE)]

        def at(values, t, part):
            if len(values[t]) == 1:
                return values[t][0][:, part]
            return values[t][part.start // H]

        def buffer(name, columns=S):
            return keep.tile([P, columns], F32, name=name)[:]

        total = {t: [buffer("total%d" % t)] for t in range(PANELS)}
        inv = {t: [buffer("inv%d" % t)] for t in range(PANELS)}
        y_sq = {1: [buffer("y_sq1")]}
        new = {2: [buffer("new2")]}
        old_0b = buffer("old_0b", H)
        old_last = buffer("old_last")

        step = {}
        step[0] = y_sq[1]
        step[1] = [inv[0][0][:, B], step[0][0][:, A]]
        shared = buffer("new0_and_y_sq2", S + H)
        new[0], y_sq[2] = [shared[:, 0:S]], [shared[:, H:]]
        shared = buffer("y_sq3_and_step3", S + H)
        y_sq[LAST], step[LAST] = [shared[:, 0:S]], [shared[:, H:]]
        new[1] = [buffer("new1a", H), shared[:, A]]
        step[2] = [shared[:, B], step[1][1]]
        y_sq[0] = [buffer("y_sq0a", H), shared[:, A]]

        def looked_up(table, t, part):
            return table[t][:].indirect(offsets(ent_sb, part))

        def square(t, part):
            nc.scalar.activation(at(y_sq, t, part), at(y, t, part), ACT.Square)

        def add_ssq(t, part):
            nc.vector.tensor_tensor(at(total, t, part), looked_up(ssq_sb, t, part), at(y_sq, t, part), ALU.add)

        def root(t):
            nc.scalar.activation(at(inv, t, WHOLE), at(total, t, WHOLE), ACT.Abs_reciprocal_sqrt)

        def product(t, part):
            nc.vector.tensor_tensor(at(step, t, part), at(y, t, part), at(inv, t, part), ALU.mult)

        def subtract_from_par(t, part):
            nc.vector.tensor_tensor(at(new, t, part), looked_up(par_sb, t, part), at(step, t, part), ALU.subtract)

        def put_back(t, part):
            nc.scalar.activation(looked_up(par_sb, t, part), at(new, t, part), ACT.Copy)

        def store_in_parts(t):
            for c in range(0, U, U // STORE_PARTS):
                cols = slice(c, c + U // STORE_PARTS)
                nc.sync.dma_start(out_rows[t][:, cols], par_sb[t][:, cols])

        nc.vector.tensor_copy(old_last, looked_up(par_sb, LAST, WHOLE))
        for part in (A, B):
            for t in (0, 1):
                square(t, part)
        square(2, WHOLE)

        for part in (A, B):
            add_ssq(0, part)
        root(0)
        square(LAST, WHOLE)
        for part in (A, B):
            add_ssq(1, part)
        root(1)
        nc.scalar.activation(old_0b, looked_up(par_sb, 0, B), ACT.Copy)
        for t, scattered in ((0, slice(0, FIRST)), (1, A)):
            for part in (A, B):
                product(t, part)
            subtract_from_par(t, A)
            put_back(t, scattered)

        for part in (A, B):
            add_ssq(2, part)
        root(2)
        nc.vector.tensor_tensor(at(new, 0, B), old_0b, at(step, 0, B), ALU.subtract)
        put_back(0, slice(FIRST, SCALAR_SHARE))
        for part in (A, B):
            add_ssq(LAST, part)
        root(LAST)
        subtract_from_par(1, B)
        put_back(1, B)
        store_in_parts(1)

        for part in (A, B):
            product(2, part)
        for part in (A, B):
            subtract_from_par(2, part)
        put_back(2, WHOLE)
        nc.vector.scalar_tensor_tensor(
            at(step, LAST, WHOLE), at(y, LAST, WHOLE), -1.0, at(inv, LAST, WHOLE), ALU.mult, ALU.mult
        )
        rest = slice(SCALAR_SHARE, S)
        nc.vector.tensor_copy(looked_up(par_sb, 0, rest), at(new, 0, rest))
        store_in_parts(0)
        nc.scalar.dma_start(out_rows[2], par_sb[2][:])
        nc.vector.tensor_tensor(looked_up(par_sb, LAST, WHOLE), old_last, at(step, LAST, WHOLE), ALU.add)
        nc.sync.dma_start(out_rows[LAST], par_sb[LAST][:])
